import numpy as np, ml_dtypes
CORES = [113,118,241,246]
N = 4
BF = ml_dtypes.bfloat16
W, C, RO, SH = 4096, 384, 5, 4
def parts(rng):
    cov = np.where(rng.random((N, 8, 1, W)) < 0.15, 0, rng.integers(0, 256, (N, 8, 16, W)))
    share = rng.choice(np.array([0.0, 0.1, 0.2, 0.3, 0.5, 0.8]), (N, 8, 1, C))
    tst = np.where(rng.random((N, 8, 16, C)) < share, 256, rng.integers(0, 256, (N, 8, 16, C)))
    return cov, tst, rng.integers(0, 160, (N, 8, 16, C)), rng.integers(200, 2000, (N, 8))
def pack(cov, tst, pr, th):
    return {"cov": np.ascontiguousarray(cov.reshape(N, 128, W)).astype(np.float32).astype(BF), "tst": np.ascontiguousarray(tst.reshape(N, 128, C)).astype(np.int32),
            "pr": np.ascontiguousarray(pr.reshape(N, 128, C)).astype(np.float32).astype(BF), "th": np.ascontiguousarray(th.reshape(N, 8, 1)).astype(np.int32)}
def setup_inputs(rng):
    return pack(*parts(rng))
def setup_inputs_corners(rng):
    cov, tst, pr, th = parts(rng)
    c = np.arange(C); lane = np.arange(16)[:, None]; full = rng.integers(0, 256, (N, 8, 16, C))
    th = rng.choice(np.array([0, 1, 500, 4080]), (N, 8))
    for r in range(N):
        for g in range(8):
            k = (g + r) % 8; x = full[r, g]
            if k == 1: x = np.full((16, C), 256)
            elif k == 2: x = np.where(lane == c % 16, 256, x)
            elif k == 3: x = np.where((lane + c) % 2 == 1, 256, x)
            elif k == 4:
                x = np.repeat(x[:, :1], C, axis=1); pr[r, g] = np.repeat(pr[r, g][:, :1], C, axis=1); th[r, g] = 0
            elif k == 5: x = np.where((lane == c % 16) | (lane == (c + 1) % 16), x, 256)
            elif k == 6:
                cov[r, g][:, rng.random(W) < 0.7] = 0; th[r, g] = 0
            elif k == 7: pr[r, g] = 255 * rng.integers(0, 2, (1, C))
            tst[r, g] = x
    q = rng.permutation(N); th[q[0]] = 0; th[q[1]] = 4080
    r = int(q[0]); g = (8 - r) % 8
    cov[r, g, 0] = 0; cov[r, g, 1:] = rng.integers(1, 256, (15, W))
    pr[r, g, :, 0::2] = 255; pr[r, g, :, 1::2] = 0
    k = np.arange(C // 2); p = 1 + k % 14; v = rng.integers(0, 256, (2, C // 2)); x = np.full((16, C), 256)
    for odd in range(2):
        x[p, 2 * k + odd] = v[0]; x[p + 1, 2 * k + odd] = v[1]
    tst[r, g] = x
    return pack(cov, tst, pr, th)
def pairs(rng, low):
    x = rng.integers(0, 256, 2 ** 15); y = rng.integers(0, 256, 2 ** 15); i = rng.integers(0, 16, 2 ** 15)
    col, at = np.unique(((((2 * x + 1) * (2 * y + 1)) >> 4) + 613 * i) & (W - 1), return_index=True)
    at = rng.permutation(at[col >= low])
    return x[at], y[at], i[at]
def lone(rng, x, y, i):
    k = len(x); c = np.arange(k); v = np.full((16, k), 256)
    v[i, c] = x; v[(i + 1) & 15, c] = y
    for d in range(3, 15, 2): v[(i + d) & 15, c] = rng.integers(0, 256, k)
    return v
def setup_inputs_crowd(rng):
    cov, tst, pr, th = parts(rng)
    a = int(rng.integers(0, N)); b = (a + 1) % N; d = (a + 2) % N
    v = rng.integers(0, 256, (8, 16, C)); v[:, [1, 5, 7, 9, 11, 13, 15]] = 256
    tst[a] = v; th[a] = rng.integers(511, 1500, 8); th[b] = 0; th[d] = 0
    cov[b] = rng.integers(1, 256, (8, 16, W)); cov[d] = rng.integers(1, 256, (8, 16, W))
    c = np.arange(C); second = ((c % 2 == 0) & (c > 0)) | (c == C - 1)
    for g in range(8):
        p = np.append(rng.permutation(C - 1)[:31], C - 1)
        few = ((((2 * v[g, 2, p] + 1) * (2 * v[g, 3, p] + 1)) >> 4) + 613 * 2) & (W - 1)
        most = ((((2 * v[g, 3, p] + 1) * (2 * v[g, 4, p] + 1)) >> 4) + 613 * 3) & (W - 1)
        cov[a, g][:, few] = 255; cov[a, g][int(rng.integers(0, 16)), few] = 254; cov[a, g][:, most] = 255
        x, y, i = pairs(rng, 0)
        tst[b, g] = lone(rng, x[:C], y[:C], i[:C])
        x, y, i = pairs(rng, W - 254 if g == 7 else 0)
        o = (c + 1) // 2; o[C - 1] = 0; o = np.where(o > 0, 1 + (o - 1) % (len(x) - 1), 0)
        tst[d, g] = lone(rng, x[o], y[o], i[o])
        lev = rng.integers(0, 16, C // 2)[o]; lev = np.where(second, (lev + rng.integers(1, 16, C)) & 15, lev)
        pr[d, g] = np.where(np.arange(16)[:, None] == lev[None, :], 0, 255)
    return pack(cov, tst, pr, th)
def setup_inputs_ties(rng):
    unit = np.where(np.arange(8) % 4 == 1, 1, 85).reshape(1, 8, 1, 1)
    cov = unit * np.where(rng.random((N, 8, 1, W)) < 0.5, rng.integers(0, 4, (N, 8, 1, W)), rng.integers(0, 4, (N, 8, 16, W)))
    pr = unit * np.where(rng.random((N, 8, 1, C)) < 0.5, rng.integers(0, 2, (N, 8, 1, C)), rng.integers(0, 2, (N, 8, 16, C)))
    few = rng.choice(np.array([0, 1, 64, 128, 255, 256]), (N, 8, 16, C)); many = np.where(rng.random((N, 8, 16, C)) < 0.2, 256, rng.integers(0, 256, (N, 8, 16, C)))
    tst = np.where(rng.random((N, 8, 1, C)) < 0.5, few, many)
    return pack(cov, tst, pr, unit[..., 0, 0] * rng.integers(0, 24, (N, 8)))
def setup_inputs_spread(rng):
    cov = np.minimum((np.exp2(8 * rng.random((N, 8, 1, W))) * rng.random((N, 8, 16, W)) * 1.01).astype(np.int64), 255)
    pr = np.minimum((np.exp2(8 * rng.random((N, 8, 16, C))) * rng.random((N, 8, 1, C))).astype(np.int64), 255)
    tst = np.minimum((256 * rng.random((N, 8, 16, C)) ** rng.choice(np.array([0.25, 1.0, 4.0]), (N, 8, 16, 1))).astype(np.int64), 255)
    tst = np.where(rng.random((N, 8, 16, C)) < rng.random((N, 8, 1, C)) * 0.6, 256, tst)
    th = np.minimum(np.exp2(12 * rng.random((N, 8))).astype(np.int64) - 1, 4080)
    return pack(cov, tst, pr, th)
def setup_inputs_ends(rng):
    kind = rng.integers(0, 3, (N, 8, 1, W)); cov = 255 * np.where(kind == 2, rng.integers(0, 2, (N, 8, 16, W)), kind)
    lane = np.arange(16)
    for t in range(RO):
        z = (613 * lane + 77 * t) & (W - 1); f = ((511 * 511 >> 4) + 613 * lane + 77 * t) & (W - 1)
        cov[..., z] = 255; cov[..., f] = 0; cov[..., f[15]] = 255; cov[:, ::2, :, f[6]] = 255
    u = rng.random((N, 8, 16, C))
    tst = np.where(u < 0.5, 0, np.where(u < 0.7, 256, np.where(u < 0.9, 255, rng.integers(0, 256, (N, 8, 16, C)))))
    tst[..., [2, C - 1]] = 0; tst[..., [5, C - 2]] = 255; tst[..., [1, C - 3]] = 256
    pr = 255 * rng.integers(0, 2, (N, 8, 16, C))
    pr[..., [2, 5, C - 2, C - 1]] = 255; pr[:, :, 15, [2, 5, C - 2, C - 1]] = 0; pr[:, 1::2, 4, [2, C - 1]] = 0
    o = np.argsort(rng.random((N, 8)), axis=1); th = 4080 * (o < rng.integers(3, 6, (N, 1))).astype(np.int64)
    th[N - 1, 7] = 4080; th[N - 1, 0] = 0
    return pack(cov, tst, pr, th)
def check_inputs(d):
    bad = []
    for k, lo, hi in (("cov", 0, 255), ("tst", 0, 256), ("pr", 0, 255), ("th", 0, 4080)):
        v = np.asarray(d[k]).astype(np.float64)
        if not (np.min(v) >= lo and np.max(v) <= hi): bad.append("range of " + k)
        elif np.any(v != np.floor(v)): bad.append("whole numbers in " + k)
    return bad
def reference(cov, tst, pr, th):
    U = cov.astype(np.float32).astype(np.int64).reshape(N, 8, 16, W); T = tst.astype(np.int64).reshape(N, 8, 16, C)
    price = pr.astype(np.float32).astype(np.int64).reshape(N, 8, 16, C); lim = th.astype(np.int64).reshape(N, 8, 1)
    lane = np.arange(16).reshape(1, 16, 1); last = np.zeros(N, np.int64)
    for t in range(RO):
        rho = (5 * t) & 15; now = np.zeros(N, np.int64)
        for r in range(N):
            s = (r + t) % N
            x = T[r]; y = np.roll(x, -(1 + t), axis=1)
            live = (x != 256) & (y != 256)
            code = ((((2 * x + 1) * (2 * y + 1)) >> 4) + 613 * lane + 77 * t) & (W - 1)
            got = np.take_along_axis(U[s], code.reshape(8, 1, 16 * C), 2).reshape(8, 16, 16, C)
            gain = np.add.reduce(np.where(live[:, None], np.maximum(got - price[s][:, :, None, :], 0), 0), axis=2)
            lev = np.argmax(gain, axis=1); best = np.max(gain, axis=1)
            useful = best >= lim[s] + (last[s] & 255); now[s] = np.sum(~useful)
            some = np.any(live, axis=1)
            vote = np.argmax(np.where(live, np.add.reduce(got, axis=1), -1), axis=1)
            taken = np.take_along_axis(code, vote[:, None, :], 1)[:, 0] >> SH
            most = np.argmax(np.where(live, np.take_along_axis(got, lev[:, None, None, :], 1)[:, 0], -1), axis=1)
            credit = np.take_along_axis(code, most[:, None, :], 1)[:, 0]
            none = x == 256; first = np.argmax(none, axis=1)
            new = np.array(x)
            g, c = np.nonzero(~useful & some & np.any(none, axis=1))
            new[g, first[g, c], c] = taken[g, c]
            new[:, rho] = np.where(useful, 16 * lev + (best & 15), 256)
            for g in range(8):
                c = np.nonzero(useful[g] & some[g])[0]
                col, at = np.unique(credit[g, c], return_index=True)
                U[s, g, lev[g, c[at]], col] = 0
            T[r] = new
        last = now
    left = np.add.reduce(U.reshape(N, 128, W // 16, 16), axis=3)
    return {"yt": T.reshape(N, 128, C).astype(np.float32), "yc": left.astype(np.float32)}

@@ -1,0 +1,592 @@
+import numpy as np
+from concourse.mybir import AluOpType as ALU, AxisListType as AX, ActivationFunctionType as AF
+
+C, W, RO = 384, 4096, 5
+VOID = -128.0
+UW = W + 48
+GTW = 16 * C + 16
+MAGIC = 12582912.0
+BIG = 1.0e9
+
+SCRATCH = {}
+SEMAPHORES = ["sv", "sa", "sp", "sg", "ld0", "ld1", "ld2", "ld3", "ld4", "st0", "st1", "out", "out2"] + ["arr%d" % t for t in range(RO)]
+VIEW = {}
+
+
+def _pack(buf, names, cols, dtype):
+    step = -(-cols // 32) * 32
+    for k, n in enumerate(names.split()):
+        VIEW[n] = (buf, k * step, cols)
+    SCRATCH[buf] = ("sbuf", [128, step * len(names.split())], dtype)
+
+
+def _sb(names, cols, dtype):
+    for n in names.split():
+        SCRATCH[n] = ("sbuf", [128, cols], dtype)
+
+
+_sb("U", UW, "bfloat16")
+_sb("tsti pi3 t2 t3 KS VS MS", C, "int32")
+_sb("prb prp nn hib FO FQ E2 E2T ones MO nBQ nB V wt x0 x1 x2 x3 x4 xo0 xo1", C, "bfloat16")
+_sb("Eq lost RSb", C + 192, "bfloat16"), _sb("RBs", C + 192, "float32")
+_sb("aS t1 h0 h1 KQ KM MD yo RS", C, "float32"), _sb("cf xd", C, "float16")
+_sb("got R", 16 * C, "bfloat16")
+_sb("GT", GTW, "bfloat16")
+_sb("yco", 256, "float32")
+_sb("RY", W // 2, "bfloat16"), _sb("ys", W // 2, "float32")
+_sb("cu", C, "uint16")
+_sb("rep rep15 wl oG RP", 32, "uint16")
+_pack("packI", "K Ai Bi Av xp thi mi L1 L2 L3", 24, "int32")
+_pack("packF", "z z8 Cc Dd al lz tkm xpf thr thb thR zr zc ma mb mc mf thf", 24, "float32")
+_pack("packB", "val tkb tkr CWh CWl", 24, "bfloat16")
+_sb("pc", 32, "int32"), _sb("pf", 32, "float32")
+_sb("uA mB sL sG sH", 128, "int32"), _sb("sT0 sT1", 128, "int32"), _sb("iN", 160, "int32")
+_sb("uM uD", 128, "float32")
+_sb("rK", RO * 128, "int32"), _sb("rKh rKl", RO * 128, "int32"), _sb("rKhb rKlb", RO * 128, "bfloat16")
+_sb("r1", 128, "int32"), _sb("rH rM", 128, "bfloat16"), _sb("rV", C, "bfloat16")
+_sb("I1 Iv I16 I64k Im256 Blk TriM T00 T01 T10 T11 PL8", 128, "bfloat16")
+_pack("packP", " ".join("P2_%d Pn_%d Cm_%d Ir_%d" % (t, t, t, t) for t in range(RO)), 128, "bfloat16")
+_sb("BO", 8, "bfloat16"), _sb("HW", 224, "bfloat16"), _sb("X MK", 96, "bfloat16"), _sb("mk", 96, "int32"), _sb("L96", 8, "uint16")
+_sb("J0 J1", 160, "float16")
+_sb("PLf onf THl", 128, "float32"), _sb("G2f I1h", 128, "float16")
+for _k in range(8):
+    SCRATCH["B%d" % _k] = ("psum", [128, 512], "float32")
+PB = (0, 1, 7)
+
+CHUNKS = [(0, 128), (128, 256), (256, 384)]
+GATH = [[("a", 0, 64), ("v", 64, 128)], [("a", 128, 256)], [("a", 256, 384)]]
+NCH = len(CHUNKS)
+SUMS = [[("v", 0, 128), ("g", 0, 128)], [("v", 128, 256), ("g", 128, 256)], [("g", 256, 384), ("v", 256, 384)], []]
+
+
+def rank_program(g, core, T, topo):
+    rank = T.rank_of(core)
+    if rank is None:
+        return
+    Q = {"v": g.vector, "a": g.scalar, "p": g.tensor, "g": g, "y": g.sync}
+    sem = {"v": T.sem.sv, "a": T.sem.sa, "p": T.sem.sp, "g": T.sem.sg}
+    cnt, clock, snap, hist = {}, {e: {} for e in Q}, {}, {}
+
+    def A(name, c0=0, c1=None, step=1, p=128):
+        name, base, cols = VIEW.get(name, (name, 0, SCRATCH.get(name, (0, (0, 0)))[1][1]))
+        c0, c1 = base + c0, base + (cols if c1 is None else c1)
+        ap = T[name][0:p, c0:c1:step] if step != 1 else T[name][0:p, c0:c1]
+        return (ap, name, c0, c1, step)
+
+    def IND(win, off):
+        return (win[0].indirect(off[0]),) + tuple(win[1:])
+
+    def meet(a, b):
+        if a[1] >= b[2] or b[1] >= a[2]:
+            return False
+        if a[3] == b[3] and a[3] > 1 and (a[1] - b[1]) % a[3]:
+            return False
+        return True
+
+    def need(e, reads, writes):
+        want = {}
+
+        def ask(f, n):
+            want[f] = max(want.get(f, 0), n)
+        for x, wr in [(x, False) for x in reads] + [(x, True) for x in writes]:
+            ps = SCRATCH[x[1]][0] == "psum"
+            for h in hist.get(x[1], []):
+                hit = meet((0,) + tuple(x[2:]), (0,) + h[1:4])
+                if h[4] != e:
+                    if ps or (hit and (wr or h[6])):
+                        ask(h[4], h[5])
+                elif hit and (wr or h[6]) and e != "p":
+                    ask(h[4], h[5])
+        for f in sorted(want, key=lambda k: -want[k]):
+            if clock[e].get(f, 0) < want[f]:
+                Q[e].wait_ge(sem[f], want[f])
+                for k, n in snap[(f, want[f])].items():
+                    clock[e][k] = max(clock[e].get(k, 0), n)
+                clock[e][f] = max(clock[e].get(f, 0), want[f])
+
+    def note(f, n, e, reads, writes):
+        snap[(f, n)] = dict(clock[e])
+        for x in writes:
+            old = hist.get(x[1], [])
+            hist[x[1]] = [h for h in old if not (x[4] == 1 and h[1] >= x[2] and h[2] <= x[3] and (clock[e].get(h[4], 0) >= h[5] or h[4] == f))]
+            hist[x[1]].append((0, x[2], x[3], x[4], f, n, True))
+        for x in reads:
+            L = hist.setdefault(x[1], [])
+            L[:] = [h for h in L if not (not h[6] and h[4] == f and h[1:4] == tuple(x[2:5]))]
+            L.append((0, x[2], x[3], x[4], f, n, False))
+
+    def run(e, make, reads, writes):
+        need(e, reads, writes)
+        ins = make(Q[e])
+        cnt[e] = cnt.get(e, 0) + 1
+        ins.then_inc(sem[e], 1)
+        note(e, cnt[e], e, reads, writes)
+
+    def dma(e, out, in_, s, oap=None, iap=None):
+        reads, writes = [x for x in (in_,) if x], [x for x in (out,) if x]
+        need(e, reads, writes)
+        Q[e].dma_start(out[0] if out else oap, in_[0] if in_ else iap).then_inc(T.sem[s], 16)
+        sem[s] = T.sem[s]
+        cnt[s] = cnt.get(s, 0) + 16
+        note(s, cnt[s], e, reads, writes)
+
+    def mm(out, l, r, start, stop):
+        run("p", lambda q: q.matmul(out[0], l[0], r[0], start, stop), [l, r], [out])
+
+    def tt(out, a, b, op, xr=()):
+        run("v", lambda q: q.tensor_tensor(out[0], a[0], b[0], op), [a, b] + list(xr), [out])
+
+    def ts(out, a, s1, op0, s2=None, op1=None):
+        xr = [s for s in (s1, s2) if isinstance(s, tuple)]
+        v1 = s1[0] if isinstance(s1, tuple) else s1
+        v2 = s2[0] if isinstance(s2, tuple) else s2
+        if op1 is None:
+            run("v", lambda q: q.tensor_scalar(out[0], a[0], v1, None, op0), [a] + xr, [out])
+        else:
+            run("v", lambda q: q.tensor_scalar(out[0], a[0], v1, v2, op0, op1), [a] + xr, [out])
+
+    def cp(out, a, xr=()):
+        run("v", lambda q: q.tensor_copy(out[0], a[0]), [a] + list(xr), [out])
+
+    def turn(out, a):
+        run("v", lambda q: q.transpose(out[0], a[0]), [a], [out])
+
+    def ms(out, c):
+        run("v", lambda q: q.memset(out[0], c), [], [out])
+
+    def act(out, a, func=AF.Copy, xr=(), **kw):
+        run("a", lambda q: q.activation(out[0], a[0], func, **kw), [a] + list(xr), [out])
+
+    def iota(out, pattern, base, cm):
+        run("g", lambda q: q.iota(out[0], pattern, base, cm), [], [out])
+
+    def sel(out, a, pattern, op, fill, base, cm):
+        run("g", lambda q: q.affine_select(out[0], a[0], pattern, op, fill, base, cm), [a], [out])
+
+    B = lambda k, c0=0, c1=C, step=1: A("B%d" % k, c0, c1, step)
+
+    def top(out, src, reset):
+        run("v", lambda q: q.tensor_tensor_scan(out[0], reset[0], src[0], -BIG, ALU.min, ALU.max), [src, reset], [out])
+
+    LAST = lambda n: A(n, 15, C, 16)
+
+    dma("y", A("tsti"), None, "ld0", iap=T.tst[:])
+    dma("a", A("prb"), None, "ld1", iap=T.pr[:])
+    dma("a", A("thi", 0, 1, 1, 8), None, "ld2", iap=T.th[:])
+    dma("y", A("U", 0, 2048), None, "ld3", iap=T.cov[:, 0:2048])
+    dma("a", A("U", 2048, 4096), None, "ld4", iap=T.cov[:, 2048:4096])
+
+    iota(A("pc", 0, 1), [[0, 1]], 0, 1)
+    iota(A("uA"), [[-1, 128]], 256, 1)
+    iota(A("mB"), [[1, 8], [0, 16]], 0, 0)
+    iota(A("rK"), [[77, RO], [0, 8], [613, 16]], 0, 0)
+    iota(A("r1"), [[0, 8], [-1, 16]], 15, 0)
+    iota(A("iN"), [[1, 160]], -16, 0)
+    iota(A("K"), [[1, 24]], 0, 0)
+    iota(A("pi3"), [[0, 24], [1, 16]], 0, 0)
+    iota(A("sL"), [[32, 4], [1, 2], [2, 16]], 0, 0)
+    iota(A("sG"), [[2, 4], [0, 16], [1, 2]], 0, 0)
+    iota(A("sH"), [[1, 4], [0, 32]], 0, 0)
+    ms(A("ones"), 1.0)
+    iota(A("mk"), [[0, 12], [1, 4], [0, 2]], 0, 0)
+    P = lambda k: A("pc", k, k + 1)
+    F = lambda k: A("pf", k, k + 1)
+    ts(P(1), P(0), 4, ALU.arith_shift_right)
+    ts(P(3), P(0), 15, ALU.bitwise_and)
+    ts(P(2), P(1), 16, ALU.mult)
+    cp(A("pf", 0, 4), A("pc", 0, 4))
+    ts(A("uA"), A("uA"), 15, ALU.bitwise_and)
+    ts(A("uD"), A("mB"), F(1), ALU.subtract, -16.0, ALU.mult)
+    tt(A("uM"), A("uA"), A("uD"), ALU.add)
+    ts(A("Iv"), A("uM"), 0.0, ALU.is_equal, -360448.0, ALU.mult)
+
+    def perms(t):
+        ts(A("P2_%d" % t), A("uM"), t + 1.0, ALU.is_equal, 2.0, ALU.mult)
+        act(A("Pn_%d" % t), A("P2_%d" % t), scale=-256.0)
+        ts(A("Cm_%d" % t), A("uM"), t + 1.0, ALU.is_equal, -131072.0, ALU.mult)
+        tt(A("Cm_%d" % t), A("Cm_%d" % t), A("Iv"), ALU.add)
+
+    def restmats(t):
+        ts(F(12 + t), F(3), float(5 * t % 16), ALU.not_equal)
+        act(A("Ir_%d" % t), A("I1"), scale=F(12 + t)[0], xr=[F(12 + t)])
+    perms(0)
+    row = lambda n, c0=0: A(n, c0, c0 + 128, 1, 1)
+    one = lambda c0=0, c1=C: A("ones", c0, c1, 1, 1)
+
+    def rows(c0, c1):
+        R0 = lambda n: A(n, c0, c1, 1, 1)
+        ts(R0("rKh"), R0("rK"), 8, ALU.arith_shift_right, 15, ALU.bitwise_and)
+        ts(R0("rKhb"), R0("rKh"), 4096.0, ALU.mult)
+        ts(R0("rKl"), R0("rK"), 255, ALU.bitwise_and)
+        ts(R0("rKlb"), R0("rKl"), 16.0, ALU.mult)
+    rows(0, 128)
+    for b in range(2):
+        cp(A("x0", b, C, 2), A("tsti", 192 * b, 192 * b + 192))
+
+    def constants2():
+        ms(A("U", W, W + 16), VOID)
+        ms(A("U", W + 16, UW), 0.0)
+        ts(A("I1"), A("uM"), 0.0, ALU.is_equal)
+        act(A("I16"), A("I1"), scale=16.0)
+        act(A("Im256"), A("I1"), scale=-256.0)
+        act(A("I64k"), A("I1"), scale=65536.0)
+        for b in range(2):
+            act(A("prp", b, C, 2), A("prb", 192 * b, 192 * b + 192))
+        for k in range(3):
+            for j in range(4):
+                mm(B(PB[k], j, 512, 4), A("I1"), A("prp", 128 * k, 128 * k + 128), True, True)
+        cp(row("rH"), row("r1"))
+        ts(A("rV", 0, C, 1, 1), A("pi3", 0, C, 1, 1), -256.0, ALU.mult, 3840.0, ALU.add)
+        ts(row("rM"), row("r1"), 4096.0, ALU.mult, 2048.0, ALU.add)
+
+    def constants3():
+        ts(A("BO"), A("iN", 16, 24), F(1), ALU.is_equal, 4096.0, ALU.mult)
+        ts(P(11), P(1), 1, ALU.bitwise_and)
+        ts(P(8), P(11), 999, ALU.mult)
+        ts(P(9), P(11), 999, ALU.mult, -999, ALU.add)
+        tt(P(8), P(0), P(8), ALU.subtract)
+        tt(P(9), P(0), P(9), ALU.add)
+        ts(P(4), P(0), 1, ALU.bitwise_and)
+        ts(P(5), P(0), 31, ALU.bitwise_and)
+        ts(P(6), P(0), 1, ALU.arith_shift_right)
+        ts(P(7), P(0), 5, ALU.arith_shift_right)
+        ts(P(17), P(0), 5, ALU.arith_shift_right)
+        ts(P(18), P(0), 31, ALU.bitwise_and)
+        ts(P(5), P(5), 1, ALU.arith_shift_right)
+        ts(P(7), P(7), 2, ALU.mult)
+        ts(P(10), P(3), W + 16, ALU.add)
+        tt(P(7), P(7), P(4), ALU.add)
+        cp(A("pf", 4, 12), A("pc", 4, 12))
+        cp(A("thf", 0, 1, 1, 8), A("thi", 0, 1, 1, 8))
+        ts(A("mi", 0, 24), A("K", 0, 24), 1, ALU.bitwise_and)
+        ts(A("THl", 0, 128, 1, 8), A("sH", 0, 128, 1, 8), A("pf", 6, 7, 1, 8), ALU.is_equal)
+        ts(A("thR", 0, 24, 1, 8), A("mi", 0, 24, 1, 8), A("pf", 4, 5, 1, 8), ALU.is_equal, 16.0, ALU.mult)
+        ts(A("thR", 0, 24, 1, 8), A("thR", 0, 24, 1, 8), A("thf", 0, 1, 1, 8), ALU.mult)
+        mm(B(6, 0, 24), A("THl", 0, 128, 1, 8), A("thR", 0, 24, 1, 8), True, True)
+        ts(A("I1h"), A("uM"), 0.0, ALU.is_equal)
+        for g2 in range(2):
+            ts(A("J%d" % g2), A("iN"), F(8 + g2), ALU.is_equal)
+        ts(A("Blk"), A("mB"), F(1), ALU.is_equal)
+        sel(A("TriM"), A("Blk"), [[1, 128]], ALU.is_gt, 0.0, 0, -1)
+        ms(A("sT0"), -1000), ms(A("sT1"), -1000)
+        iota(A("sT0", 0, 128, 2), [[32, 4], [1, 2], [2, 8]], 0, 0)
+        iota(A("sT1", 1, 128, 2), [[32, 4], [1, 2], [2, 8]], 0, 0)
+        tt(A("TriM"), A("TriM"), A("I1"), ALU.subtract)
+        cp(A("thb"), B(6, 0, 24))
+        cp(A("thr"), A("thb"))
+        ms(A("RS"), BIG)
+        sel(A("RS"), A("RS"), [[0, 24], [1, 16]], ALU.not_equal, -BIG, 0, 0)
+
+    def constants4():
+        ms(A("GT", 16 * C, GTW), VOID)
+        for q3 in range(2):
+            for g2 in range(2):
+                ts(A("T%d%d" % (q3, g2)), A("sT%d" % g2), 16.0 * q3, ALU.add, F(0), ALU.is_equal)
+        ts(A("CWh"), A("K", 0, 24), 256.0, ALU.mult)
+        ts(A("CWl"), A("ones", 0, 24), F(3), ALU.mult, 16.0, ALU.mult)
+        ts(A("CWl"), A("CWl"), 15.0, ALU.add)
+        cp(A("rep", 0, 24), A("K", 0, 24))
+        ts(A("rep15", 0, 24), A("K", 0, 24), 16.0, ALU.mult, 15.0, ALU.add)
+        restmats(0)
+
+    def constants4b():
+        cp(A("pf", 17, 19), A("pc", 17, 19))
+        ms(A("HW"), 0.0)
+        ts(A("L1", 0, 6), A("K", 0, 6), 16.0, ALU.mult, F(3), ALU.add)
+        ts(A("L2", 0, 6), A("L1", 0, 6), 43.0, ALU.mult)
+        ts(A("MK"), A("mk"), F(17), ALU.is_equal)
+        ts(A("HW", 96, 128), A("iN", 16, 48), F(18), ALU.is_equal)
+        ts(A("L2", 0, 6), A("L2", 0, 6), 10, ALU.arith_shift_right)
+        ts(A("L3", 0, 6), A("L2", 0, 6), -24.0, ALU.mult)
+        tt(A("L1", 0, 6), A("L1", 0, 6), A("L3", 0, 6), ALU.add)
+        ts(A("L2", 0, 6), A("L2", 0, 6), 2.0, ALU.mult)
+        ts(A("L3", 0, 6), A("L1", 0, 6), 1, ALU.bitwise_and)
+        ts(A("L1", 0, 6), A("L1", 0, 6), 24, ALU.bitwise_and)
+        tt(A("L2", 0, 6), A("L2", 0, 6), A("L3", 0, 6), ALU.add)
+        tt(A("L1", 0, 6), A("L1", 0, 6), A("L2", 0, 6), ALU.add)
+        cp(A("L96", 0, 6), A("L1", 0, 6))
+
+    def constants5():
+        ts(A("MD"), A("pi3"), F(5), ALU.is_equal)
+        ts(A("MO"), A("pi3"), F(5), ALU.is_ge, 32768.0, ALU.mult)
+        ts(A("PLf"), A("sL"), F(0), ALU.is_equal)
+        act(A("PL8"), A("PLf"), scale=8192.0)
+        ts(A("G2f"), A("sG"), F(7), ALU.is_equal)
+        act(A("onf"), A("I1"), AF.Identity, scale=0.0, bias=16.0)
+        act(A("RSb", 0, C), A("RS"))
+        act(A("RSb", C, C + 192), A("RS", 0, 192))
+        L1, L2, L3 = A("L1"), A("L2"), A("L3")
+        ts(L1, A("K"), 12.0, ALU.is_ge)
+        ts(L2, L1, -12.0, ALU.mult)
+        tt(L2, L2, A("K"), ALU.add)
+        ts(L1, L1, 2.0, ALU.mult)
+        ts(L3, L2, 1, ALU.bitwise_and)
+        ts(L2, L2, 2.0, ALU.mult)
+        tt(L1, L1, L3, ALU.subtract)
+        tt(L1, L1, L2, ALU.add)
+        cp(A("RP", 0, 24), L1)
+        ts(F(19), F(10), 16.0, ALU.add)
+
+    def constants6(t):
+        rows(128 * t, 128 * t + 128)
+        perms(t)
+        restmats(t)
+
+    def constants7():
+        act(A("RY"), A("U", 0, W // 2), AF.Identity, scale=0.0, bias=1.0)
+        sel(A("RY"), A("RY"), [[0, W // 32], [1, 16]], ALU.not_equal, 0.0, 0, 0)
+
+    def codes0(t):
+        mm(B(2), one(0, 128), one(), True, False)
+        mm(B(3), row("rKhb", 128 * t), one(), True, False)
+        mm(B(3), row("rKlb", 128 * t), one(), False, False)
+
+    def codes1(t):
+        x = A("x%d" % t)
+        act(A("nn"), x, AF.Relu, bias=-255.0)
+        act(A("aS"), x, AF.Identity, bias=1.0, scale=2.0)
+        mm(B(2), A("P2_%d" % t), x, False, False)
+        mm(B(2), A("Pn_%d" % t), A("nn"), False, True)
+        mm(B(3), A("Cm_%d" % t), A("nn"), False, True)
+
+    def codes2(t):
+        for c0, c1 in (CHUNKS[0], (CHUNKS[0][1], C)):
+            tt(A("t1", c0, c1), A("aS", c0, c1), B(2, c0, c1), ALU.mult)
+            tt(A("t2", c0, c1), A("t1", c0, c1), B(3, c0, c1), ALU.add)
+            ts(A("t3", c0, c1), A("t2", c0, c1), 4, ALU.arith_shift_right, 0x8FFF, ALU.bitwise_and)
+            ts(A("cu", c0, c1), A("t3", c0, c1), 4096, ALU.min)
+
+    def starts(t):
+        mm(B(4), row("rH"), one(), True, False)
+        mm(B(4), A("Im256"), A("prp"), False, False)
+
+    def starts1(t):
+        mm(B(5), one(0, 128), A("rV", 0, C, 1, 1), True, False)
+
+    def starts2(t):
+        mm(B(3), A("TriM"), A("nn"), True, False)
+        mm(B(3), one(0, 128), one(), False, True)
+        mm(B(2), A("I1h"), A("cf"), True, True)
+
+    def starts3(t):
+        mm(B(6), row("rM"), one(), True, False)
+        for b in range(2):
+            for g2 in range(2):
+                s = 16 + 16 * (g2 - b)
+                mm(B(6, g2, C, 2), A("J%d" % g2, s, s + 128), A("cf", b, C, 2), False, False)
+
+    def highs(t):
+        act(A("h0"), B(2), AF.Identity, bias=128.0 - 0.46875, scale=0.0625)
+        act(A("h1"), A("h0"), AF.Identity, bias=MAGIC)
+        act(A("FO"), B(3), AF.Relu, bias=1.0, scale=-1.0)
+        act(A("hib"), A("h1"), AF.Identity, bias=-MAGIC)
+
+    def gather(k):
+        for e, c0, c1 in GATH[k]:
+            out, win, off = A("got", 16 * c0, 16 * c1), A("U"), A("cu", c0, c1)
+            (act if e == "a" else cp)(out, IND(win, off), xr=[off])
+
+    def price(k):
+        c0, c1 = CHUNKS[k]
+        n, f = 4 * (c1 - c0), 4 * (c0 % 128)
+        for s in range(4):
+            r = 4 * C * s + 4 * c0
+            tt(A("R", r, r + n), A("got", 16 * c0 + s, 16 * c1, 4), B(PB[c0 // 128], f, f + n), ALU.max)
+
+    def gains(c0, c1):
+        for i in range(16):
+            r = 4 * C * (i % 4) + i // 4
+            mm(B(4, c0, c1), A("I16"), A("R", r + 4 * c0, r - i // 4 + 4 * c1, 4), False, c1 == C and i == 15)
+
+    def votes(c0, c1):
+        for i in range(16):
+            mm(B(5, c0 + i, c1, 16), A("got", 16 * c0 + i, 16 * c1, 16), A("BO"), False, False)
+
+    def sums(L):
+        for what, c0, c1 in L:
+            (gains if what == "g" else votes)(c0, c1)
+
+    def gturn(k):
+        c0, c1 = CHUNKS[k]
+        turn(A("GT", 16 * c0, 16 * c1), A("got", 16 * c0, 16 * c1))
+
+    def best1(t):
+        turn(A("KQ"), B(4))
+        top(A("KS"), A("KQ"), A("RS"))
+        ts(A("Ai"), LAST("KS"), 15, ALU.bitwise_and)
+        tt(A("z"), LAST("KS"), A("thr"), ALU.is_lt)
+        ts(A("z8"), A("z"), 8192.0, ALU.mult)
+        tt(A("val"), A("z8"), A("Ai"), ALU.subtract)
+        mm(B(4, 0, 24), A("I1"), A("CWh"), True, False)
+        mm(B(4, 0, 24), A("I1"), A("CWl"), False, False)
+        for q3 in range(2):
+            for g2 in range(2):
+                mm(B(4, q3, 24, 2), A("T%d%d" % (q3, g2)), A("val", g2, 24, 2), False, q3 == 1 and g2 == 1)
+
+    def best2(t):
+        ts(A("wl", 0, 24), B(4, 0, 24), 16.0 * C, ALU.min)
+        act(A("wt"), IND(A("GT"), A("wl", 0, 24)), xr=[A("wl", 0, 24)])
+
+    def notb(t):
+        tt(A("nBQ"), IND(A("KS"), A("rep15", 0, 24)), A("KQ"), ALU.not_equal, xr=[A("rep15", 0, 24)])
+        turn(A("nB"), A("nBQ"))
+
+    def level(t):
+        ts(A("Bi"), LAST("KS"), 4, ALU.arith_shift_right, 15, ALU.bitwise_and)
+        ts(A("Cc"), A("val"), 16.0, ALU.mult, 240.0, ALU.add)
+        tt(A("Dd"), A("Bi"), A("Cc"), ALU.add)
+
+    def vote(t):
+        top(A("VS"), B(5), A("RS"))
+
+    def update(t):
+        rho, xo = (5 * t) % 16, "xo%d" % (t % 2)
+        ts(A("Av"), LAST("VS"), 255, ALU.bitwise_and)
+        ts(A("al"), LAST("VS"), 0.0, ALU.is_ge)
+        ts(A("tkm"), A("Av"), -256.0, ALU.add)
+        tt(A("tkr"), A("tkm"), A("al"), ALU.mult)
+        tt(A("X"), IND(A("tkr"), A("L96", 0, 6)), A("MK"), ALU.mult, xr=[A("L96", 0, 6)])
+        level(t)
+        for a in range(4):
+            mm(B(5, 0, 24), A("HW", 96 - 32 * a, 224 - 32 * a), A("X", 24 * a, 24 * a + 24), a == 0, a == 3)
+        mm(B(6), A("I64k"), A("wt"), False, True)
+        useless(t)
+        tt(A("tkb"), B(5, 0, 24), A("z"), ALU.mult)
+        tt(A("E2"), IND(A("tkb"), A("rep", 0, 24)), A("FQ"), ALU.mult, xr=[A("rep", 0, 24)])
+        ts(A("E2", rho, C, 16), A("Dd"), 256.0, ALU.min)
+        turn(A("E2T"), A("E2"))
+        mm(B(5), A("Ir_%d" % t), A("x%d" % t), True, False)
+        mm(B(5), A("I1"), A("E2T"), False, True)
+        act(A(xo), B(5))
+        if t < RO - 1:
+            to = T.cores[(rank + 1) % len(T.cores)]
+            rid, pid = topo.addr(to, core)
+            eng = topo.engines(core, to)[:8]
+            need("g", [A(xo)], [])
+            s, a = "st%d" % (t % 2), "arr%d" % (t + 1)
+            g.remote_dma(T["x%d" % (t + 1)][:, :], A(xo)[0], T.sem[a], T.sem[s], pid, rid, sum(1 << k for k in eng))
+            sem[s] = T.sem[s]
+            cnt[s] = cnt.get(s, 0) + len(eng)
+            note(s, cnt[s], "g", [A(xo)], [])
+            src = T.cores[(rank - 1) % len(T.cores)]
+            sem[a], cnt[a] = T.sem[a], len(topo.engines(src, core)[:8])
+            snap[(a, cnt[a])] = {}
+            hist["x%d" % (t + 1)] = [(0, 0, C, 1, a, cnt[a], True)]
+
+    def useless(t):
+        if t == RO - 1:
+            return
+        one1 = A("zr", 0, 1)
+        run("a", lambda q: q.activation(A("zc")[0], A("z")[0], AF.Copy, accum_out=one1[0]), [A("z")], [A("zc"), one1])
+        mm(B(3, 0, 1), A("onf"), one1, True, True)
+        act(A("ma", 0, 1), B(3, 0, 1), AF.Identity, scale=1.0 / 4096, bias=-255.0 / 512)
+        act(A("mb", 0, 1), A("ma", 0, 1), AF.Identity, bias=MAGIC)
+        act(A("mc", 0, 1), A("mb", 0, 1), AF.Identity, scale=-4096.0, bias=4096.0 * MAGIC)
+        act(A("mf", 0, 1), B(3, 0, 1))
+
+    def limits(t):
+        if t < RO - 1:
+            ts(A("thr"), A("thb"), A("mf", 0, 1), ALU.add, A("mc", 0, 1), ALU.add)
+
+    def claims1(t):
+        turn(A("KM"), B(6))
+        top(A("MS"), A("KM"), A("RS"))
+        ts(A("xp"), LAST("MS"), (1 << 24) | 4095, ALU.bitwise_and)
+        ts(A("xpf"), A("xp"), -2048.0, ALU.add, 32768.0, ALU.min)
+        rp = A("RP", 0, 24)
+        mm(B(4), A("I1"), A("MO"), True, False)
+        tt(A("xd"), IND(A("xpf"), rp), A("MD"), ALU.mult, xr=[rp])
+        mm(B(4), A("G2f"), A("xd"), False, True)
+        mm(B(6, 0, 192), A("G2f"), A("xd", 0, 192), True, True)
+        act(A("RBs", 0, C), B(4))
+        act(A("RBs", C, C + 192), B(6, 0, 192))
+
+    def claims2(t):
+        for rp, c0, c1 in ((A("RP", 0, 24), 0, C), (A("RP", 12, 24), C, C + 192)):
+            tt(A("Eq", c0, c1), IND(A("xpf"), rp), A("RBs", c0, c1), ALU.is_equal, xr=[rp])
+        top(A("lost"), A("Eq"), A("RSb"))
+        mm(B(4, 0, 24), A("I1"), A("HW", 0, 24), True, False)
+        for b in range(2):
+            mm(B(4, 12 * b, 12 * b + 12), A("PLf"), A("xpf", b, 24, 2), False, False)
+        for n in range(3):
+            for b in range(2):
+                h = min(n, 1)
+                mm(B(4, 12 * b + h, 12 * b + 12, 2), A("PL8"), A("lost", 15 + 16 * (12 * n + b), 192 * n + 192, 32), False, n == 2 and b == 1)
+        limits(t)
+
+    def claims3a(t):
+        for h in range(2):
+            ts(A("oG", h, 24, 2), B(4, h, 24, 2), 2048.0, ALU.add, F(10 + 9 * h), ALU.min)
+
+    def claims3(t):
+        for b in range(2):
+            o = A("oG", 12 * b, 12 * b + 12)
+            tt(A("V", 192 * b, 192 * b + 192), IND(A("U"), o), A("nB", b, C, 2), ALU.mult, xr=[o])
+        for b in (1, 0):
+            for k in range(5, -1, -1):
+                o = A("oG", 12 * b + 2 * k, 12 * b + 2 * k + 2)
+                cp(IND(A("U"), o), A("V", 192 * b + 32 * k, 192 * b + 32 * k + 32), xr=[o])
+
+    codes0(0)
+    codes1(0)
+    constants2()
+    constants3()
+    codes2(0)
+    for t in range(RO):
+        if t == 0:
+            starts(t)
+            starts1(t)
+        ts(A("cf"), A("t3"), 4096, ALU.min, -2048.0, ALU.add)
+        for k in range(NCH):
+            gather(k)
+        starts2(t)
+        starts3(t)
+        for k in range(NCH):
+            price(k)
+            gturn(k)
+            sums(SUMS[k])
+            if t == 0 and k == 0:
+                constants4()
+            if t == 0 and k == 1:
+                constants4b()
+        highs(t)
+        if t == 1:
+            constants7()
+        if t < RO - 1:
+            constants6(t + 1)
+        turn(A("FQ"), A("FO"))
+        for c0, c1 in CHUNKS:
+            mm(B(5, c0, c1), A("hib", c0, c1), A("I1"), False, c1 == C)
+        best1(t)
+        vote(t)
+        best2(t)
+        if t == 0:
+            constants5()
+        update(t)
+        claims1(t)
+        if t < RO - 1:
+            codes0(t + 1)
+        notb(t)
+        claims2(t)
+        claims3a(t)
+        if t < RO - 1:
+            starts(t + 1)
+            codes1(t + 1)
+            starts1(t + 1)
+        claims3(t)
+        if t < RO - 1:
+            codes2(t + 1)
+
+    top2 = [A("ys"), A("RY"), A("U", 0, W // 2)]
+    run("v", lambda q: q.tensor_tensor_scan(top2[0][0], top2[1][0], top2[2][0], 0.0, ALU.mult, ALU.add), top2[1:], top2[:1])
+    for k in range(16):
+        mm(B(4, 0, 128), A("I1"), A("U", W // 2 + k, W, 16), k == 0, k == 15)
+    for b in range(2):
+        act(A("yo", 192 * b, 192 * b + 192), A("xo0", b, C, 2))
+    dma("a", None, A("yo"), "out", oap=T.yt[:])
+    act(A("yco", 128, 256), B(4, 0, 128))
+    cp(A("yco", 0, 128), A("ys", 15, W // 2, 16))
+    dma("y", None, A("yco"), "out2", oap=T.yc[:])
+    for s in sem:
+        if cnt.get(s, 0):
+            g.wait_ge(sem[s], cnt[s])

@@ -2,61 +2,51 @@ import numpy as np
 from concourse.mybir import AluOpType as ALU, AxisListType as AX, ActivationFunctionType as AF
 
 C, W, RO = 384, 4096, 5
-VOID = -128.0
-UW = W + 48
-GTW = 16 * C + 16
+VOID = -2.0
+LOW = 16
+UW = LOW + W + 16
+BW = 136
+RW = 16 * BW
+NOWT = RW + 16
 MAGIC = 12582912.0
-BIG = 1.0e9
+M256 = 256 * MAGIC
+BIG = 2.0 ** 30
+FAR = 4224.0
+FLAG = 2.0 ** 24 + 2.0 ** 18
+CYCLE, HOP, FLIGHT, SLACK = 0.83, 100.0, 2500.0, 40.0
+ORDER = (2, 1, 0)
+PIECES = ((0, 3), (3, 6), (6, 9), (9, 12), (12, 14), (14, 16))
+GATHERS = ((0, 6), (6, 12), (12, 16))
 
 SCRATCH = {}
-SEMAPHORES = ["sv", "sa", "sp", "sg", "ld0", "ld1", "ld2", "ld3", "ld4", "st0", "st1", "out", "out2"] + ["arr%d" % t for t in range(RO)]
-VIEW = {}
-
-
-def _pack(buf, names, cols, dtype):
-    step = -(-cols // 32) * 32
-    for k, n in enumerate(names.split()):
-        VIEW[n] = (buf, k * step, cols)
-    SCRATCH[buf] = ("sbuf", [128, step * len(names.split())], dtype)
+PLAN = []
+SEMAPHORES = (["sv", "sa", "sp", "sg", "ld0", "ld1", "ld2", "ld3", "ld4", "st", "o0", "o1", "o2", "o3", "o4"]
+              + ["arr%d_%d" % (t, k) for t in range(1, RO) for k in range(3)])
 
 
 def _sb(names, cols, dtype):
     for n in names.split():
-        SCRATCH[n] = ("sbuf", [128, cols], dtype)
+        SCRATCH[n] = ("sbuf", [128] + (cols if isinstance(cols, list) else [cols]), dtype)
 
 
 _sb("U", UW, "bfloat16")
-_sb("tsti pi3 t2 t3 KS VS MS", C, "int32")
-_sb("prb prp nn hib FO FQ E2 E2T ones MO nBQ nB V wt x0 x1 x2 x3 x4 xo0 xo1", C, "bfloat16")
-_sb("Eq lost RSb", C + 192, "bfloat16"), _sb("RBs", C + 192, "float32")
-_sb("aS t1 h0 h1 KQ KM MD yo RS", C, "float32"), _sb("cf xd", C, "float16")
-_sb("got R", 16 * C, "bfloat16")
-_sb("GT", GTW, "bfloat16")
+_sb("tsti", [24, 16], "int32"), _sb("prb", [24, 16], "bfloat16")
+_sb("prp FQ Vr nB x0 x1 x2 x3 x4", C, "bfloat16"), _sb("xo", 4 * C, "bfloat16")
+_sb("got0 got1 got2", 2048, "bfloat16"), _sb("RT0 RT1 RT2", RW + 32, "bfloat16"), _sb("PT", 3 * RW, "bfloat16")
+_sb("pT", 3 * BW, "bfloat16")
+_sb("aH nH cf", C, "float16"), _sb("TT", [12, 32], "float16"), _sb("XS", 144, "float16"), _sb("X1", 128, "float16")
+_sb("t1 yo", C, "float32"), _sb("t2 t3 KS", C, "int32"), _sb("cu", C, "uint16")
+_sb("MS VS uA mB si", 128, "int32"), _sb("DA LS KT uM uD", 128, "float32")
+_sb("ka", 8, "int32"), _sb("tkb", 16, "bfloat16")
+_sb("xp y1 y2 r1 r2 vx i8 pc thi", 16, "int32"), _sb("wl lv rep", 16, "uint16"), _sb("oL", 48, "uint16")
+_sb("pf CV THs THn A16 XB acc mneg", 16, "float32"), _sb("acch cst D8 BO", 16, "bfloat16")
+_sb("pk OH E2 ones onesN Blk Blk8 I4096 I16 I64k Ineg Rneg TriN Perm PermN PermF PermT BI8 Bn8 LK RK TL MASK DM RS0 RSm RSp", 128, "bfloat16")
+_sb("R136", BW, "bfloat16"), _sb("SEL WR E3", 144, "bfloat16"), _sb("iN", 144, "int32")
+_sb("Pt Tri Ir", RO * 128, "bfloat16"), _sb("J RV W32 w32", 512, "bfloat16")
 _sb("yco", 256, "float32")
-_sb("RY", W // 2, "bfloat16"), _sb("ys", W // 2, "float32")
-_sb("cu", C, "uint16")
-_sb("rep rep15 wl oG RP", 32, "uint16")
-_pack("packI", "K Ai Bi Av xp thi mi L1 L2 L3", 24, "int32")
-_pack("packF", "z z8 Cc Dd al lz tkm xpf thr thb thR zr zc ma mb mc mf thf", 24, "float32")
-_pack("packB", "val tkb tkr CWh CWl", 24, "bfloat16")
-_sb("pc", 32, "int32"), _sb("pf", 32, "float32")
-_sb("uA mB sL sG sH", 128, "int32"), _sb("sT0 sT1", 128, "int32"), _sb("iN", 160, "int32")
-_sb("uM uD", 128, "float32")
-_sb("rK", RO * 128, "int32"), _sb("rKh rKl", RO * 128, "int32"), _sb("rKhb rKlb", RO * 128, "bfloat16")
-_sb("r1", 128, "int32"), _sb("rH rM", 128, "bfloat16"), _sb("rV", C, "bfloat16")
-_sb("I1 Iv I16 I64k Im256 Blk TriM T00 T01 T10 T11 PL8", 128, "bfloat16")
-_pack("packP", " ".join("P2_%d Pn_%d Cm_%d Ir_%d" % (t, t, t, t) for t in range(RO)), 128, "bfloat16")
-_sb("BO", 8, "bfloat16"), _sb("HW", 224, "bfloat16"), _sb("X MK", 96, "bfloat16"), _sb("mk", 96, "int32"), _sb("L96", 8, "uint16")
-_sb("J0 J1", 160, "float16")
-_sb("PLf onf THl", 128, "float32"), _sb("G2f I1h", 128, "float16")
-for _k in range(8):
-    SCRATCH["B%d" % _k] = ("psum", [128, 512], "float32")
-PB = (0, 1, 7)
-
-CHUNKS = [(0, 128), (128, 256), (256, 384)]
-GATH = [[("a", 0, 64), ("v", 64, 128)], [("a", 128, 256)], [("a", 256, 384)]]
-NCH = len(CHUNKS)
-SUMS = [[("v", 0, 128), ("g", 0, 128)], [("v", 128, 256), ("g", 128, 256)], [("g", 256, 384), ("v", 256, 384)], []]
+_sb("BI8n Bp8", 128, "bfloat16")
+for _n in "T0 T1 G V K D M1 M2".split():
+    SCRATCH[_n] = ("psum", [128, 512], "float32")
 
 
 def rank_program(g, core, T, topo):
@@ -67,19 +57,25 @@ def rank_program(g, core, T, topo):
     sem = {"v": T.sem.sv, "a": T.sem.sa, "p": T.sem.sp, "g": T.sem.sg}
     cnt, clock, snap, hist = {}, {e: {} for e in Q}, {}, {}
 
-    def A(name, c0=0, c1=None, step=1, p=128):
-        name, base, cols = VIEW.get(name, (name, 0, SCRATCH.get(name, (0, (0, 0)))[1][1]))
-        c0, c1 = base + c0, base + (cols if c1 is None else c1)
-        ap = T[name][0:p, c0:c1:step] if step != 1 else T[name][0:p, c0:c1]
-        return (ap, name, c0, c1, step)
+    def A(name, c0=0, c1=None, step=1, p=(0, 128)):
+        c1 = SCRATCH[name][1][1] if c1 is None else c1
+        ap = T[name][p[0]:p[1], c0:c1:step] if step != 1 else T[name][p[0]:p[1], c0:c1]
+        return (ap, name, c0, c1, step, len(range(c0, c1, step)))
+
+    def A3(name, i, j):
+        n, w = SCRATCH[name][1][1:]
+        ri, rj = [range(*x.indices(m)) if isinstance(x, slice) else range(x, x + 1) for x, m in ((i, n), (j, w))]
+        return (T[name][:, i, j], name, ri[0] * w, (ri[-1] + 1) * w, 1, len(ri) * len(rj))
+
+    S = slice
 
     def IND(win, off):
-        return (win[0].indirect(off[0]),) + tuple(win[1:])
+        return (win[0].indirect(off[0]),) + win[1:5] + (16 * off[5], True)
 
     def meet(a, b):
-        if a[1] >= b[2] or b[1] >= a[2]:
+        if a[0] >= b[1] or b[0] >= a[1]:
             return False
-        if a[3] == b[3] and a[3] > 1 and (a[1] - b[1]) % a[3]:
+        if a[2] == b[2] and a[2] > 1 and (a[0] - b[0]) % a[2]:
             return False
         return True
 
@@ -91,12 +87,12 @@ def rank_program(g, core, T, topo):
         for x, wr in [(x, False) for x in reads] + [(x, True) for x in writes]:
             ps = SCRATCH[x[1]][0] == "psum"
             for h in hist.get(x[1], []):
-                hit = meet((0,) + tuple(x[2:]), (0,) + h[1:4])
-                if h[4] != e:
-                    if ps or (hit and (wr or h[6])):
-                        ask(h[4], h[5])
-                elif hit and (wr or h[6]) and e != "p":
-                    ask(h[4], h[5])
+                hit = meet(x[2:5], h[0:3])
+                if h[3] != e:
+                    if ps or (hit and (wr or h[5])):
+                        ask(h[3], h[4])
+                elif hit and (wr or h[5]) and (e != "p" or x[0] is None):
+                    ask(h[3], h[4])
         for f in sorted(want, key=lambda k: -want[k]):
             if clock[e].get(f, 0) < want[f]:
                 Q[e].wait_ge(sem[f], want[f])
@@ -108,485 +104,412 @@ def rank_program(g, core, T, topo):
         snap[(f, n)] = dict(clock[e])
         for x in writes:
             old = hist.get(x[1], [])
-            hist[x[1]] = [h for h in old if not (x[4] == 1 and h[1] >= x[2] and h[2] <= x[3] and (clock[e].get(h[4], 0) >= h[5] or h[4] == f))]
-            hist[x[1]].append((0, x[2], x[3], x[4], f, n, True))
+            hist[x[1]] = [h for h in old if not (x[4] == 1 and h[0] >= x[2] and h[1] <= x[3] and (clock[e].get(h[3], 0) >= h[4] or h[3] == f))]
+            hist[x[1]].append((x[2], x[3], x[4], f, n, True))
         for x in reads:
             L = hist.setdefault(x[1], [])
-            L[:] = [h for h in L if not (not h[6] and h[4] == f and h[1:4] == tuple(x[2:5]))]
-            L.append((0, x[2], x[3], x[4], f, n, False))
+            L[:] = [h for h in L if not (not h[5] and h[3] == f and h[0:3] == x[2:5])]
+            L.append((x[2], x[3], x[4], f, n, False))
 
-    def run(e, make, reads, writes):
+    def issue(e, make, reads, writes, s, n):
         need(e, reads, writes)
         ins = make(Q[e])
-        cnt[e] = cnt.get(e, 0) + 1
-        ins.then_inc(sem[e], 1)
-        note(e, cnt[e], e, reads, writes)
+        if n:
+            if s not in sem:
+                sem[s] = T.sem[s]
+            cnt[s] = cnt.get(s, 0) + n
+            ins.then_inc(sem[s], n)
+            note(s, cnt[s], e, reads, writes)
+
+    ops = []
+
+    def run(e, make, reads, writes, ns):
+        ops.append((e, make, reads, writes, e, 1, ns, HOP))
 
     def dma(e, out, in_, s, oap=None, iap=None):
-        reads, writes = [x for x in (in_,) if x], [x for x in (out,) if x]
-        need(e, reads, writes)
-        Q[e].dma_start(out[0] if out else oap, in_[0] if in_ else iap).then_inc(T.sem[s], 16)
-        sem[s] = T.sem[s]
-        cnt[s] = cnt.get(s, 0) + 16
-        note(s, cnt[s], e, reads, writes)
+        ops.append((e, lambda q: q.dma_start(out[0] if out else oap, in_[0] if in_ else iap), [x for x in (in_,) if x], [x for x in (out,) if x],
+                    s, 16, 100.0, FLIGHT + (out or in_)[5]))
 
-    def mm(out, l, r, start, stop):
-        run("p", lambda q: q.matmul(out[0], l[0], r[0], start, stop), [l, r], [out])
+    def cost(out, ins, c=None):
+        if len(out) > 6:
+            return 50 + out[5] * 3.8 * CYCLE
+        if len(ins[0]) > 6:
+            return 60 + out[5] * 1.56 * CYCLE
+        if c is None:
+            c = 0.5 if all(SCRATCH[x[1]][2] in ("bfloat16", "float16", "uint16") for x in [out] + ins) else 1.0
+        return max(64, out[5] * c) * CYCLE
+
+    def order():
+        last, pre = {}, []
+        for n, op in enumerate(ops):
+            d = set()
+            for x, wr in [(x, False) for x in op[2]] + [(x, True) for x in op[3]]:
+                ps = SCRATCH[x[1]][0] == "psum"
+                for h in last.get(x[1], []):
+                    if ps or (meet(x[2:5], h[0:3]) and (wr or h[4])):
+                        d.add(h[3])
+            for x, wr in [(x, False) for x in op[2]] + [(x, True) for x in op[3]]:
+                ps = SCRATCH[x[1]][0] == "psum"
+                last[x[1]] = [h for h in last.get(x[1], []) if not (ps or (wr and x[4] == 1 and h[0] >= x[2] and h[1] <= x[3]))] + [x[2:5] + (n, wr)]
+            pre.append(d - {n})
+        gap = lambda m, n: 0.0 if ops[m][0] == ops[n][0] == "p" else ops[m][7]
+        way, post = [op[6] for op in ops], [[] for _ in ops]
+        for n in range(len(ops) - 1, -1, -1):
+            for m in pre[n]:
+                post[m].append(n)
+                way[m] = max(way[m], ops[m][6] + gap(m, n) + way[n])
+        left, ready, free, out = [len(d) for d in pre], [0.0] * len(ops), {e: 0.0 for e in Q}, []
+        can = {e: [n for n, op in enumerate(ops) if op[0] == e and not pre[n]] for e in Q}
+        while len(out) < len(ops):
+            t0, e = min((max(free[e], min(ready[n] for n in can[e])), e) for e in Q if can[e])
+            n = max((n for n in can[e] if ready[n] <= t0 + SLACK), key=lambda n: (way[n], -n))
+            can[e].remove(n)
+            out.append(n)
+            free[e] = max(free[e], ready[n]) + ops[n][6]
+            for m in post[n]:
+                ready[m] = max(ready[m], free[e] + gap(n, m))
+                left[m] -= 1
+                if not left[m]:
+                    can[ops[m][0]].append(m)
+        return out
+
+    ROWS = (None, "pc", 200, 201, 1, 1)
+
+    def mm(out, l, r, start=False, stop=False, rows=None):
+        run("p", lambda q: q.matmul(out[0], l[0], r[0], start, stop), [l, r] + [ROWS] * (rows is False), [out] + [ROWS] * (rows is True),
+            max(min(64, l[5]), r[5]) * CYCLE / 2)
 
     def tt(out, a, b, op, xr=()):
-        run("v", lambda q: q.tensor_tensor(out[0], a[0], b[0], op), [a, b] + list(xr), [out])
+        run("v", lambda q: q.tensor_tensor(out[0], a[0], b[0], op), [a, b] + list(xr), [out],
+            cost(out, [a, b], 2.0 if SCRATCH[a[1]][0] == SCRATCH[b[1]][0] else 1.0))
 
     def ts(out, a, s1, op0, s2=None, op1=None):
         xr = [s for s in (s1, s2) if isinstance(s, tuple)]
         v1 = s1[0] if isinstance(s1, tuple) else s1
         v2 = s2[0] if isinstance(s2, tuple) else s2
         if op1 is None:
-            run("v", lambda q: q.tensor_scalar(out[0], a[0], v1, None, op0), [a] + xr, [out])
+            run("v", lambda q: q.tensor_scalar(out[0], a[0], v1, None, op0), [a] + xr, [out], cost(out, [a]))
         else:
-            run("v", lambda q: q.tensor_scalar(out[0], a[0], v1, v2, op0, op1), [a] + xr, [out])
+            run("v", lambda q: q.tensor_scalar(out[0], a[0], v1, v2, op0, op1), [a] + xr, [out], cost(out, [a]))
 
-    def cp(out, a, xr=()):
-        run("v", lambda q: q.tensor_copy(out[0], a[0]), [a] + list(xr), [out])
+    def cp(out, a):
+        run("v", lambda q: q.tensor_copy(out[0], a[0]), [a], [out], cost(out, [a]))
 
     def turn(out, a):
-        run("v", lambda q: q.transpose(out[0], a[0]), [a], [out])
+        run("v", lambda q: q.transpose(out[0], a[0]), [a], [out], cost(out, [a]))
 
     def ms(out, c):
-        run("v", lambda q: q.memset(out[0], c), [], [out])
+        run("v", lambda q: q.memset(out[0], c), [], [out], cost(out, [out]))
 
-    def act(out, a, func=AF.Copy, xr=(), **kw):
-        run("a", lambda q: q.activation(out[0], a[0], func, **kw), [a] + list(xr), [out])
+    def scan(out, d0, d1, init, op0, op1):
+        run("v", lambda q: q.tensor_tensor_scan(out[0], d0[0], d1[0], init, op0, op1), [d0, d1], [out], cost(out, [d0, d1]))
 
-    def iota(out, pattern, base, cm):
-        run("g", lambda q: q.iota(out[0], pattern, base, cm), [], [out])
+    def act(out, a, func=AF.Identity, xr=(), acc=None, **kw):
+        xr = list(xr) + [v for v in kw.values() if isinstance(v, tuple)]
+        kw = {k: (v[0] if isinstance(v, tuple) else v) for k, v in kw.items()}
+        if acc:
+            kw["accum_out"] = acc[0]
+        run("a", lambda q: q.activation(out[0], a[0], func, **kw), [a] + xr, [out] + ([acc] if acc else []), cost(out, [a], 1.0))
+
+    POOL = (None, "pc", 100, 101, 1, 1)
+
+    def iota(out, pattern, base, cm, alone=False):
+        kw = {} if SCRATCH[out[1]][2] == "int32" else {"allow_small_or_imprecise_dtypes": True}
+        run("g", lambda q: q.iota(out[0], pattern, base, cm, **kw), [POOL], [out] + [POOL] * alone, 130 + 2 * out[5] * CYCLE)
 
     def sel(out, a, pattern, op, fill, base, cm):
-        run("g", lambda q: q.affine_select(out[0], a[0], pattern, op, fill, base, cm), [a], [out])
+        run("g", lambda q: q.affine_select(out[0], a[0], pattern, op, fill, base, cm), [a, POOL], [out], 170 + 2 * out[5] * CYCLE)
 
-    B = lambda k, c0=0, c1=C, step=1: A("B%d" % k, c0, c1, step)
+    CH = lambda n, k, c0=0, c1=128, step=1: A(n, 128 * k + c0, 128 * k + c1, step)
+    B = lambda n, c0=0, c1=128, step=1: A(n, c0, c1, step)
+    LAST = lambda n, k=0: CH(n, k, 15, 128, 16)
+    E8 = lambda n: A(n, 0, 8)
+    F = lambda k, p=(0, 128): A("pf", k, k + 1, 1, p)
+    ROW = lambda n, c0=0, c1=128, p=0: A(n, c0, c1, 1, (p, p + 1))
+    I1 = A("R136", 8, BW)
+    LANE = [[0, 8], [1, 16]]
+    rho = lambda t: (5 * t) % 16
 
-    def top(out, src, reset):
-        run("v", lambda q: q.tensor_tensor_scan(out[0], reset[0], src[0], -BIG, ALU.min, ALU.max), [src, reset], [out])
+    dma("y", A3("tsti", S(0, 24), S(0, 16)), None, "ld0", iap=T.tst[:])
+    dma("a", A3("prb", S(0, 24), S(0, 16)), None, "ld1", iap=T.pr[:])
+    dma("y", A("U", LOW, LOW + 2048), None, "ld3", iap=T.cov[:, 0:2048])
+    dma("a", A("U", LOW + 2048, LOW + W), None, "ld4", iap=T.cov[:, 2048:4096])
+    dma("y", A("thi", 0, 1, 1, (0, 8)), None, "ld2", iap=T.th[:])
 
-    LAST = lambda n: A(n, 15, C, 16)
-
-    dma("y", A("tsti"), None, "ld0", iap=T.tst[:])
-    dma("a", A("prb"), None, "ld1", iap=T.pr[:])
-    dma("a", A("thi", 0, 1, 1, 8), None, "ld2", iap=T.th[:])
-    dma("y", A("U", 0, 2048), None, "ld3", iap=T.cov[:, 0:2048])
-    dma("a", A("U", 2048, 4096), None, "ld4", iap=T.cov[:, 2048:4096])
-
-    iota(A("pc", 0, 1), [[0, 1]], 0, 1)
-    iota(A("uA"), [[-1, 128]], 256, 1)
-    iota(A("mB"), [[1, 8], [0, 16]], 0, 0)
-    iota(A("rK"), [[77, RO], [0, 8], [613, 16]], 0, 0)
-    iota(A("r1"), [[0, 8], [-1, 16]], 15, 0)
-    iota(A("iN"), [[1, 160]], -16, 0)
-    iota(A("K"), [[1, 24]], 0, 0)
-    iota(A("pi3"), [[0, 24], [1, 16]], 0, 0)
-    iota(A("sL"), [[32, 4], [1, 2], [2, 16]], 0, 0)
-    iota(A("sG"), [[2, 4], [0, 16], [1, 2]], 0, 0)
-    iota(A("sH"), [[1, 4], [0, 32]], 0, 0)
-    ms(A("ones"), 1.0)
-    iota(A("mk"), [[0, 12], [1, 4], [0, 2]], 0, 0)
-    P = lambda k: A("pc", k, k + 1)
-    F = lambda k: A("pf", k, k + 1)
-    ts(P(1), P(0), 4, ALU.arith_shift_right)
-    ts(P(3), P(0), 15, ALU.bitwise_and)
-    ts(P(2), P(1), 16, ALU.mult)
-    cp(A("pf", 0, 4), A("pc", 0, 4))
-    ts(A("uA"), A("uA"), 15, ALU.bitwise_and)
-    ts(A("uD"), A("mB"), F(1), ALU.subtract, -16.0, ALU.mult)
-    tt(A("uM"), A("uA"), A("uD"), ALU.add)
-    ts(A("Iv"), A("uM"), 0.0, ALU.is_equal, -360448.0, ALU.mult)
-
-    def perms(t):
-        ts(A("P2_%d" % t), A("uM"), t + 1.0, ALU.is_equal, 2.0, ALU.mult)
-        act(A("Pn_%d" % t), A("P2_%d" % t), scale=-256.0)
-        ts(A("Cm_%d" % t), A("uM"), t + 1.0, ALU.is_equal, -131072.0, ALU.mult)
-        tt(A("Cm_%d" % t), A("Cm_%d" % t), A("Iv"), ALU.add)
-
-    def restmats(t):
-        ts(F(12 + t), F(3), float(5 * t % 16), ALU.not_equal)
-        act(A("Ir_%d" % t), A("I1"), scale=F(12 + t)[0], xr=[F(12 + t)])
-    perms(0)
-    row = lambda n, c0=0: A(n, c0, c0 + 128, 1, 1)
-    one = lambda c0=0, c1=C: A("ones", c0, c1, 1, 1)
-
-    def rows(c0, c1):
-        R0 = lambda n: A(n, c0, c1, 1, 1)
-        ts(R0("rKh"), R0("rK"), 8, ALU.arith_shift_right, 15, ALU.bitwise_and)
-        ts(R0("rKhb"), R0("rKh"), 4096.0, ALU.mult)
-        ts(R0("rKl"), R0("rK"), 255, ALU.bitwise_and)
-        ts(R0("rKlb"), R0("rKl"), 16.0, ALU.mult)
-    rows(0, 128)
-    for b in range(2):
-        cp(A("x0", b, C, 2), A("tsti", 192 * b, 192 * b + 192))
-
-    def constants2():
-        ms(A("U", W, W + 16), VOID)
-        ms(A("U", W + 16, UW), 0.0)
-        ts(A("I1"), A("uM"), 0.0, ALU.is_equal)
-        act(A("I16"), A("I1"), scale=16.0)
-        act(A("Im256"), A("I1"), scale=-256.0)
-        act(A("I64k"), A("I1"), scale=65536.0)
-        for b in range(2):
-            act(A("prp", b, C, 2), A("prb", 192 * b, 192 * b + 192))
+    def constants():
+        iota(A("pc", 0, 1), [[0, 1]], 0, 1)
+        iota(A("uA"), [[-1, 128]], 256, 1)
+        iota(A("mB"), [[1, 8], [0, 16]], 0, 0)
+        iota(A("i8"), [[1, 16]], 0, 0)
+        iota(A("w32"), [[1, 32], [0, 16]], 0, -1)
+        iota(A("iN"), [[1, 144]], 0, 0)
+        P = lambda k: A("pc", k, k + 1)
+        ms(A("ones"), 1.0)
+        ts(P(1), P(0), 4, ALU.arith_shift_right)
+        ts(P(2), P(0), 15, ALU.bitwise_and)
+        ts(P(3), P(0), 5, ALU.arith_shift_right)
+        cp(A("pf", 0, 2), A("pc", 1, 3))
+        ts(A("uA"), A("uA"), 15, ALU.bitwise_and)
+        ts(A("uD"), A("mB"), F(0), ALU.subtract, -16.0, ALU.mult)
+        act(F(6), F(1), scale=16.0 * 613)
+        tt(A("uM"), A("uA"), A("uD"), ALU.add)
+        ts(F(7), P(3), -32.0, ALU.mult)
+        ts(I1, A("uM"), 0.0, ALU.is_equal)
+        ts(A("A16", 0, RO), A("i8", 0, RO), 16.0 * 77, ALU.mult, F(6), ALU.add)
+        act(A("I4096"), I1, scale=4096.0)
+        sel(A("R136", 0, 8), A("ones", 0, 8), [[-16, 8]], ALU.is_equal, 0.0, 0, 1)
+        ts(A("W32"), A("w32"), F(7), ALU.is_equal)
+        ms(A("pT"), VOID)
+        ms(A("U", 0, LOW), 0.0), ms(A("U", LOW + W, UW), VOID)
+        for c in range(8):
+            act(A("prp", c, C, 8), A3("prb", S(c, 24, 8), S(0, 16)))
+        for c in range(8):
+            ts(A("x0", c, C, 8), A3("tsti", S(c, 24, 8), S(0, 16)), -1.0, ALU.mult, 256.0, ALU.add)
+        for k in ORDER:
+            mm(B("V", 128 * k, 128 * k + 128), CH("prp", k), I1, True, True)
+            act(A("pT", BW * k + 8, BW * k + BW), B("V", 128 * k, 128 * k + 128))
+        act(F(2), F(0), scale=16.0, bias=15.0)
+        act(F(3), F(1), scale=-136.0, bias=2048.0)
+        act(F(4), F(1), scale=128.0, bias=15.0)
+        act(F(5), F(1), scale=16.0, bias=-256.0)
+        act(A("Rneg"), I1, scale=-65536.0)
+        act(A("I16"), I1, scale=0.0625)
+        iota(A("RK"), [[-16, 8], [-1, 16]], 136, 0)
+        iota(A("RK", 0, 128, 16), [[-1, 8]], 144, 0)
+        ts(A("SEL"), A("iN"), F(2), ALU.is_equal, 4096.0, ALU.mult)
+        ts(E8("BO"), E8("i8"), F(0), ALU.is_equal, 4096.0, ALU.mult)
+        ts(A("Blk"), A("mB"), F(0), ALU.is_equal)
+        ts(A("KT"), A("RK"), F(3), ALU.add)
+        ms(A("LK"), 0.0), ms(A("RV", 0, 128), 0.0), ms(A("TL"), 0.0)
+        iota(ROW("LK", p=32), [[0, 8], [-136, 16]], 2048, 0, True)
+        ms(ROW("LK"), 1.0), ms(ROW("LK", p=64), 1.0), ms(A("LK", 0, 128, 1, (96, 98)), 1.0)
+        ms(ROW("RK", p=32), 1.0), ms(ROW("RK"), 0.0)
+        p8 = (0, 8)
+        sel(A("Blk8", 0, 128, 1, p8), A("ones", 0, 128, 1, p8), [[-1, 8], [0, 16]], ALU.is_equal, 0.0, 0, 1)
+        ts(A("thi", 2, 3, 1, p8), A("thi", 0, 1, 1, p8), 4, ALU.arith_shift_right)
+        ts(A("thi", 3, 4, 1, p8), A("thi", 0, 1, 1, p8), 15, ALU.bitwise_and)
+        ts(A("TL", 96, 97, 1, p8), A("thi", 2, 3, 1, p8), -65536.0, ALU.mult)
+        ts(A("TL", 97, 98, 1, p8), A("thi", 3, 4, 1, p8), -4096.0, ALU.mult)
+        for j in range(2):
+            ts(A("D8", 8 * j, 8 * j + 8, 1, p8), A("Blk8", 0, 128, 16, p8), A("TL", 96 + j, 97 + j, 1, p8), ALU.mult)
+        mm(A("M2", 0, 128, 1, (0, 98)), A("TL", 0, 98, 1, p8), A("Blk8", 0, 128, 1, p8), True, True)
+        for j in range(2):
+            mm(B("M2", 128, 136), A("ones", 0, 128, 1, p8), A("D8", 8 * j, 8 * j + 8, 1, p8), j == 0, j == 1)
+        act(A("RK", 0, 128, 1, (96, 98)), A("M2", 0, 128, 1, (96, 98)))
+        act(E8("THs"), B("M2", 128, 136))
+        act(E8("THn"), B("M2", 128, 136))
+        ms(ROW("RV"), -MAGIC), ms(ROW("RV", 128, 256), -0.46875), ms(ROW("RV", 256, 384), MAGIC)
+        iota(ROW("RV", p=64), [[0, 8], [-256, 16]], 3968, 0, True)
+        iota(ROW("RV", 384, 512), [[0, 8], [-4096, 16]], 63488, 0)
+        sel(A("TriN"), A("Blk"), [[1, 128]], ALU.is_gt, 0.0, 0, -1)
+        tt(A("TriN"), I1, A("TriN"), ALU.subtract)
+        for u in range(2):
+            for g1 in range(2):
+                sel(CH("J", 2 * u + g1), A("ones"), [[32, 4], [1000, 2], [2, 16]], ALU.is_equal, 0.0, u - 1000 * g1, -1)
         for k in range(3):
-            for j in range(4):
-                mm(B(PB[k], j, 512, 4), A("I1"), A("prp", 128 * k, 128 * k + 128), True, True)
-        cp(row("rH"), row("r1"))
-        ts(A("rV", 0, C, 1, 1), A("pi3", 0, C, 1, 1), -256.0, ALU.mult, 3840.0, ALU.add)
-        ts(row("rM"), row("r1"), 4096.0, ALU.mult, 2048.0, ALU.add)
+            ms(A("RT%d" % k, RW, RW + 32), VOID)
+        ms(A("RS0"), BIG), ms(A("RSp"), 0.0), ms(A("X1"), 0.0), ms(A("E3"), 0.0)
+        cp(E8("rep"), E8("i8"))
+        iota(A("si"), LANE, 0, 0)
+        sel(A("Perm"), A("ones"), [[1, 16], [16, 8]], ALU.is_equal, 0.0, 0, -1)
+        act(A("RSm"), A("RS0"))
+        ms(A("RS0", 0, 128, 16), 0.0), ms(A("RSm", 0, 128, 16), -BIG), ms(A("RSp", 0, 128, 16), BIG)
+        act(A("I64k"), I1, scale=65536.0)
+        act(A("PermF"), A("Perm"), scale=FLAG)
+        act(A("PermN"), A("Perm"), scale=-1.0)
+        act(A("Ineg"), I1, scale=-1.0)
+        ts(A("DM"), A("si"), F(1), ALU.is_le)
+        ts(A("MASK"), A("si"), F(1), ALU.is_ge, 2.0 ** 25, ALU.mult)
+        ms(A("DM", 0, 128, 16), 0.0), ms(A("MASK", 15, 128, 16), 2048.0 + LOW)
+        act(A("Bn8"), A("Blk"), scale=-FAR)
+        act(A("Bp8"), A("Blk"), scale=FAR)
+        tt(A("BI8n"), I1, A("Blk"), ALU.subtract)
+        act(A("BI8"), A("BI8n"), scale=-FAR)
+        act(A("BI8n"), A("BI8n"), scale=FAR)
+        ms(A("XS"), 0.0)
+        ts(E8("CV"), E8("i8"), 16.0, ALU.mult, F(4), ALU.add)
+        ts(A("WR"), A("iN"), F(2), ALU.is_equal, F(5), ALU.mult)
+        for t in range(RO):
+            last = t == RO - 1
+            ts(A("XB", t, t + 1), F(1), float(rho(t)), ALU.is_equal, -2176.0 if last else 2176.0, ALU.mult)
+        ts(A("XB", RO - 1, RO), A("XB", RO - 1, RO), 256.0, ALU.add)
+        act(A("onesN"), A("ones"), scale=-1.0)
+        ms(ROW("cst", 0, 1), 127.5), ms(ROW("cst", 1, 2), M256), ms(ROW("cst", 2, 3), -M256)
+        for t in range(RO):
+            ts(CH("Pt", t), A("uM"), t + 1.0, ALU.is_equal, 4096.0, ALU.mult)
+            sel(CH("Tri", t), A("TriN"), LANE, ALU.not_equal, 0.0, -rho(t), 0)
+            sel(CH("Ir", t), I1, LANE, ALU.not_equal, 0.0, -rho(t), 0)
+        sel(A("PermT"), A("onesN"), [[1, 8], [8, 16]], ALU.is_equal, 0.0, 0, -1)
 
-    def constants3():
-        ts(A("BO"), A("iN", 16, 24), F(1), ALU.is_equal, 4096.0, ALU.mult)
-        ts(P(11), P(1), 1, ALU.bitwise_and)
-        ts(P(8), P(11), 999, ALU.mult)
-        ts(P(9), P(11), 999, ALU.mult, -999, ALU.add)
-        tt(P(8), P(0), P(8), ALU.subtract)
-        tt(P(9), P(0), P(9), ALU.add)
-        ts(P(4), P(0), 1, ALU.bitwise_and)
-        ts(P(5), P(0), 31, ALU.bitwise_and)
-        ts(P(6), P(0), 1, ALU.arith_shift_right)
-        ts(P(7), P(0), 5, ALU.arith_shift_right)
-        ts(P(17), P(0), 5, ALU.arith_shift_right)
-        ts(P(18), P(0), 31, ALU.bitwise_and)
-        ts(P(5), P(5), 1, ALU.arith_shift_right)
-        ts(P(7), P(7), 2, ALU.mult)
-        ts(P(10), P(3), W + 16, ALU.add)
-        tt(P(7), P(7), P(4), ALU.add)
-        cp(A("pf", 4, 12), A("pc", 4, 12))
-        cp(A("thf", 0, 1, 1, 8), A("thi", 0, 1, 1, 8))
-        ts(A("mi", 0, 24), A("K", 0, 24), 1, ALU.bitwise_and)
-        ts(A("THl", 0, 128, 1, 8), A("sH", 0, 128, 1, 8), A("pf", 6, 7, 1, 8), ALU.is_equal)
-        ts(A("thR", 0, 24, 1, 8), A("mi", 0, 24, 1, 8), A("pf", 4, 5, 1, 8), ALU.is_equal, 16.0, ALU.mult)
-        ts(A("thR", 0, 24, 1, 8), A("thR", 0, 24, 1, 8), A("thf", 0, 1, 1, 8), ALU.mult)
-        mm(B(6, 0, 24), A("THl", 0, 128, 1, 8), A("thR", 0, 24, 1, 8), True, True)
-        ts(A("I1h"), A("uM"), 0.0, ALU.is_equal)
-        for g2 in range(2):
-            ts(A("J%d" % g2), A("iN"), F(8 + g2), ALU.is_equal)
-        ts(A("Blk"), A("mB"), F(1), ALU.is_equal)
-        sel(A("TriM"), A("Blk"), [[1, 128]], ALU.is_gt, 0.0, 0, -1)
-        ms(A("sT0"), -1000), ms(A("sT1"), -1000)
-        iota(A("sT0", 0, 128, 2), [[32, 4], [1, 2], [2, 8]], 0, 0)
-        iota(A("sT1", 1, 128, 2), [[32, 4], [1, 2], [2, 8]], 0, 0)
-        tt(A("TriM"), A("TriM"), A("I1"), ALU.subtract)
-        cp(A("thb"), B(6, 0, 24))
-        cp(A("thr"), A("thb"))
-        ms(A("RS"), BIG)
-        sel(A("RS"), A("RS"), [[0, 24], [1, 16]], ALU.not_equal, -BIG, 0, 0)
+    def prices(k, n, bank, e):
+        b0, b1 = PIECES[n]
+        for b in range(b0, b1):
+            q = (32 * (b // 4), 32 * (b // 4) + 32)
+            mm(B(bank, BW * (b - b0), BW * (b - b0 + 1)), A("W32", 128 * (b % 4), 128 * (b % 4) + 128, 1, q), A("pT", BW * k, BW * k + BW, 1, q), True, True,
+               b % 4 == 0)
+        (act if e == "a" else cp)(A("PT", RW * k + BW * b0, RW * k + BW * b1), B(bank, 0, BW * (b1 - b0)))
 
-    def constants4():
-        ms(A("GT", 16 * C, GTW), VOID)
-        for q3 in range(2):
-            for g2 in range(2):
-                ts(A("T%d%d" % (q3, g2)), A("sT%d" % g2), 16.0 * q3, ALU.add, F(0), ALU.is_equal)
-        ts(A("CWh"), A("K", 0, 24), 256.0, ALU.mult)
-        ts(A("CWl"), A("ones", 0, 24), F(3), ALU.mult, 16.0, ALU.mult)
-        ts(A("CWl"), A("CWl"), 15.0, ALU.add)
-        cp(A("rep", 0, 24), A("K", 0, 24))
-        ts(A("rep15", 0, 24), A("K", 0, 24), 16.0, ALU.mult, 15.0, ALU.add)
-        restmats(0)
+    def codes(t, k):
+        x = CH("x%d" % t, k)
+        act(CH("nH", k), x, AF.Relu, scale=-16384.0, bias=16384.0)
+        act(CH("aH", k), x, scale=-1.0 / 32, bias=513.0 / 64)
+        mm(B("M1"), CH("Pt", t), CH("aH", k), True)
+        mm(B("M1"), CH("Pt", t), CH("nH", k))
+        mm(B("M1"), A("I4096"), CH("nH", k), False, True)
+        tt(CH("t1", k), CH("aH", k), B("M1"), ALU.mult)
+        ts(CH("t2", k), CH("t1", k), A("A16", t, t + 1), ALU.add)
+        ts(CH("t3", k), CH("t2", k), 4, ALU.arith_shift_right, 0x7FFF0FFF, ALU.bitwise_and)
+        ts(CH("cu", k), CH("t3", k), 4096.0, ALU.min, float(LOW), ALU.add)
+        mm(B("M1", 128, 256), CH("nH", k), CH("Tri", t), True, True)
+        act(CH("FQ", k), B("M1", 128, 256), AF.Relu, scale=1.0 / 16384)
+        ts(CH("cf", k), CH("cu", k), -2048.0 - LOW, ALU.add, 2047.0, ALU.min)
+        for c in range(4):
+            turn(A3("TT", 4 * k + c, S(0, 32)), CH("cf", k, c, 128, 4))
 
-    def constants4b():
-        cp(A("pf", 17, 19), A("pc", 17, 19))
-        ms(A("HW"), 0.0)
-        ts(A("L1", 0, 6), A("K", 0, 6), 16.0, ALU.mult, F(3), ALU.add)
-        ts(A("L2", 0, 6), A("L1", 0, 6), 43.0, ALU.mult)
-        ts(A("MK"), A("mk"), F(17), ALU.is_equal)
-        ts(A("HW", 96, 128), A("iN", 16, 48), F(18), ALU.is_equal)
-        ts(A("L2", 0, 6), A("L2", 0, 6), 10, ALU.arith_shift_right)
-        ts(A("L3", 0, 6), A("L2", 0, 6), -24.0, ALU.mult)
-        tt(A("L1", 0, 6), A("L1", 0, 6), A("L3", 0, 6), ALU.add)
-        ts(A("L2", 0, 6), A("L2", 0, 6), 2.0, ALU.mult)
-        ts(A("L3", 0, 6), A("L1", 0, 6), 1, ALU.bitwise_and)
-        ts(A("L1", 0, 6), A("L1", 0, 6), 24, ALU.bitwise_and)
-        tt(A("L2", 0, 6), A("L2", 0, 6), A("L3", 0, 6), ALU.add)
-        tt(A("L1", 0, 6), A("L1", 0, 6), A("L2", 0, 6), ALU.add)
-        cp(A("L96", 0, 6), A("L1", 0, 6))
+    def gains(t, k):
+        got, RT = "got%d" % k, "RT%d" % k
+        for b0, b1 in GATHERS:
+            off = CH("cu", k, 8 * b0, 8 * b1)
+            act(A(got, 128 * b0, 128 * b1), IND(A("U"), off), AF.Copy, xr=[off])
+        mm(B("G"), A3("prb", S(8 * k, 8 * k + 8), S(0, 16)), A("Rneg"), True)
+        mm(B("G"), A("LK", 0, 128, 1, (0, 98)), A("RK", 0, 128, 1, (0, 98)))
+        for n, (b0, b1) in enumerate(PIECES):
+            bank = "T%d" % (n % 2)
+            for b in range(b0, b1):
+                mm(B(bank, BW * (b - b0), BW * (b - b0 + 1)), A(got, 128 * b, 128 * b + 128), A("R136"), True, True)
+            tt(A(RT, BW * b0, BW * b1), B(bank, 0, BW * (b1 - b0)), A("PT", RW * k + BW * b0, RW * k + BW * b1), ALU.max)
+            for b in range(b0, b1):
+                mm(B("G"), A("SEL", 15 - b, 143 - b), A(RT, BW * b + 8, BW * b + BW), False, b == 15)
 
-    def constants5():
-        ts(A("MD"), A("pi3"), F(5), ALU.is_equal)
-        ts(A("MO"), A("pi3"), F(5), ALU.is_ge, 32768.0, ALU.mult)
-        ts(A("PLf"), A("sL"), F(0), ALU.is_equal)
-        act(A("PL8"), A("PLf"), scale=8192.0)
-        ts(A("G2f"), A("sG"), F(7), ALU.is_equal)
-        act(A("onf"), A("I1"), AF.Identity, scale=0.0, bias=16.0)
-        act(A("RSb", 0, C), A("RS"))
-        act(A("RSb", C, C + 192), A("RS", 0, 192))
-        L1, L2, L3 = A("L1"), A("L2"), A("L3")
-        ts(L1, A("K"), 12.0, ALU.is_ge)
-        ts(L2, L1, -12.0, ALU.mult)
-        tt(L2, L2, A("K"), ALU.add)
-        ts(L1, L1, 2.0, ALU.mult)
-        ts(L3, L2, 1, ALU.bitwise_and)
-        ts(L2, L2, 2.0, ALU.mult)
-        tt(L1, L1, L3, ALU.subtract)
-        tt(L1, L1, L2, ALU.add)
-        cp(A("RP", 0, 24), L1)
-        ts(F(19), F(10), 16.0, ALU.add)
-
-    def constants6(t):
-        rows(128 * t, 128 * t + 128)
-        perms(t)
-        restmats(t)
-
-    def constants7():
-        act(A("RY"), A("U", 0, W // 2), AF.Identity, scale=0.0, bias=1.0)
-        sel(A("RY"), A("RY"), [[0, W // 32], [1, 16]], ALU.not_equal, 0.0, 0, 0)
-
-    def codes0(t):
-        mm(B(2), one(0, 128), one(), True, False)
-        mm(B(3), row("rKhb", 128 * t), one(), True, False)
-        mm(B(3), row("rKlb", 128 * t), one(), False, False)
-
-    def codes1(t):
-        x = A("x%d" % t)
-        act(A("nn"), x, AF.Relu, bias=-255.0)
-        act(A("aS"), x, AF.Identity, bias=1.0, scale=2.0)
-        mm(B(2), A("P2_%d" % t), x, False, False)
-        mm(B(2), A("Pn_%d" % t), A("nn"), False, True)
-        mm(B(3), A("Cm_%d" % t), A("nn"), False, True)
-
-    def codes2(t):
-        for c0, c1 in (CHUNKS[0], (CHUNKS[0][1], C)):
-            tt(A("t1", c0, c1), A("aS", c0, c1), B(2, c0, c1), ALU.mult)
-            tt(A("t2", c0, c1), A("t1", c0, c1), B(3, c0, c1), ALU.add)
-            ts(A("t3", c0, c1), A("t2", c0, c1), 4, ALU.arith_shift_right, 0x8FFF, ALU.bitwise_and)
-            ts(A("cu", c0, c1), A("t3", c0, c1), 4096, ALU.min)
-
-    def starts(t):
-        mm(B(4), row("rH"), one(), True, False)
-        mm(B(4), A("Im256"), A("prp"), False, False)
-
-    def starts1(t):
-        mm(B(5), one(0, 128), A("rV", 0, C, 1, 1), True, False)
-
-    def starts2(t):
-        mm(B(3), A("TriM"), A("nn"), True, False)
-        mm(B(3), one(0, 128), one(), False, True)
-        mm(B(2), A("I1h"), A("cf"), True, True)
-
-    def starts3(t):
-        mm(B(6), row("rM"), one(), True, False)
-        for b in range(2):
-            for g2 in range(2):
-                s = 16 + 16 * (g2 - b)
-                mm(B(6, g2, C, 2), A("J%d" % g2, s, s + 128), A("cf", b, C, 2), False, False)
-
-    def highs(t):
-        act(A("h0"), B(2), AF.Identity, bias=128.0 - 0.46875, scale=0.0625)
-        act(A("h1"), A("h0"), AF.Identity, bias=MAGIC)
-        act(A("FO"), B(3), AF.Relu, bias=1.0, scale=-1.0)
-        act(A("hib"), A("h1"), AF.Identity, bias=-MAGIC)
-
-    def gather(k):
-        for e, c0, c1 in GATH[k]:
-            out, win, off = A("got", 16 * c0, 16 * c1), A("U"), A("cu", c0, c1)
-            (act if e == "a" else cp)(out, IND(win, off), xr=[off])
-
-    def price(k):
-        c0, c1 = CHUNKS[k]
-        n, f = 4 * (c1 - c0), 4 * (c0 % 128)
-        for s in range(4):
-            r = 4 * C * s + 4 * c0
-            tt(A("R", r, r + n), A("got", 16 * c0 + s, 16 * c1, 4), B(PB[c0 // 128], f, f + n), ALU.max)
-
-    def gains(c0, c1):
+    def votes(k):
+        mm(B("V"), ROW("ones"), ROW("RV", 128, 256), True)
+        mm(B("V"), CH("cf", k), A("I16"))
+        mm(B("V"), ROW("ones"), ROW("RV", 256, 384))
+        mm(B("V"), A("LK", 0, 128, 1, (0, 65)), A("RV", 0, 128, 1, (0, 65)))
         for i in range(16):
-            r = 4 * C * (i % 4) + i // 4
-            mm(B(4, c0, c1), A("I16"), A("R", r + 4 * c0, r - i // 4 + 4 * c1, 4), False, c1 == C and i == 15)
+            mm(B("V", i, 128, 16), A("got%d" % k, i, 2048, 16), E8("BO"))
 
-    def votes(c0, c1):
-        for i in range(16):
-            mm(B(5, c0 + i, c1, 16), A("got", 16 * c0 + i, 16 * c1, 16), A("BO"), False, False)
+    def best(k):
+        scan(CH("KS", k), A("RS0"), B("G"), 0.0, ALU.min, ALU.max)
+        ts(A("ka"), LAST("KS", k), 4095, ALU.bitwise_and)
+        ts(E8("wl"), A("ka"), -1.0, ALU.mult, float(NOWT), ALU.add)
+        act(A("pk"), IND(A("RT%d" % k), E8("wl")), AF.Copy, xr=[E8("wl")])
+        tt(A("OH"), IND(A("ka"), E8("rep")), A("KT"), ALU.is_equal, xr=[E8("rep")])
+        mm(B("M2"), A("OH"), A("Perm"), True, True)
+        act(CH("nB", k), B("M2"), scale=-1.0, bias=1.0, acc=A("acc", k, k + 1))
 
-    def sums(L):
-        for what, c0, c1 in L:
-            (gains if what == "g" else votes)(c0, c1)
+    def claims(k):
+        mm(B("K"), ROW("ones"), ROW("RV", 384, 512), True)
+        for u in range(2):
+            for g1 in range(2):
+                mm(B("K", 64 * u, 64 * u + 64), CH("J", 2 * u + g1), A3("TT", S(4 * k, 4 * k + 4), S(16 * g1, 16 * g1 + 16)))
+        mm(B("K"), A("pk"), A("I64k"), False, True)
+        scan(A("MS"), A("RSm"), B("K"), -BIG, ALU.min, ALU.max)
+        ts(E8("xp"), LAST("MS"), 4095 - 2 ** 31, ALU.bitwise_and)
+        ts(A("X1", 0, 128, 16), E8("xp"), -2048.0, ALU.add, -2048.0 - LOW, ALU.max)
+        scan(B("XS"), A("DM"), A("X1"), 0.0, ALU.mult, ALU.add)
+        mm(B("D"), I1, A("MASK"), True)
+        mm(B("D"), A("BI8"), B("XS"))
+        mm(B("D"), A("Bn8"), B("XS", 1, 129))
+        mm(LAST("D"), A("BI8n"), LAST("XS"))
+        mm(LAST("D"), A("Bp8"), A("XS", 16, 144, 16))
+        mm(LAST("D"), I1, A("X1", 0, 128, 16), False, True)
+        act(A("DA"), B("D"), AF.Abs)
+        ts(E8("y1"), LAST("MS"), 12, ALU.arith_shift_right, 15, ALU.bitwise_and)
+        tt(E8("y2"), E8("CV"), E8("y1"), ALU.subtract)
+        cp(E8("lv"), E8("y2"))
+        act(CH("Vr", k), IND(A("got%d" % k), E8("lv")), AF.Copy, xr=[E8("lv")])
+        scan(A("LS"), A("RSp"), A("DA"), 0.0, ALU.max, ALU.min)
+        ts(A("oL", 16 * k, 16 * k + 16, 2), LAST("LS"), F(1), ALU.max)
 
-    def gturn(k):
-        c0, c1 = CHUNKS[k]
-        turn(A("GT", 16 * c0, 16 * c1), A("got", 16 * c0, 16 * c1))
+    def scatter(k, c):
+        o = A("oL", 16 * k + 2 * c, 16 * k + 2 * c + 1)
+        tt(IND(A("U"), o), CH("Vr", k, 16 * c, 16 * c + 16), CH("nB", k, c, 128, 8), ALU.mult, xr=[o])
 
-    def best1(t):
-        turn(A("KQ"), B(4))
-        top(A("KS"), A("KQ"), A("RS"))
-        ts(A("Ai"), LAST("KS"), 15, ALU.bitwise_and)
-        tt(A("z"), LAST("KS"), A("thr"), ALU.is_lt)
-        ts(A("z8"), A("z"), 8192.0, ALU.mult)
-        tt(A("val"), A("z8"), A("Ai"), ALU.subtract)
-        mm(B(4, 0, 24), A("I1"), A("CWh"), True, False)
-        mm(B(4, 0, 24), A("I1"), A("CWl"), False, False)
-        for q3 in range(2):
-            for g2 in range(2):
-                mm(B(4, q3, 24, 2), A("T%d%d" % (q3, g2)), A("val", g2, 24, 2), False, q3 == 1 and g2 == 1)
+    def places(t, k):
+        tt(E8("r1"), LAST("KS", k), E8("THn"), ALU.subtract)
+        ts(E8("r2"), E8("r1"), 12, ALU.arith_shift_right, 15, ALU.bitwise_and)
+        tt(LAST("E3"), E8("r2"), LAST("KS", k), ALU.min)
+        mm(B("V"), A("PermF"), A("OH"), False, True)
+        scan(A("VS"), A("RSm"), B("V"), -BIG, ALU.min, ALU.max)
+        ts(E8("vx"), LAST("VS"), 255 + 3 * 2 ** 24, ALU.bitwise_and)
+        ts(E8("tkb"), E8("vx"), 256.0, ALU.min, -256.0, ALU.add)
+        tt(A("E2"), IND(E8("tkb"), E8("rep")), CH("FQ", k), ALU.mult, xr=[E8("rep")])
+        s, X = 15 - rho(t), lambda c0=0, c1=128: B("M2", 128 + c0, 128 + c1)
+        if t == RO - 1:
+            mm(X(), A("E3", s, s + 128), A("Ineg"), True)
+            for c in range(8):
+                mm(X(16 * c, 16 * c + 16), CH("Ir", t), CH("x%d" % t, k, c, 128, 8))
+                mm(X(16 * c, 16 * c + 16), A("WR", s, s + 128), CH("nB", k, c, 128, 8))
+            mm(X(), A("E2"), A("PermT"), False, True)
+            act(CH("yo", k), X(), scale=-1.0, bias=A("XB", t, t + 1))
+            dma("y", None, CH("yo", k), "o%d" % k, oap=T.yt[:, 128 * k:128 * k + 128])
+            return
+        mm(X(), CH("Ir", t), CH("x%d" % t, k), True)
+        mm(X(), A("WR", s, s + 128), CH("nB", k))
+        mm(X(), A("E3", s, s + 128), A("PermN"))
+        mm(X(), A("E2"), A("Ineg"), False, True)
+        xo = CH("xo", 3 * t + k)
+        act(xo, X(), bias=A("XB", t, t + 1))
+        to, src = T.cores[(rank + 1) % len(T.cores)], T.cores[(rank - 1) % len(T.cores)]
+        rid, pid = topo.addr(to, core)
+        eng = topo.engines(core, to)[:8]
+        a, dst = "arr%d_%d" % (t + 1, k), CH("x%d" % (t + 1), k)
 
-    def best2(t):
-        ts(A("wl", 0, 24), B(4, 0, 24), 16.0 * C, ALU.min)
-        act(A("wt"), IND(A("GT"), A("wl", 0, 24)), xr=[A("wl", 0, 24)])
-
-    def notb(t):
-        tt(A("nBQ"), IND(A("KS"), A("rep15", 0, 24)), A("KQ"), ALU.not_equal, xr=[A("rep15", 0, 24)])
-        turn(A("nB"), A("nBQ"))
-
-    def level(t):
-        ts(A("Bi"), LAST("KS"), 4, ALU.arith_shift_right, 15, ALU.bitwise_and)
-        ts(A("Cc"), A("val"), 16.0, ALU.mult, 240.0, ALU.add)
-        tt(A("Dd"), A("Bi"), A("Cc"), ALU.add)
-
-    def vote(t):
-        top(A("VS"), B(5), A("RS"))
-
-    def update(t):
-        rho, xo = (5 * t) % 16, "xo%d" % (t % 2)
-        ts(A("Av"), LAST("VS"), 255, ALU.bitwise_and)
-        ts(A("al"), LAST("VS"), 0.0, ALU.is_ge)
-        ts(A("tkm"), A("Av"), -256.0, ALU.add)
-        tt(A("tkr"), A("tkm"), A("al"), ALU.mult)
-        tt(A("X"), IND(A("tkr"), A("L96", 0, 6)), A("MK"), ALU.mult, xr=[A("L96", 0, 6)])
-        level(t)
-        for a in range(4):
-            mm(B(5, 0, 24), A("HW", 96 - 32 * a, 224 - 32 * a), A("X", 24 * a, 24 * a + 24), a == 0, a == 3)
-        mm(B(6), A("I64k"), A("wt"), False, True)
-        useless(t)
-        tt(A("tkb"), B(5, 0, 24), A("z"), ALU.mult)
-        tt(A("E2"), IND(A("tkb"), A("rep", 0, 24)), A("FQ"), ALU.mult, xr=[A("rep", 0, 24)])
-        ts(A("E2", rho, C, 16), A("Dd"), 256.0, ALU.min)
-        turn(A("E2T"), A("E2"))
-        mm(B(5), A("Ir_%d" % t), A("x%d" % t), True, False)
-        mm(B(5), A("I1"), A("E2T"), False, True)
-        act(A(xo), B(5))
-        if t < RO - 1:
-            to = T.cores[(rank + 1) % len(T.cores)]
-            rid, pid = topo.addr(to, core)
-            eng = topo.engines(core, to)[:8]
-            need("g", [A(xo)], [])
-            s, a = "st%d" % (t % 2), "arr%d" % (t + 1)
-            g.remote_dma(T["x%d" % (t + 1)][:, :], A(xo)[0], T.sem[a], T.sem[s], pid, rid, sum(1 << k for k in eng))
-            sem[s] = T.sem[s]
-            cnt[s] = cnt.get(s, 0) + len(eng)
-            note(s, cnt[s], "g", [A(xo)], [])
-            src = T.cores[(rank - 1) % len(T.cores)]
+        def write(q):
+            q.remote_dma(dst[0], xo[0], T.sem[a], T.sem.st, pid, rid, sum(1 << e for e in eng))
+            sem["st"], cnt["st"] = T.sem.st, cnt.get("st", 0) + len(eng)
             sem[a], cnt[a] = T.sem[a], len(topo.engines(src, core)[:8])
             snap[(a, cnt[a])] = {}
-            hist["x%d" % (t + 1)] = [(0, 0, C, 1, a, cnt[a], True)]
+            hist.setdefault(dst[1], []).append(dst[2:5] + (a, cnt[a], True))
+        ops.append(("g", write, [xo], [dst], "st", 0, 600.0, FLIGHT + 500))
 
-    def useless(t):
-        if t == RO - 1:
-            return
-        one1 = A("zr", 0, 1)
-        run("a", lambda q: q.activation(A("zc")[0], A("z")[0], AF.Copy, accum_out=one1[0]), [A("z")], [A("zc"), one1])
-        mm(B(3, 0, 1), A("onf"), one1, True, True)
-        act(A("ma", 0, 1), B(3, 0, 1), AF.Identity, scale=1.0 / 4096, bias=-255.0 / 512)
-        act(A("mb", 0, 1), A("ma", 0, 1), AF.Identity, bias=MAGIC)
-        act(A("mc", 0, 1), A("mb", 0, 1), AF.Identity, scale=-4096.0, bias=4096.0 * MAGIC)
-        act(A("mf", 0, 1), B(3, 0, 1))
+    def useless():
+        m = B("M1", 256, 257)
+        act(A("acch", 0, 3), A("acc", 0, 3), bias=-64.0)
+        mm(m, ROW("ones"), ROW("cst", 0, 1), True)
+        for k in range(3):
+            mm(m, A("onesN"), A("acch", k, k + 1))
+        mm(m, ROW("ones"), ROW("cst", 1, 2))
+        mm(m, ROW("ones"), ROW("cst", 2, 3))
+        for k in range(3):
+            mm(m, A("ones"), A("acch", k, k + 1), False, k == 2)
+        act(A("mneg", 0, 1), m, scale=-4096.0)
+        act(ROW("RK"), ROW("ones"), scale=A("mneg", 0, 1, 1, (0, 1)))
+        act(E8("THn"), E8("THs"), bias=A("mneg", 0, 1))
 
-    def limits(t):
-        if t < RO - 1:
-            ts(A("thr"), A("thb"), A("mf", 0, 1), ALU.add, A("mc", 0, 1), ALU.add)
-
-    def claims1(t):
-        turn(A("KM"), B(6))
-        top(A("MS"), A("KM"), A("RS"))
-        ts(A("xp"), LAST("MS"), (1 << 24) | 4095, ALU.bitwise_and)
-        ts(A("xpf"), A("xp"), -2048.0, ALU.add, 32768.0, ALU.min)
-        rp = A("RP", 0, 24)
-        mm(B(4), A("I1"), A("MO"), True, False)
-        tt(A("xd"), IND(A("xpf"), rp), A("MD"), ALU.mult, xr=[rp])
-        mm(B(4), A("G2f"), A("xd"), False, True)
-        mm(B(6, 0, 192), A("G2f"), A("xd", 0, 192), True, True)
-        act(A("RBs", 0, C), B(4))
-        act(A("RBs", C, C + 192), B(6, 0, 192))
-
-    def claims2(t):
-        for rp, c0, c1 in ((A("RP", 0, 24), 0, C), (A("RP", 12, 24), C, C + 192)):
-            tt(A("Eq", c0, c1), IND(A("xpf"), rp), A("RBs", c0, c1), ALU.is_equal, xr=[rp])
-        top(A("lost"), A("Eq"), A("RSb"))
-        mm(B(4, 0, 24), A("I1"), A("HW", 0, 24), True, False)
-        for b in range(2):
-            mm(B(4, 12 * b, 12 * b + 12), A("PLf"), A("xpf", b, 24, 2), False, False)
-        for n in range(3):
-            for b in range(2):
-                h = min(n, 1)
-                mm(B(4, 12 * b + h, 12 * b + 12, 2), A("PL8"), A("lost", 15 + 16 * (12 * n + b), 192 * n + 192, 32), False, n == 2 and b == 1)
-        limits(t)
-
-    def claims3a(t):
-        for h in range(2):
-            ts(A("oG", h, 24, 2), B(4, h, 24, 2), 2048.0, ALU.add, F(10 + 9 * h), ALU.min)
-
-    def claims3(t):
-        for b in range(2):
-            o = A("oG", 12 * b, 12 * b + 12)
-            tt(A("V", 192 * b, 192 * b + 192), IND(A("U"), o), A("nB", b, C, 2), ALU.mult, xr=[o])
-        for b in (1, 0):
-            for k in range(5, -1, -1):
-                o = A("oG", 12 * b + 2 * k, 12 * b + 2 * k + 2)
-                cp(IND(A("U"), o), A("V", 192 * b + 32 * k, 192 * b + 32 * k + 32), xr=[o])
-
-    codes0(0)
-    codes1(0)
-    constants2()
-    constants3()
-    codes2(0)
+    constants()
+    for n in range(6):
+        prices(ORDER[0], n, "T%d" % (n % 2), "av"[n % 2])
     for t in range(RO):
-        if t == 0:
-            starts(t)
-            starts1(t)
-        ts(A("cf"), A("t3"), 4096, ALU.min, -2048.0, ALU.add)
-        for k in range(NCH):
-            gather(k)
-        starts2(t)
-        starts3(t)
-        for k in range(NCH):
-            price(k)
-            gturn(k)
-            sums(SUMS[k])
-            if t == 0 and k == 0:
-                constants4()
-            if t == 0 and k == 1:
-                constants4b()
-        highs(t)
-        if t == 1:
-            constants7()
+        for k in ORDER:
+            if not (t and k == ORDER[0]):
+                codes(t, k)
+            if t == 0 and k != ORDER[0]:
+                for n in range(6):
+                    prices(k, n, "K", "v")
+            gains(t, k)
+            votes(k)
+            best(k)
+            claims(k)
+            places(t, k)
         if t < RO - 1:
-            constants6(t + 1)
-        turn(A("FQ"), A("FO"))
-        for c0, c1 in CHUNKS:
-            mm(B(5, c0, c1), A("hib", c0, c1), A("I1"), False, c1 == C)
-        best1(t)
-        vote(t)
-        best2(t)
-        if t == 0:
-            constants5()
-        update(t)
-        claims1(t)
-        if t < RO - 1:
-            codes0(t + 1)
-        notb(t)
-        claims2(t)
-        claims3a(t)
-        if t < RO - 1:
-            starts(t + 1)
-            codes1(t + 1)
-            starts1(t + 1)
-        claims3(t)
-        if t < RO - 1:
-            codes2(t + 1)
+            codes(t + 1, ORDER[0])
+            useless()
+        for k in ORDER:
+            for c in range(7, -1, -1):
+                scatter(k, c)
 
-    top2 = [A("ys"), A("RY"), A("U", 0, W // 2)]
-    run("v", lambda q: q.tensor_tensor_scan(top2[0][0], top2[1][0], top2[2][0], 0.0, ALU.mult, ALU.add), top2[1:], top2[:1])
-    for k in range(16):
-        mm(B(4, 0, 128), A("I1"), A("U", W // 2 + k, W, 16), k == 0, k == 15)
-    for b in range(2):
-        act(A("yo", 192 * b, 192 * b + 192), A("xo0", b, C, 2))
-    dma("a", None, A("yo"), "out", oap=T.yt[:])
-    act(A("yco", 128, 256), B(4, 0, 128))
-    cp(A("yco", 0, 128), A("ys", 15, W // 2, 16))
-    dma("y", None, A("yco"), "out2", oap=T.yc[:])
+    for h in range(2):
+        for j in range(16):
+            mm(B("T%d" % h), I1, A("U", LOW + 2048 * h + j, LOW + 2048 * h + 2048, 16), j == 0, j == 15)
+        act(CH("yco", h), B("T%d" % h))
+        dma("a" if h else "y", None, CH("yco", h), "o%d" % (3 + h), oap=T.yc[:, 128 * h:128 * h + 128])
+
+    if not PLAN:
+        PLAN.extend(order())
+    for n in PLAN:
+        issue(*ops[n][:6])
     for s in sem:
         if cnt.get(s, 0):
             g.wait_ge(sem[s], cnt[s])

@@ -3,7 +3,7 @@ from concourse.mybir import AluOpType as ALU, AxisListType as AX, ActivationFunc
 
 C, W, RO = 384, 4096, 5
 VOID = -2.0
-LOW = 16
+LOW = 64
 UW = LOW + W + 16
 BW = 136
 RW = 16 * BW
@@ -11,9 +11,9 @@ NOWT = RW + 16
 MAGIC = 12582912.0
 M256 = 256 * MAGIC
 BIG = 2.0 ** 30
-FAR = 4224.0
+FAR = 8192.0
 FLAG = 2.0 ** 24 + 2.0 ** 18
-CYCLE, HOP, FLIGHT, SLACK = 0.83, 100.0, 2500.0, 40.0
+CYCLE, HOP, FLIGHT, SLACK = 0.83, 200.0, 2500.0, 40.0
 ORDER = (2, 1, 0)
 PIECES = ((0, 3), (3, 6), (6, 9), (9, 12), (12, 14), (14, 16))
 GATHERS = ((0, 6), (6, 12), (12, 16))
@@ -31,20 +31,20 @@ def _sb(names, cols, dtype):
 
 _sb("U", UW, "bfloat16")
 _sb("tsti", [24, 16], "int32"), _sb("prb", [24, 16], "bfloat16")
-_sb("prp FQ Vr nB x0 x1 x2 x3 x4", C, "bfloat16"), _sb("xo", 4 * C, "bfloat16")
+_sb("prp FQ Vr nB", C, "bfloat16"), _sb("x0 x1 x2 x3 x4", C, "float16"), _sb("xo", 4 * C, "float16"), _sb("Im32", 128, "bfloat16")
 _sb("got0 got1 got2", 2048, "bfloat16"), _sb("RT0 RT1 RT2", RW + 32, "bfloat16"), _sb("PT", 3 * RW, "bfloat16")
 _sb("pT", 3 * BW, "bfloat16")
-_sb("aH nH cf", C, "float16"), _sb("TT", [12, 32], "float16"), _sb("XS", 144, "float16"), _sb("X1", 128, "float16")
+_sb("nH cf", C, "float16"), _sb("TT", [12, 32], "float16"), _sb("XD", 128, "float16"), _sb("X1", 8, "float32")
+_sb("DA LS", 528, "float32"), _sb("RSp", 528, "bfloat16"), _sb("MASK", 512, "bfloat16")
 _sb("t1 yo", C, "float32"), _sb("t2 t3 KS", C, "int32"), _sb("cu", C, "uint16")
-_sb("MS VS uA mB si", 128, "int32"), _sb("DA LS KT uM uD", 128, "float32")
+_sb("MS VS uA mB si", 128, "int32"), _sb("KT uM uD", 128, "float32")
 _sb("ka", 8, "int32"), _sb("tkb", 16, "bfloat16")
 _sb("xp y1 y2 r1 r2 vx i8 pc thi", 16, "int32"), _sb("wl lv rep", 16, "uint16"), _sb("oL", 48, "uint16")
 _sb("pf CV THs THn A16 XB acc mneg", 16, "float32"), _sb("acch cst D8 BO", 16, "bfloat16")
-_sb("pk OH E2 ones onesN Blk Blk8 I4096 I16 I64k Ineg Rneg TriN Perm PermN PermF PermT BI8 Bn8 LK RK TL MASK DM RS0 RSm RSp", 128, "bfloat16")
+_sb("pk OH E2 ones onesN Blk Blk8 I4096 I16 I64k Ineg Rneg TriN Perm PermN PermF PermT LK RK TL DG RS0 RSm", 128, "bfloat16")
 _sb("R136", BW, "bfloat16"), _sb("SEL WR E3", 144, "bfloat16"), _sb("iN", 144, "int32")
 _sb("Pt Tri Ir", RO * 128, "bfloat16"), _sb("J RV W32 w32", 512, "bfloat16")
 _sb("yco", 256, "float32")
-_sb("BI8n Bp8", 128, "bfloat16")
 for _n in "T0 T1 G V K D M1 M2".split():
     SCRATCH[_n] = ("psum", [128, 512], "float32")
 
@@ -142,17 +142,17 @@ def rank_program(g, core, T, topo):
     def order():
         last, pre = {}, []
         for n, op in enumerate(ops):
-            d = set()
+            d = {}
             for x, wr in [(x, False) for x in op[2]] + [(x, True) for x in op[3]]:
                 ps = SCRATCH[x[1]][0] == "psum"
                 for h in last.get(x[1], []):
                     if ps or (meet(x[2:5], h[0:3]) and (wr or h[4])):
-                        d.add(h[3])
+                        d[h[3]] = max(d.get(h[3], 0.0), 0.0 if ps and ops[h[3]][0] == op[0] else ops[h[3]][7])
             for x, wr in [(x, False) for x in op[2]] + [(x, True) for x in op[3]]:
                 ps = SCRATCH[x[1]][0] == "psum"
                 last[x[1]] = [h for h in last.get(x[1], []) if not (ps or (wr and x[4] == 1 and h[0] >= x[2] and h[1] <= x[3]))] + [x[2:5] + (n, wr)]
-            pre.append(d - {n})
-        gap = lambda m, n: 0.0 if ops[m][0] == ops[n][0] == "p" else ops[m][7]
+            pre.append(d)
+        gap = lambda m, n: pre[n][m]
         way, post = [op[6] for op in ops], [[] for _ in ops]
         for n in range(len(ops) - 1, -1, -1):
             for m in pre[n]:
@@ -173,11 +173,8 @@ def rank_program(g, core, T, topo):
                     can[ops[m][0]].append(m)
         return out
 
-    ROWS = (None, "pc", 200, 201, 1, 1)
-
-    def mm(out, l, r, start=False, stop=False, rows=None):
-        run("p", lambda q: q.matmul(out[0], l[0], r[0], start, stop), [l, r] + [ROWS] * (rows is False), [out] + [ROWS] * (rows is True),
-            max(min(64, l[5]), r[5]) * CYCLE / 2)
+    def mm(out, l, r, start=False, stop=False):
+        run("p", lambda q: q.matmul(out[0], l[0], r[0], start, stop), [l, r], [out], max(min(64, l[5]), r[5]) * CYCLE / 2)
 
     def tt(out, a, b, op, xr=()):
         run("v", lambda q: q.tensor_tensor(out[0], a[0], b[0], op), [a, b] + list(xr), [out],
@@ -264,7 +261,7 @@ def rank_program(g, core, T, topo):
         for c in range(8):
             act(A("prp", c, C, 8), A3("prb", S(c, 24, 8), S(0, 16)))
         for c in range(8):
-            ts(A("x0", c, C, 8), A3("tsti", S(c, 24, 8), S(0, 16)), -1.0, ALU.mult, 256.0, ALU.add)
+            ts(A("x0", c, C, 8), A3("tsti", S(c, 24, 8), S(0, 16)), 1.0 / 32, ALU.mult, 1.0 / 64, ALU.add)
         for k in ORDER:
             mm(B("V", 128 * k, 128 * k + 128), CH("prp", k), I1, True, True)
             act(A("pT", BW * k + 8, BW * k + BW), B("V", 128 * k, 128 * k + 128))
@@ -308,56 +305,53 @@ def rank_program(g, core, T, topo):
                 sel(CH("J", 2 * u + g1), A("ones"), [[32, 4], [1000, 2], [2, 16]], ALU.is_equal, 0.0, u - 1000 * g1, -1)
         for k in range(3):
             ms(A("RT%d" % k, RW, RW + 32), VOID)
-        ms(A("RS0"), BIG), ms(A("RSp"), 0.0), ms(A("X1"), 0.0), ms(A("E3"), 0.0)
+        ms(A("RS0"), BIG), ms(A("RSp"), 0.0), ms(A("E3"), 0.0)
         cp(E8("rep"), E8("i8"))
         iota(A("si"), LANE, 0, 0)
         sel(A("Perm"), A("ones"), [[1, 16], [16, 8]], ALU.is_equal, 0.0, 0, -1)
         act(A("RSm"), A("RS0"))
-        ms(A("RS0", 0, 128, 16), 0.0), ms(A("RSm", 0, 128, 16), -BIG), ms(A("RSp", 0, 128, 16), BIG)
+        ms(A("RS0", 0, 128, 16), 0.0), ms(A("RSm", 0, 128, 16), -BIG), ms(A("RSp", 0, 528, 66), BIG)
         act(A("I64k"), I1, scale=65536.0)
         act(A("PermF"), A("Perm"), scale=FLAG)
         act(A("PermN"), A("Perm"), scale=-1.0)
         act(A("Ineg"), I1, scale=-1.0)
-        ts(A("DM"), A("si"), F(1), ALU.is_le)
-        ts(A("MASK"), A("si"), F(1), ALU.is_ge, 2.0 ** 25, ALU.mult)
-        ms(A("DM", 0, 128, 16), 0.0), ms(A("MASK", 15, 128, 16), 2048.0 + LOW)
-        act(A("Bn8"), A("Blk"), scale=-FAR)
-        act(A("Bp8"), A("Blk"), scale=FAR)
-        tt(A("BI8n"), I1, A("Blk"), ALU.subtract)
-        act(A("BI8"), A("BI8n"), scale=-FAR)
-        act(A("BI8n"), A("BI8n"), scale=FAR)
-        ms(A("XS"), 0.0)
+        ts(A("DG"), A("si"), F(1), ALU.is_equal)
+        iota(A("MASK"), [[0, 2], [-16, 4], [1, 64]], 0, 0)
+        ts(A("MASK"), A("MASK"), F(1), ALU.is_ge, FAR, ALU.mult)
+        act(F(8), F(1), scale=1.0 / FAR)
+        for u in range(2):
+            ts(A("RSp", 264 * u + 65, 264 * u + 264, 66), A("i8", 0, 4), 16.0 / FAR, ALU.mult, F(8), ALU.add)
+        ms(A("DA", 65, 528, 66), 1.0)
         ts(E8("CV"), E8("i8"), 16.0, ALU.mult, F(4), ALU.add)
         ts(A("WR"), A("iN"), F(2), ALU.is_equal, F(5), ALU.mult)
         for t in range(RO):
             last = t == RO - 1
-            ts(A("XB", t, t + 1), F(1), float(rho(t)), ALU.is_equal, -2176.0 if last else 2176.0, ALU.mult)
-        ts(A("XB", RO - 1, RO), A("XB", RO - 1, RO), 256.0, ALU.add)
+            ts(A("XB", t, t + 1), F(1), float(rho(t)), ALU.is_equal, 256.5 - 2176 if last else (256.5 - 2176) / 32, ALU.mult)
+        ts(A("XB", RO - 1, RO), A("XB", RO - 1, RO), -0.5, ALU.add)
+        act(A("Im32"), I1, scale=-32.0)
         act(A("onesN"), A("ones"), scale=-1.0)
         ms(ROW("cst", 0, 1), 127.5), ms(ROW("cst", 1, 2), M256), ms(ROW("cst", 2, 3), -M256)
         for t in range(RO):
             ts(CH("Pt", t), A("uM"), t + 1.0, ALU.is_equal, 4096.0, ALU.mult)
             sel(CH("Tri", t), A("TriN"), LANE, ALU.not_equal, 0.0, -rho(t), 0)
-            sel(CH("Ir", t), I1, LANE, ALU.not_equal, 0.0, -rho(t), 0)
+            sel(CH("Ir", t), A("Im32"), LANE, ALU.not_equal, 0.0, -rho(t), 0)
         sel(A("PermT"), A("onesN"), [[1, 8], [8, 16]], ALU.is_equal, 0.0, 0, -1)
 
     def prices(k, n, bank, e):
-        b0, b1 = PIECES[n]
+        b0, b1 = 2 * n, 2 * n + 2
         for b in range(b0, b1):
             q = (32 * (b // 4), 32 * (b // 4) + 32)
-            mm(B(bank, BW * (b - b0), BW * (b - b0 + 1)), A("W32", 128 * (b % 4), 128 * (b % 4) + 128, 1, q), A("pT", BW * k, BW * k + BW, 1, q), True, True,
-               b % 4 == 0)
+            mm(B(bank, BW * (b - b0), BW * (b - b0 + 1)), A("W32", 128 * (b % 4), 128 * (b % 4) + 128, 1, q), A("pT", BW * k, BW * k + BW, 1, q), True, True)
         (act if e == "a" else cp)(A("PT", RW * k + BW * b0, RW * k + BW * b1), B(bank, 0, BW * (b1 - b0)))
 
     def codes(t, k):
         x = CH("x%d" % t, k)
-        act(CH("nH", k), x, AF.Relu, scale=-16384.0, bias=16384.0)
-        act(CH("aH", k), x, scale=-1.0 / 32, bias=513.0 / 64)
-        mm(B("M1"), CH("Pt", t), CH("aH", k), True)
+        act(CH("nH", k), x, AF.Relu, scale=2.0 ** 20, bias=-2.0 ** 23)
+        mm(B("M1"), CH("Pt", t), x, True)
         mm(B("M1"), CH("Pt", t), CH("nH", k))
         mm(B("M1"), A("I4096"), CH("nH", k), False, True)
-        tt(CH("t1", k), CH("aH", k), B("M1"), ALU.mult)
-        ts(CH("t2", k), CH("t1", k), A("A16", t, t + 1), ALU.add)
+        tt(CH("t1", k), x, B("M1"), ALU.mult)
+        act(CH("t2", k), CH("t1", k), bias=A("A16", t, t + 1))
         ts(CH("t3", k), CH("t2", k), 4, ALU.arith_shift_right, 0x7FFF0FFF, ALU.bitwise_and)
         ts(CH("cu", k), CH("t3", k), 4096.0, ALU.min, float(LOW), ALU.add)
         mm(B("M1", 128, 256), CH("nH", k), CH("Tri", t), True, True)
@@ -392,10 +386,10 @@ def rank_program(g, core, T, topo):
     def best(k):
         scan(CH("KS", k), A("RS0"), B("G"), 0.0, ALU.min, ALU.max)
         ts(A("ka"), LAST("KS", k), 4095, ALU.bitwise_and)
-        ts(E8("wl"), A("ka"), -1.0, ALU.mult, float(NOWT), ALU.add)
+        act(E8("wl"), A("ka"), scale=-1.0, bias=float(NOWT))
         act(A("pk"), IND(A("RT%d" % k), E8("wl")), AF.Copy, xr=[E8("wl")])
         tt(A("OH"), IND(A("ka"), E8("rep")), A("KT"), ALU.is_equal, xr=[E8("rep")])
-        mm(B("M2"), A("OH"), A("Perm"), True, True)
+        mm(B("M2"), A("OH"), I1, True, True)
         act(CH("nB", k), B("M2"), scale=-1.0, bias=1.0, acc=A("acc", k, k + 1))
 
     def claims(k):
@@ -406,25 +400,26 @@ def rank_program(g, core, T, topo):
         mm(B("K"), A("pk"), A("I64k"), False, True)
         scan(A("MS"), A("RSm"), B("K"), -BIG, ALU.min, ALU.max)
         ts(E8("xp"), LAST("MS"), 4095 - 2 ** 31, ALU.bitwise_and)
-        ts(A("X1", 0, 128, 16), E8("xp"), -2048.0, ALU.add, -2048.0 - LOW, ALU.max)
-        scan(B("XS"), A("DM"), A("X1"), 0.0, ALU.mult, ALU.add)
-        mm(B("D"), I1, A("MASK"), True)
-        mm(B("D"), A("BI8"), B("XS"))
-        mm(B("D"), A("Bn8"), B("XS", 1, 129))
-        mm(LAST("D"), A("BI8n"), LAST("XS"))
-        mm(LAST("D"), A("Bp8"), A("XS", 16, 144, 16))
-        mm(LAST("D"), I1, A("X1", 0, 128, 16), False, True)
-        act(A("DA"), B("D"), AF.Abs)
+        ts(A("X1"), E8("xp"), -2048.0, ALU.add, -2048.0 - LOW, ALU.max)
+        tt(A("XD"), IND(A("X1"), E8("rep")), A("DG"), ALU.mult, xr=[E8("rep")])
+        mm(B("D", 0, 512), I1, A("MASK"), True)
+        for c in range(8):
+            mm(B("D", 64 * c, 64 * c + 64), A("Blk"), A("XD", 64 * (c // 4), 64 * (c // 4) + 64), False, c == 7)
+        act(A("DA", 64, 528, 66), A("X1"), scale=1.0 / FAR, bias=(2048.0 + LOW) / FAR)
         ts(E8("y1"), LAST("MS"), 12, ALU.arith_shift_right, 15, ALU.bitwise_and)
         tt(E8("y2"), E8("CV"), E8("y1"), ALU.subtract)
-        cp(E8("lv"), E8("y2"))
+        act(E8("lv"), E8("y2"))
         act(CH("Vr", k), IND(A("got%d" % k), E8("lv")), AF.Copy, xr=[E8("lv")])
-        scan(A("LS"), A("RSp"), A("DA"), 0.0, ALU.max, ALU.min)
-        ts(A("oL", 16 * k, 16 * k + 16, 2), LAST("LS"), F(1), ALU.max)
+        for u in (1, 0):
+            for c in range(4 * u, 4 * u + 4):
+                act(A("DA", 66 * c, 66 * c + 64), B("D", 64 * c, 64 * c + 64), AF.Abs, scale=-1.0, bias=A("X1", c, c + 1))
+            h = lambda n, c0=0, step=1: A(n, 264 * u + c0, 264 * u + 264, step)
+            scan(h("LS"), h("RSp"), h("DA"), 0.0, ALU.max, ALU.min)
+            ts(A("oL", 8 * k + 4 * u, 8 * k + 4 * u + 4), h("LS", 65, 66), FAR, ALU.mult)
 
-    def scatter(k, c):
-        o = A("oL", 16 * k + 2 * c, 16 * k + 2 * c + 1)
-        tt(IND(A("U"), o), CH("Vr", k, 16 * c, 16 * c + 16), CH("nB", k, c, 128, 8), ALU.mult, xr=[o])
+    def scatter(k, u):
+        o = A("oL", 8 * k + 4 * u, 8 * k + 4 * u + 4)
+        tt(IND(A("U"), o), CH("Vr", k, 64 * u, 64 * u + 64), CH("nB", k, 64 * u, 64 * u + 64), ALU.mult, xr=[o])
 
     def places(t, k):
         tt(E8("r1"), LAST("KS", k), E8("THn"), ALU.subtract)
@@ -440,17 +435,18 @@ def rank_program(g, core, T, topo):
             mm(X(), A("E3", s, s + 128), A("Ineg"), True)
             for c in range(8):
                 mm(X(16 * c, 16 * c + 16), CH("Ir", t), CH("x%d" % t, k, c, 128, 8))
-                mm(X(16 * c, 16 * c + 16), A("WR", s, s + 128), CH("nB", k, c, 128, 8))
+            mm(X(), A("WR", s, s + 128), CH("nB", k))
             mm(X(), A("E2"), A("PermT"), False, True)
             act(CH("yo", k), X(), scale=-1.0, bias=A("XB", t, t + 1))
             dma("y", None, CH("yo", k), "o%d" % k, oap=T.yt[:, 128 * k:128 * k + 128])
             return
         mm(X(), CH("Ir", t), CH("x%d" % t, k), True)
-        mm(X(), A("WR", s, s + 128), CH("nB", k))
+        for c in range(8):
+            mm(B("M2", 128 + c, 256, 8), A("WR", s, s + 128), CH("nB", k, 16 * c, 16 * c + 16))
         mm(X(), A("E3", s, s + 128), A("PermN"))
         mm(X(), A("E2"), A("Ineg"), False, True)
         xo = CH("xo", 3 * t + k)
-        act(xo, X(), bias=A("XB", t, t + 1))
+        act(xo, X(), scale=-1.0 / 32, bias=A("XB", t, t + 1))
         to, src = T.cores[(rank + 1) % len(T.cores)], T.cores[(rank - 1) % len(T.cores)]
         rid, pid = topo.addr(to, core)
         eng = topo.engines(core, to)[:8]
@@ -479,15 +475,15 @@ def rank_program(g, core, T, topo):
         act(E8("THn"), E8("THs"), bias=A("mneg", 0, 1))
 
     constants()
-    for n in range(6):
-        prices(ORDER[0], n, "T%d" % (n % 2), "av"[n % 2])
+    for n in range(8):
+        prices(ORDER[0], n, ("T0", "T1", "K", "D")[n % 4], "aaav"[n % 4])
+    for k in ORDER[1:]:
+        for n in range(8):
+            prices(k, n, "KD"[n % 2], "av"[n % 2])
     for t in range(RO):
         for k in ORDER:
             if not (t and k == ORDER[0]):
                 codes(t, k)
-            if t == 0 and k != ORDER[0]:
-                for n in range(6):
-                    prices(k, n, "K", "v")
             gains(t, k)
             votes(k)
             best(k)
@@ -497,8 +493,8 @@ def rank_program(g, core, T, topo):
             codes(t + 1, ORDER[0])
             useless()
         for k in ORDER:
-            for c in range(7, -1, -1):
-                scatter(k, c)
+            for u in (1, 0):
+                scatter(k, u)
 
     for h in range(2):
         for j in range(16):

@@ -14,9 +14,11 @@ BIG = 2.0 ** 30
 FAR = 8192.0
 FLAG = 2.0 ** 24 + 2.0 ** 18
 CYCLE, HOP, FLIGHT, SLACK = 0.83, 200.0, 2500.0, 40.0
+ROUNDS = 4
 ORDER = (2, 1, 0)
 PIECES = ((0, 3), (3, 6), (6, 9), (9, 12), (12, 14), (14, 16))
-GATHERS = ((0, 6), (6, 12), (12, 16))
+_G = (("a", 0, 3), ("a", 3, 6), ("a", 6, 9), ("a", 9, 12), ("a", 12, 16))
+GATHERS = (_G, _G, (("v", 0, 3), ("a", 3, 6), ("v", 6, 9), ("a", 9, 12), ("v", 12, 14), ("a", 14, 16)))
 
 SCRATCH = {}
 PLAN = []
@@ -34,7 +36,7 @@ _sb("tsti", [24, 16], "int32"), _sb("prb", [24, 16], "bfloat16")
 _sb("prp FQ Vr nB", C, "bfloat16"), _sb("x0 x1 x2 x3 x4", C, "float16"), _sb("xo", 4 * C, "float16"), _sb("Im32", 128, "bfloat16")
 _sb("got0 got1 got2", 2048, "bfloat16"), _sb("RT0 RT1 RT2", RW + 32, "bfloat16"), _sb("PT", 3 * RW, "bfloat16")
 _sb("pT", 3 * BW, "bfloat16")
-_sb("nH cf", C, "float16"), _sb("TT", [12, 32], "float16"), _sb("XD", 128, "float16"), _sb("X1", 8, "float32")
+_sb("nH cf", C, "float16"), _sb("TT", [4, 96], "float16"), _sb("XD", 128, "float16"), _sb("X1", 8, "float32")
 _sb("DA LS", 528, "float32"), _sb("RSp", 528, "bfloat16"), _sb("MASK", 512, "bfloat16")
 _sb("t1 yo", C, "float32"), _sb("t2 t3 KS", C, "int32"), _sb("cu", C, "uint16")
 _sb("MS VS uA mB si", 128, "int32"), _sb("KT uM uD", 128, "float32")
@@ -44,7 +46,7 @@ _sb("pf CV THs THn A16 XB acc mneg", 16, "float32"), _sb("acch cst D8 BO", 16, "
 _sb("pk OH E2 ones onesN Blk Blk8 I4096 I16 I64k Ineg Rneg TriN Perm PermN PermF PermT LK RK TL DG RS0 RSm", 128, "bfloat16")
 _sb("R136", BW, "bfloat16"), _sb("SEL WR E3", 144, "bfloat16"), _sb("iN", 144, "int32")
 _sb("Pt Tri Ir", RO * 128, "bfloat16"), _sb("J RV W32 w32", 512, "bfloat16")
-_sb("yco", 256, "float32")
+_sb("yco", 256, "float32"), _sb("RY", 2048, "bfloat16"), _sb("ys", 2048, "float16")
 for _n in "T0 T1 G V K D M1 M2".split():
     SCRATCH[_n] = ("psum", [128, 512], "float32")
 
@@ -152,26 +154,35 @@ def rank_program(g, core, T, topo):
                 ps = SCRATCH[x[1]][0] == "psum"
                 last[x[1]] = [h for h in last.get(x[1], []) if not (ps or (wr and x[4] == 1 and h[0] >= x[2] and h[1] <= x[3]))] + [x[2:5] + (n, wr)]
             pre.append(d)
-        gap = lambda m, n: pre[n][m]
-        way, post = [op[6] for op in ops], [[] for _ in ops]
+        way, post = [op[6] for op in ops], [{} for _ in ops]
         for n in range(len(ops) - 1, -1, -1):
-            for m in pre[n]:
-                post[m].append(n)
-                way[m] = max(way[m], ops[m][6] + gap(m, n) + way[n])
-        left, ready, free, out = [len(d) for d in pre], [0.0] * len(ops), {e: 0.0 for e in Q}, []
-        can = {e: [n for n, op in enumerate(ops) if op[0] == e and not pre[n]] for e in Q}
-        while len(out) < len(ops):
-            t0, e = min((max(free[e], min(ready[n] for n in can[e])), e) for e in Q if can[e])
-            n = max((n for n in can[e] if ready[n] <= t0 + SLACK), key=lambda n: (way[n], -n))
-            can[e].remove(n)
-            out.append(n)
-            free[e] = max(free[e], ready[n]) + ops[n][6]
-            for m in post[n]:
-                ready[m] = max(ready[m], free[e] + gap(n, m))
-                left[m] -= 1
-                if not left[m]:
-                    can[ops[m][0]].append(m)
-        return out
+            for m, gap in pre[n].items():
+                post[m][n] = gap
+                way[m] = max(way[m], ops[m][6] + gap + way[n])
+
+        def lay(before, after, first):
+            left, ready, free, out, end = [len(d) for d in before], [0.0] * len(ops), {e: 0.0 for e in Q}, [], [0.0] * len(ops)
+            can = {e: [n for n, op in enumerate(ops) if op[0] == e and not before[n]] for e in Q}
+            while len(out) < len(ops):
+                t0, e = min((max(free[e], min(ready[n] for n in can[e])), e) for e in Q if can[e])
+                n = max((n for n in can[e] if ready[n] <= t0 + SLACK), key=lambda n: (first[n], -n))
+                can[e].remove(n)
+                out.append(n)
+                end[n] = free[e] = max(free[e], ready[n]) + ops[n][6]
+                for m, gap in after[n].items():
+                    ready[m] = max(ready[m], free[e] + gap)
+                    left[m] -= 1
+                    if not left[m]:
+                        can[ops[m][0]].append(m)
+            return out, end
+        best = None
+        for early in (0, 5, 20):
+            again = lay(pre, post, [way[n] - early * n for n in range(len(ops))])
+            for _ in range(ROUNDS):
+                again = lay(pre, post, lay(post, pre, again[1])[1])
+                if best is None or max(again[1]) < max(best[1]):
+                    best = again
+        return best[0]
 
     def mm(out, l, r, start=False, stop=False):
         run("p", lambda q: q.matmul(out[0], l[0], r[0], start, stop), [l, r], [out], max(min(64, l[5]), r[5]) * CYCLE / 2)
@@ -189,8 +200,8 @@ def rank_program(g, core, T, topo):
         else:
             run("v", lambda q: q.tensor_scalar(out[0], a[0], v1, v2, op0, op1), [a] + xr, [out], cost(out, [a]))
 
-    def cp(out, a):
-        run("v", lambda q: q.tensor_copy(out[0], a[0]), [a], [out], cost(out, [a]))
+    def cp(out, a, xr=()):
+        run("v", lambda q: q.tensor_copy(out[0], a[0]), [a] + list(xr), [out], cost(out, [a]))
 
     def turn(out, a):
         run("v", lambda q: q.transpose(out[0], a[0]), [a], [out], cost(out, [a]))
@@ -335,7 +346,7 @@ def rank_program(g, core, T, topo):
             ts(CH("Pt", t), A("uM"), t + 1.0, ALU.is_equal, 4096.0, ALU.mult)
             sel(CH("Tri", t), A("TriN"), LANE, ALU.not_equal, 0.0, -rho(t), 0)
             sel(CH("Ir", t), A("Im32"), LANE, ALU.not_equal, 0.0, -rho(t), 0)
-        sel(A("PermT"), A("onesN"), [[1, 8], [8, 16]], ALU.is_equal, 0.0, 0, -1)
+        sel(A("PermT"), A("ones"), [[1, 8], [8, 16]], ALU.is_equal, 0.0, 0, -1)
 
     def prices(k, n, bank, e):
         b0, b1 = 2 * n, 2 * n + 2
@@ -357,14 +368,16 @@ def rank_program(g, core, T, topo):
         mm(B("M1", 128, 256), CH("nH", k), CH("Tri", t), True, True)
         act(CH("FQ", k), B("M1", 128, 256), AF.Relu, scale=1.0 / 16384)
         ts(CH("cf", k), CH("cu", k), -2048.0 - LOW, ALU.add, 2047.0, ALU.min)
-        for c in range(4):
-            turn(A3("TT", 4 * k + c, S(0, 32)), CH("cf", k, c, 128, 4))
+        if k != ORDER[0]:
+            n = 2 if k == ORDER[1] else 1
+            for c in range(4):
+                turn(A3("TT", c, S(32 * k, 32 * (k + n))), CH("cf", k, c, 128 * n, 4))
 
     def gains(t, k):
         got, RT = "got%d" % k, "RT%d" % k
-        for b0, b1 in GATHERS:
+        for e, b0, b1 in GATHERS[k]:
             off = CH("cu", k, 8 * b0, 8 * b1)
-            act(A(got, 128 * b0, 128 * b1), IND(A("U"), off), AF.Copy, xr=[off])
+            (act if e == "a" else cp)(A(got, 128 * b0, 128 * b1), IND(A("U"), off), xr=[off])
         mm(B("G"), A3("prb", S(8 * k, 8 * k + 8), S(0, 16)), A("Rneg"), True)
         mm(B("G"), A("LK", 0, 128, 1, (0, 98)), A("RK", 0, 128, 1, (0, 98)))
         for n, (b0, b1) in enumerate(PIECES):
@@ -396,7 +409,7 @@ def rank_program(g, core, T, topo):
         mm(B("K"), ROW("ones"), ROW("RV", 384, 512), True)
         for u in range(2):
             for g1 in range(2):
-                mm(B("K", 64 * u, 64 * u + 64), CH("J", 2 * u + g1), A3("TT", S(4 * k, 4 * k + 4), S(16 * g1, 16 * g1 + 16)))
+                mm(B("K", 64 * u, 64 * u + 64), CH("J", 2 * u + g1), A3("TT", S(0, 4), S(32 * k + 16 * g1, 32 * k + 16 * g1 + 16)))
         mm(B("K"), A("pk"), A("I64k"), False, True)
         scan(A("MS"), A("RSm"), B("K"), -BIG, ALU.min, ALU.max)
         ts(E8("xp"), LAST("MS"), 4095 - 2 ** 31, ALU.bitwise_and)
@@ -415,7 +428,7 @@ def rank_program(g, core, T, topo):
                 act(A("DA", 66 * c, 66 * c + 64), B("D", 64 * c, 64 * c + 64), AF.Abs, scale=-1.0, bias=A("X1", c, c + 1))
             h = lambda n, c0=0, step=1: A(n, 264 * u + c0, 264 * u + 264, step)
             scan(h("LS"), h("RSp"), h("DA"), 0.0, ALU.max, ALU.min)
-            ts(A("oL", 8 * k + 4 * u, 8 * k + 4 * u + 4), h("LS", 65, 66), FAR, ALU.mult)
+            act(A("oL", 8 * k + 4 * u, 8 * k + 4 * u + 4), h("LS", 65, 66), scale=FAR)
 
     def scatter(k, u):
         o = A("oL", 8 * k + 4 * u, 8 * k + 4 * u + 4)
@@ -428,7 +441,7 @@ def rank_program(g, core, T, topo):
         mm(B("V"), A("PermF"), A("OH"), False, True)
         scan(A("VS"), A("RSm"), B("V"), -BIG, ALU.min, ALU.max)
         ts(E8("vx"), LAST("VS"), 255 + 3 * 2 ** 24, ALU.bitwise_and)
-        ts(E8("tkb"), E8("vx"), 256.0, ALU.min, -256.0, ALU.add)
+        act(E8("tkb"), E8("vx"), AF.Relu, scale=-1.0, bias=256.0)
         tt(A("E2"), IND(E8("tkb"), E8("rep")), CH("FQ", k), ALU.mult, xr=[E8("rep")])
         s, X = 15 - rho(t), lambda c0=0, c1=128: B("M2", 128 + c0, 128 + c1)
         if t == RO - 1:
@@ -444,7 +457,7 @@ def rank_program(g, core, T, topo):
         for c in range(8):
             mm(B("M2", 128 + c, 256, 8), A("WR", s, s + 128), CH("nB", k, 16 * c, 16 * c + 16))
         mm(X(), A("E3", s, s + 128), A("PermN"))
-        mm(X(), A("E2"), A("Ineg"), False, True)
+        mm(X(), A("E2"), I1, False, True)
         xo = CH("xo", 3 * t + k)
         act(xo, X(), scale=-1.0 / 32, bias=A("XB", t, t + 1))
         to, src = T.cores[(rank + 1) % len(T.cores)], T.cores[(rank - 1) % len(T.cores)]
@@ -458,7 +471,7 @@ def rank_program(g, core, T, topo):
             sem[a], cnt[a] = T.sem[a], len(topo.engines(src, core)[:8])
             snap[(a, cnt[a])] = {}
             hist.setdefault(dst[1], []).append(dst[2:5] + (a, cnt[a], True))
-        ops.append(("g", write, [xo], [dst], "st", 0, 600.0, FLIGHT + 500))
+        ops.append(("g", write, [xo], [dst], "st", 0, 600.0, FLIGHT + 2000))
 
     def useless():
         m = B("M1", 256, 257)
@@ -482,8 +495,9 @@ def rank_program(g, core, T, topo):
             prices(k, n, "KD"[n % 2], "av"[n % 2])
     for t in range(RO):
         for k in ORDER:
-            if not (t and k == ORDER[0]):
-                codes(t, k)
+            if k != ORDER[1]:
+                for j in (ORDER[t > 0:2] if k == ORDER[0] else [k]):
+                    codes(t, j)
             gains(t, k)
             votes(k)
             best(k)
@@ -496,11 +510,14 @@ def rank_program(g, core, T, topo):
             for u in (1, 0):
                 scatter(k, u)
 
+    for j in range(16):
+        mm(B("T0"), I1, A("U", LOW + j, LOW + 2048, 16), j == 0, j == 15)
+    act(CH("yco", 0), B("T0"))
+    iota(A("RY"), [[0, 256], [4096, 8]], 0, 0)
+    scan(A("ys"), A("RY"), A("U", LOW + 2048, LOW + W), 0.0, ALU.min, ALU.add)
+    tt(CH("yco", 1), A("ys", 7, 2048, 16), A("ys", 15, 2048, 16), ALU.add)
     for h in range(2):
-        for j in range(16):
-            mm(B("T%d" % h), I1, A("U", LOW + 2048 * h + j, LOW + 2048 * h + 2048, 16), j == 0, j == 15)
-        act(CH("yco", h), B("T%d" % h))
-        dma("a" if h else "y", None, CH("yco", h), "o%d" % (3 + h), oap=T.yc[:, 128 * h:128 * h + 128])
+        dma("ay"[h], None, CH("yco", h), "o%d" % (3 + h), oap=T.yc[:, 128 * h:128 * h + 128])
 
     if not PLAN:
         PLAN.extend(order())

@@ -3,8 +3,8 @@ from concourse.mybir import AluOpType as ALU, AxisListType as AX, ActivationFunc
 
 C, W, RO = 384, 4096, 5
 VOID = -2.0
-LOW = 64
-UW = LOW + W + 16
+LOW = 80
+UW = LOW + W
 BW = 136
 RW = 16 * BW
 NOWT = RW + 16
@@ -13,16 +13,19 @@ M256 = 256 * MAGIC
 BIG = 2.0 ** 30
 FAR = 8192.0
 FLAG = 2.0 ** 24 + 2.0 ** 18
-CYCLE, HOP, FLIGHT, SLACK = 0.83, 200.0, 2500.0, 40.0
-ROUNDS = 4
+CYCLE, HOP, FLIGHT, SLACK = 0.92, 200.0, 2500.0, 40.0
+ROUNDS, SHAKES = 3, 120
 ORDER = (2, 1, 0)
+FIRST, LATEST = ORDER[0], ORDER[2]
 PIECES = ((0, 3), (3, 6), (6, 9), (9, 12), (12, 14), (14, 16))
-_G = (("a", 0, 3), ("a", 3, 6), ("a", 6, 9), ("a", 9, 12), ("a", 12, 16))
-GATHERS = (_G, _G, (("v", 0, 3), ("a", 3, 6), ("v", 6, 9), ("a", 9, 12), ("v", 12, 14), ("a", 14, 16)))
+ENDS = PIECES[:4] + ((12, 15), (15, 16))
+GATHERS = {FIRST: (("v", 0, 3), ("a", 3, 6), ("v", 6, 9), ("a", 9, 12), ("a", 12, 16)),
+           ORDER[1]: (("a", 0, 3), ("a", 3, 6), ("a", 6, 9), ("a", 9, 12), ("a", 12, 16)),
+           LATEST: tuple(("a",) + p for p in ENDS)}
 
 SCRATCH = {}
 PLAN = []
-SEMAPHORES = (["sv", "sa", "sp", "sg", "ld0", "ld1", "ld2", "ld3", "ld4", "st", "o0", "o1", "o2", "o3", "o4"]
+SEMAPHORES = (["sv", "sa", "sp", "sg", "ld0", "ld1", "ld2", "ld3", "ld4", "dp0", "dp1", "pt0", "pt1", "st", "o0", "o1", "o2", "o3", "o4"]
               + ["arr%d_%d" % (t, k) for t in range(1, RO) for k in range(3)])
 
 
@@ -33,21 +36,20 @@ def _sb(names, cols, dtype):
 
 _sb("U", UW, "bfloat16")
 _sb("tsti", [24, 16], "int32"), _sb("prb", [24, 16], "bfloat16")
-_sb("prp FQ Vr nB", C, "bfloat16"), _sb("x0 x1 x2 x3 x4", C, "float16"), _sb("xo", 4 * C, "float16"), _sb("Im32", 128, "bfloat16")
-_sb("got0 got1 got2", 2048, "bfloat16"), _sb("RT0 RT1 RT2", RW + 32, "bfloat16"), _sb("PT", 3 * RW, "bfloat16")
-_sb("pT", 3 * BW, "bfloat16")
-_sb("nH cf", C, "float16"), _sb("TT", [4, 96], "float16"), _sb("XD", 128, "float16"), _sb("X1", 8, "float32")
-_sb("DA LS", 528, "float32"), _sb("RSp", 528, "bfloat16"), _sb("MASK", 512, "bfloat16")
+_sb("FQ Vr nB", C, "bfloat16"), _sb("x0 x1 x2 x3 x4 nH cf", C, "float16"), _sb("xo", 4 * C, "float16")
+_sb("got0 got1 got2 WB", 2048, "bfloat16"), _sb("RT0 RT1 RT2", RW + 32, "bfloat16"), _sb("PT", 3 * RW, "bfloat16")
+_sb("pT", 3 * BW, "bfloat16"), _sb("ys", 1536, "float16"), _sb("RY", 1536, "bfloat16")
+_sb("TT", [4, 96], "float16"), _sb("XD", 128, "float16"), _sb("X1 XF", 8, "float32")
+_sb("DA", 528, "float32"), _sb("RSp", 528, "bfloat16"), _sb("MASK J RV", 512, "bfloat16")
 _sb("t1 yo", C, "float32"), _sb("t2 t3 KS", C, "int32"), _sb("cu", C, "uint16")
-_sb("MS VS uA mB si", 128, "int32"), _sb("KT uM uD", 128, "float32")
-_sb("ka", 8, "int32"), _sb("tkb", 16, "bfloat16")
-_sb("xp y1 y2 r1 r2 vx i8 pc thi", 16, "int32"), _sb("wl lv rep", 16, "uint16"), _sb("oL", 48, "uint16")
-_sb("pf CV THs THn A16 XB acc mneg", 16, "float32"), _sb("acch cst D8 BO", 16, "bfloat16")
-_sb("pk OH E2 ones onesN Blk Blk8 I4096 I16 I64k Ineg Rneg TriN Perm PermN PermF PermT LK RK TL DG RS0 RSm", 128, "bfloat16")
+_sb("MS VS uA mB si", 128, "int32"), _sb("KT KB uM uD", 128, "float32")
+_sb("ka", 8, "int32"), _sb("xp y1 y2 r1 r2 vx pc thi", 16, "int32"), _sb("wl lv rep r15", 16, "uint16"), _sb("oL", 3 * 528, "uint16")
+_sb("pf CV THs THn A16 XB acc mneg o16", 16, "float32"), _sb("tkb acch cst D8 BO", 16, "bfloat16")
+_sb("pk OH E2 ones onesN Blk Blk8 I4k B4k BlkN I16 I64k Ineg Im32 Rneg TriN Perm PermN PermF PermT LK RK TL DG RS0 RSm", 128, "bfloat16")
 _sb("R136", BW, "bfloat16"), _sb("SEL WR E3", 144, "bfloat16"), _sb("iN", 144, "int32")
-_sb("Pt Tri Ir", RO * 128, "bfloat16"), _sb("J RV W32 w32", 512, "bfloat16")
-_sb("yco", 256, "float32"), _sb("RY", 2048, "bfloat16"), _sb("ys", 2048, "float16")
-for _n in "T0 T1 G V K D M1 M2".split():
+_sb("Pn Tri Ir", RO * 128, "bfloat16"), _sb("Pt", [8 * RO, 16], "bfloat16"), _sb("yco", 256, "float32")
+SCRATCH["Dp"] = ("dram", [2, 8, RW], "bfloat16")
+for _n in "T0 T1 G V K D T2 M2".split():
     SCRATCH[_n] = ("psum", [128, 512], "float32")
 
 
@@ -93,7 +95,7 @@ def rank_program(g, core, T, topo):
                 if h[3] != e:
                     if ps or (hit and (wr or h[5])):
                         ask(h[3], h[4])
-                elif hit and (wr or h[5]) and (e != "p" or x[0] is None):
+                elif hit and (wr or h[5]) and e != "p":
                     ask(h[3], h[4])
         for f in sorted(want, key=lambda k: -want[k]):
             if clock[e].get(f, 0) < want[f]:
@@ -182,6 +184,10 @@ def rank_program(g, core, T, topo):
                 again = lay(pre, post, lay(post, pre, again[1])[1])
                 if best is None or max(again[1]) < max(best[1]):
                     best = again
+        for r in range(1, SHAKES):
+            again = lay(pre, post, lay(post, pre, [e + (n * 7919 + r * 104729) % (101, 201, 401)[r % 3] for n, e in enumerate(best[1])])[1])
+            if max(again[1]) < max(best[1]):
+                best = again
         return best[0]
 
     def mm(out, l, r, start=False, stop=False):
@@ -219,14 +225,21 @@ def rank_program(g, core, T, topo):
             kw["accum_out"] = acc[0]
         run("a", lambda q: q.activation(out[0], a[0], func, **kw), [a] + xr, [out] + ([acc] if acc else []), cost(out, [a], 1.0))
 
+    def pick(out, win, off, e="a"):
+        (act if e == "a" else cp)(out, IND(win, off), xr=[off])
+
+    SENT = (None, "pc", 300, 301, 1, 1)
     POOL = (None, "pc", 100, 101, 1, 1)
 
     def iota(out, pattern, base, cm, alone=False):
         kw = {} if SCRATCH[out[1]][2] == "int32" else {"allow_small_or_imprecise_dtypes": True}
-        run("g", lambda q: q.iota(out[0], pattern, base, cm, **kw), [POOL], [out] + [POOL] * alone, 130 + 2 * out[5] * CYCLE)
+        run("g", lambda q: q.iota(out[0], pattern, base, cm, **kw), [POOL, SENT], [out] + [POOL] * alone, 130 + 2 * out[5] * CYCLE)
 
     def sel(out, a, pattern, op, fill, base, cm):
-        run("g", lambda q: q.affine_select(out[0], a[0], pattern, op, fill, base, cm), [a, POOL], [out], 170 + 2 * out[5] * CYCLE)
+        run("g", lambda q: q.affine_select(out[0], a[0], pattern, op, fill, base, cm), [a, POOL, SENT], [out], 170 + 2 * out[5] * CYCLE)
+
+    def fill(out, c):
+        iota(out, [[0, out[5]]], int(c), 0)
 
     CH = lambda n, k, c0=0, c1=128, step=1: A(n, 128 * k + c0, 128 * k + c1, step)
     B = lambda n, c0=0, c1=128, step=1: A(n, c0, c1, step)
@@ -234,6 +247,8 @@ def rank_program(g, core, T, topo):
     E8 = lambda n: A(n, 0, 8)
     F = lambda k, p=(0, 128): A("pf", k, k + 1, 1, p)
     ROW = lambda n, c0=0, c1=128, p=0: A(n, c0, c1, 1, (p, p + 1))
+    PR = lambda k: A3("prb", S(8 * k, 8 * k + 8), S(0, 16))
+    PT3 = lambda t: A3("Pt", S(8 * t, 8 * t + 8), S(0, 16))
     I1 = A("R136", 8, BW)
     LANE = [[0, 8], [1, 16]]
     rho = lambda t: (5 * t) % 16
@@ -246,35 +261,36 @@ def rank_program(g, core, T, topo):
 
     def constants():
         iota(A("pc", 0, 1), [[0, 1]], 0, 1)
-        iota(A("uA"), [[-1, 128]], 256, 1)
-        iota(A("mB"), [[1, 8], [0, 16]], 0, 0)
-        iota(A("i8"), [[1, 16]], 0, 0)
-        iota(A("w32"), [[1, 32], [0, 16]], 0, -1)
         iota(A("iN"), [[1, 144]], 0, 0)
         P = lambda k: A("pc", k, k + 1)
         ms(A("ones"), 1.0)
         ts(P(1), P(0), 4, ALU.arith_shift_right)
         ts(P(2), P(0), 15, ALU.bitwise_and)
-        ts(P(3), P(0), 5, ALU.arith_shift_right)
         cp(A("pf", 0, 2), A("pc", 1, 3))
+        ts(F(9), P(0), 256.0, ALU.add)
+        ts(A("uA"), B("iN"), -1.0, ALU.mult, F(9), ALU.add)
+        ts(A("mB"), B("iN"), 4, ALU.arith_shift_right)
+        ts(A("si"), B("iN"), 15, ALU.bitwise_and)
         ts(A("uA"), A("uA"), 15, ALU.bitwise_and)
         ts(A("uD"), A("mB"), F(0), ALU.subtract, -16.0, ALU.mult)
         act(F(6), F(1), scale=16.0 * 613)
         tt(A("uM"), A("uA"), A("uD"), ALU.add)
-        ts(F(7), P(3), -32.0, ALU.mult)
         ts(I1, A("uM"), 0.0, ALU.is_equal)
-        ts(A("A16", 0, RO), A("i8", 0, RO), 16.0 * 77, ALU.mult, F(6), ALU.add)
-        act(A("I4096"), I1, scale=4096.0)
+        ts(A("A16", 0, RO), A("iN", 0, RO), 16.0 * 77, ALU.mult, F(6), ALU.add)
+        act(A("I4k"), I1, scale=4096.0)
         sel(A("R136", 0, 8), A("ones", 0, 8), [[-16, 8]], ALU.is_equal, 0.0, 0, 1)
-        ts(A("W32"), A("w32"), F(7), ALU.is_equal)
+        ts(A("Blk"), A("mB"), F(0), ALU.is_equal)
+        act(A("B4k"), A("Blk"), scale=-4096.0)
+        act(A("BlkN"), A("Blk"), scale=-1.0)
+        ts(A("o16"), A("iN", 0, 16), F(1), ALU.is_equal)
+        for b in range(16):
+            ts(CH("WB", b), A("Blk"), A("o16", b, b + 1), ALU.mult)
         ms(A("pT"), VOID)
-        ms(A("U", 0, LOW), 0.0), ms(A("U", LOW + W, UW), VOID)
-        for c in range(8):
-            act(A("prp", c, C, 8), A3("prb", S(c, 24, 8), S(0, 16)))
+        fill(A("U", 0, LOW), VOID)
         for c in range(8):
             ts(A("x0", c, C, 8), A3("tsti", S(c, 24, 8), S(0, 16)), 1.0 / 32, ALU.mult, 1.0 / 64, ALU.add)
         for k in ORDER:
-            mm(B("V", 128 * k, 128 * k + 128), CH("prp", k), I1, True, True)
+            mm(B("V", 128 * k, 128 * k + 128), PR(k), I1, True, True)
             act(A("pT", BW * k + 8, BW * k + BW), B("V", 128 * k, 128 * k + 128))
         act(F(2), F(0), scale=16.0, bias=15.0)
         act(F(3), F(1), scale=-136.0, bias=2048.0)
@@ -285,8 +301,7 @@ def rank_program(g, core, T, topo):
         iota(A("RK"), [[-16, 8], [-1, 16]], 136, 0)
         iota(A("RK", 0, 128, 16), [[-1, 8]], 144, 0)
         ts(A("SEL"), A("iN"), F(2), ALU.is_equal, 4096.0, ALU.mult)
-        ts(E8("BO"), E8("i8"), F(0), ALU.is_equal, 4096.0, ALU.mult)
-        ts(A("Blk"), A("mB"), F(0), ALU.is_equal)
+        ts(E8("BO"), E8("iN"), F(0), ALU.is_equal, 4096.0, ALU.mult)
         ts(A("KT"), A("RK"), F(3), ALU.add)
         ms(A("LK"), 0.0), ms(A("RV", 0, 128), 0.0), ms(A("TL"), 0.0)
         iota(ROW("LK", p=32), [[0, 8], [-136, 16]], 2048, 0, True)
@@ -309,16 +324,16 @@ def rank_program(g, core, T, topo):
         ms(ROW("RV"), -MAGIC), ms(ROW("RV", 128, 256), -0.46875), ms(ROW("RV", 256, 384), MAGIC)
         iota(ROW("RV", p=64), [[0, 8], [-256, 16]], 3968, 0, True)
         iota(ROW("RV", 384, 512), [[0, 8], [-4096, 16]], 63488, 0)
-        sel(A("TriN"), A("Blk"), [[1, 128]], ALU.is_gt, 0.0, 0, -1)
-        tt(A("TriN"), I1, A("TriN"), ALU.subtract)
+        sel(A("TriN"), A("BlkN"), [[1, 128]], ALU.is_gt, 0.0, 0, -1)
+        sel(A("TriN"), A("TriN"), [[-1, 128]], ALU.not_equal, 1.0, 0, 1)
         for u in range(2):
             for g1 in range(2):
                 sel(CH("J", 2 * u + g1), A("ones"), [[32, 4], [1000, 2], [2, 16]], ALU.is_equal, 0.0, u - 1000 * g1, -1)
         for k in range(3):
-            ms(A("RT%d" % k, RW, RW + 32), VOID)
-        ms(A("RS0"), BIG), ms(A("RSp"), 0.0), ms(A("E3"), 0.0)
-        cp(E8("rep"), E8("i8"))
-        iota(A("si"), LANE, 0, 0)
+            fill(A("RT%d" % k, RW, RW + 32), VOID)
+        ms(A("RS0"), BIG), fill(A("RSp"), 0.0), fill(A("E3"), 0.0)
+        cp(E8("rep"), E8("iN"))
+        ts(E8("r15"), E8("iN"), 16.0, ALU.mult, 15.0, ALU.add)
         sel(A("Perm"), A("ones"), [[1, 16], [16, 8]], ALU.is_equal, 0.0, 0, -1)
         act(A("RSm"), A("RS0"))
         ms(A("RS0", 0, 128, 16), 0.0), ms(A("RSm", 0, 128, 16), -BIG), ms(A("RSp", 0, 528, 66), BIG)
@@ -329,11 +344,11 @@ def rank_program(g, core, T, topo):
         ts(A("DG"), A("si"), F(1), ALU.is_equal)
         iota(A("MASK"), [[0, 2], [-16, 4], [1, 64]], 0, 0)
         ts(A("MASK"), A("MASK"), F(1), ALU.is_ge, FAR, ALU.mult)
-        act(F(8), F(1), scale=1.0 / FAR)
+        act(F(8), F(1), bias=16.0)
         for u in range(2):
-            ts(A("RSp", 264 * u + 65, 264 * u + 264, 66), A("i8", 0, 4), 16.0 / FAR, ALU.mult, F(8), ALU.add)
-        ms(A("DA", 65, 528, 66), 1.0)
-        ts(E8("CV"), E8("i8"), 16.0, ALU.mult, F(4), ALU.add)
+            ts(A("RSp", 264 * u + 65, 264 * u + 264, 66), A("iN", 0, 4), 16.0, ALU.mult, F(8), ALU.add)
+        fill(A("DA", 65, 528, 66), FAR)
+        ts(E8("CV"), E8("iN"), 16.0, ALU.mult, F(4), ALU.add)
         ts(A("WR"), A("iN"), F(2), ALU.is_equal, F(5), ALU.mult)
         for t in range(RO):
             last = t == RO - 1
@@ -342,46 +357,60 @@ def rank_program(g, core, T, topo):
         act(A("Im32"), I1, scale=-32.0)
         act(A("onesN"), A("ones"), scale=-1.0)
         ms(ROW("cst", 0, 1), 127.5), ms(ROW("cst", 1, 2), M256), ms(ROW("cst", 2, 3), -M256)
-        for t in range(RO):
-            ts(CH("Pt", t), A("uM"), t + 1.0, ALU.is_equal, 4096.0, ALU.mult)
-            sel(CH("Tri", t), A("TriN"), LANE, ALU.not_equal, 0.0, -rho(t), 0)
-            sel(CH("Ir", t), A("Im32"), LANE, ALU.not_equal, 0.0, -rho(t), 0)
         sel(A("PermT"), A("ones"), [[1, 8], [8, 16]], ALU.is_equal, 0.0, 0, -1)
 
+    def matrices(t):
+        if t == 0:
+            ts(PT3(t), A("uM"), t + 1.0, ALU.is_equal, -4096.0, ALU.mult)
+            tt(CH("Pn", t), A("I4k"), PT3(t), ALU.subtract)
+        else:
+            sel(PT3(t), A("B4k"), [[-1, 128]], ALU.is_equal, 0.0, -1 - t, 1)
+            wrap = A3("Pt", S(8 * t, 8 * t + 8), S(15 - t, 16))
+            sel(wrap, wrap, [[-16, 8], [-1, t + 1]], ALU.not_equal, -4096.0, 0, 1)
+            act(CH("Pn", t), PT3(t), scale=-1.0)
+            sel(CH("Pn", t), CH("Pn", t), [[-1, 128]], ALU.not_equal, 4096.0, 0, 1)
+        sel(CH("Tri", t), A("TriN"), LANE, ALU.not_equal, 0.0, -rho(t), 0)
+        sel(CH("Ir", t), A("Im32"), LANE, ALU.not_equal, 0.0, -rho(t), 0)
+
     def prices(k, n, bank, e):
-        b0, b1 = 2 * n, 2 * n + 2
+        b0, b1 = PIECES[n]
         for b in range(b0, b1):
-            q = (32 * (b // 4), 32 * (b // 4) + 32)
-            mm(B(bank, BW * (b - b0), BW * (b - b0 + 1)), A("W32", 128 * (b % 4), 128 * (b % 4) + 128, 1, q), A("pT", BW * k, BW * k + BW, 1, q), True, True)
+            mm(B(bank, BW * (b - b0), BW * (b - b0 + 1)), CH("WB", b), A("pT", BW * k, BW * k + BW), True, True)
         (act if e == "a" else cp)(A("PT", RW * k + BW * b0, RW * k + BW * b1), B(bank, 0, BW * (b1 - b0)))
+
+    def spread(k):
+        rows = (T.Dp[k], "Dp", k, k + 1, 1, BW)
+        dma("y", rows, A("pT", BW * k, BW * k + BW), "dp%d" % k)
+        for i in range(16):
+            dma("y", (T.PT[i:128:16, RW * k:RW * k + RW], "PT", RW * k + i, RW * k + RW, 16, 2500), rows, "pt%d" % k)
 
     def codes(t, k):
         x = CH("x%d" % t, k)
         act(CH("nH", k), x, AF.Relu, scale=2.0 ** 20, bias=-2.0 ** 23)
-        mm(B("M1"), CH("Pt", t), x, True)
-        mm(B("M1"), CH("Pt", t), CH("nH", k))
-        mm(B("M1"), A("I4096"), CH("nH", k), False, True)
-        tt(CH("t1", k), x, B("M1"), ALU.mult)
-        act(CH("t2", k), CH("t1", k), bias=A("A16", t, t + 1))
-        ts(CH("t3", k), CH("t2", k), 4, ALU.arith_shift_right, 0x7FFF0FFF, ALU.bitwise_and)
-        ts(CH("cu", k), CH("t3", k), 4096.0, ALU.min, float(LOW), ALU.add)
-        mm(B("M1", 128, 256), CH("nH", k), CH("Tri", t), True, True)
-        act(CH("FQ", k), B("M1", 128, 256), AF.Relu, scale=1.0 / 16384)
-        ts(CH("cf", k), CH("cu", k), -2048.0 - LOW, ALU.add, 2047.0, ALU.min)
-        if k != ORDER[0]:
-            n = 2 if k == ORDER[1] else 1
+        mm(B("V", 128, 256), PT3(t), x, True)
+        mm(B("V", 128, 256), CH("Pn", t), CH("nH", k), False, True)
+        tt(CH("t1", k), x, B("V", 128, 256), ALU.mult)
+        act(CH("t2", k), CH("t1", k), scale=-1.0, bias=A("A16", t, t + 1))
+        ts(CH("t3", k), CH("t2", k), 4, ALU.arith_shift_right, 4095 - 2 ** 31, ALU.bitwise_and)
+        if k == FIRST:
+            act(CH("cu", k), CH("t3", k), AF.Relu, bias=float(LOW))
+        else:
+            ts(CH("cu", k), CH("t3", k), float(LOW), ALU.add, 0.0, ALU.max)
+        mm(B("M2", 256, 384), CH("nH", k), CH("Tri", t), True, True)
+        act(CH("FQ", k), B("M2", 256, 384), AF.Relu, scale=1.0 / 16384)
+        ts(CH("cf", k), CH("cu", k), -2048.0 - LOW, ALU.add)
+        if k == LATEST:
             for c in range(4):
-                turn(A3("TT", c, S(32 * k, 32 * (k + n))), CH("cf", k, c, 128 * n, 4))
+                turn(A3("TT", c, S(0, 96)), A("cf", c, C, 4))
 
     def gains(t, k):
         got, RT = "got%d" % k, "RT%d" % k
         for e, b0, b1 in GATHERS[k]:
-            off = CH("cu", k, 8 * b0, 8 * b1)
-            (act if e == "a" else cp)(A(got, 128 * b0, 128 * b1), IND(A("U"), off), xr=[off])
-        mm(B("G"), A3("prb", S(8 * k, 8 * k + 8), S(0, 16)), A("Rneg"), True)
+            pick(A(got, 128 * b0, 128 * b1), A("U"), CH("cu", k, 8 * b0, 8 * b1), e)
+        mm(B("G"), PR(k), A("Rneg"), True)
         mm(B("G"), A("LK", 0, 128, 1, (0, 98)), A("RK", 0, 128, 1, (0, 98)))
-        for n, (b0, b1) in enumerate(PIECES):
-            bank = "T%d" % (n % 2)
+        for n, (b0, b1) in enumerate(ENDS if k == LATEST else PIECES):
+            bank = "T%d" % (n % 3)
             for b in range(b0, b1):
                 mm(B(bank, BW * (b - b0), BW * (b - b0 + 1)), A(got, 128 * b, 128 * b + 128), A("R136"), True, True)
             tt(A(RT, BW * b0, BW * b1), B(bank, 0, BW * (b1 - b0)), A("PT", RW * k + BW * b0, RW * k + BW * b1), ALU.max)
@@ -400,10 +429,16 @@ def rank_program(g, core, T, topo):
         scan(CH("KS", k), A("RS0"), B("G"), 0.0, ALU.min, ALU.max)
         ts(A("ka"), LAST("KS", k), 4095, ALU.bitwise_and)
         act(E8("wl"), A("ka"), scale=-1.0, bias=float(NOWT))
-        act(A("pk"), IND(A("RT%d" % k), E8("wl")), AF.Copy, xr=[E8("wl")])
-        tt(A("OH"), IND(A("ka"), E8("rep")), A("KT"), ALU.is_equal, xr=[E8("rep")])
+        pick(A("pk"), A("RT%d" % k), E8("wl"))
+        if k == LATEST:
+            pick(A("KB"), CH("KS", k), E8("r15"))
+            tt(A("OH"), A("KB"), B("G"), ALU.is_equal)
+        else:
+            tt(A("OH"), IND(A("ka"), E8("rep")), A("KT"), ALU.is_equal, xr=[E8("rep")])
         mm(B("M2"), A("OH"), I1, True, True)
         act(CH("nB", k), B("M2"), scale=-1.0, bias=1.0, acc=A("acc", k, k + 1))
+
+    OL = lambda k, u, c0=260, c1=264, step=1: A("oL", 528 * k + 264 * u + c0, 528 * k + 264 * u + c1, step)
 
     def claims(k):
         mm(B("K"), ROW("ones"), ROW("RV", 384, 512), True)
@@ -414,24 +449,29 @@ def rank_program(g, core, T, topo):
         scan(A("MS"), A("RSm"), B("K"), -BIG, ALU.min, ALU.max)
         ts(E8("xp"), LAST("MS"), 4095 - 2 ** 31, ALU.bitwise_and)
         ts(A("X1"), E8("xp"), -2048.0, ALU.add, -2048.0 - LOW, ALU.max)
-        tt(A("XD"), IND(A("X1"), E8("rep")), A("DG"), ALU.mult, xr=[E8("rep")])
-        mm(B("D", 0, 512), I1, A("MASK"), True)
-        for c in range(8):
-            mm(B("D", 64 * c, 64 * c + 64), A("Blk"), A("XD", 64 * (c // 4), 64 * (c // 4) + 64), False, c == 7)
-        act(A("DA", 64, 528, 66), A("X1"), scale=1.0 / FAR, bias=(2048.0 + LOW) / FAR)
-        ts(E8("y1"), LAST("MS"), 12, ALU.arith_shift_right, 15, ALU.bitwise_and)
-        tt(E8("y2"), E8("CV"), E8("y1"), ALU.subtract)
-        act(E8("lv"), E8("y2"))
-        act(CH("Vr", k), IND(A("got%d" % k), E8("lv")), AF.Copy, xr=[E8("lv")])
+        D = lambda c0, c1: B("T0" if k == LATEST and c0 < 256 else "D", c0, c1)
+        for u, m in (((1, 1), (0, 1)) if k == LATEST else ((0, 2),)):
+            r = A("rep", 4 * u, 4 * (u + m))
+            tt(A("XD", 64 * u, 64 * (u + m)), IND(A("X1"), r), A("DG", 0, 64 * m), ALU.mult, xr=[r])
+            mm(D(256 * u, 256 * (u + m)), I1, A("MASK", 0, 256 * m), True)
+            for c in range(4 * u, 4 * (u + m)):
+                mm(D(64 * c, 64 * c + 64), A("Blk"), A("XD", 64 * (c // 4), 64 * (c // 4) + 64), False, c == 4 * (u + m) - 1)
+        act(A("DA", 64, 528, 66), A("X1"), bias=2048.0 + LOW)
+        act(A("XF"), A("X1"), scale=FAR)
+        if k != FIRST:
+            ts(E8("y1"), LAST("MS"), 12, ALU.arith_shift_right, 15, ALU.bitwise_and)
+            tt(E8("y2"), E8("CV"), E8("y1"), ALU.subtract)
+            act(E8("lv"), E8("y2"))
+            pick(CH("Vr", k), A("got%d" % k), E8("lv"))
         for u in (1, 0):
             for c in range(4 * u, 4 * u + 4):
-                act(A("DA", 66 * c, 66 * c + 64), B("D", 64 * c, 64 * c + 64), AF.Abs, scale=-1.0, bias=A("X1", c, c + 1))
-            h = lambda n, c0=0, step=1: A(n, 264 * u + c0, 264 * u + 264, step)
-            scan(h("LS"), h("RSp"), h("DA"), 0.0, ALU.max, ALU.min)
-            act(A("oL", 8 * k + 4 * u, 8 * k + 4 * u + 4), h("LS", 65, 66), scale=FAR)
+                act(A("DA", 66 * c, 66 * c + 64), D(64 * c, 64 * c + 64), AF.Abs, scale=-FAR, bias=A("XF", c, c + 1))
+                scan(OL(k, u, c % 4, 264, 4), A("RSp", 66 * c, 66 * c + 66), A("DA", 66 * c, 66 * c + 66), 0.0, ALU.max, ALU.min)
+            if k == FIRST:
+                pick(CH("Vr", k, 64 * u, 64 * u + 64), A("U"), OL(k, u))
 
     def scatter(k, u):
-        o = A("oL", 8 * k + 4 * u, 8 * k + 4 * u + 4)
+        o = OL(k, u)
         tt(IND(A("U"), o), CH("Vr", k, 64 * u, 64 * u + 64), CH("nB", k, 64 * u, 64 * u + 64), ALU.mult, xr=[o])
 
     def places(t, k):
@@ -471,10 +511,10 @@ def rank_program(g, core, T, topo):
             sem[a], cnt[a] = T.sem[a], len(topo.engines(src, core)[:8])
             snap[(a, cnt[a])] = {}
             hist.setdefault(dst[1], []).append(dst[2:5] + (a, cnt[a], True))
-        ops.append(("g", write, [xo], [dst], "st", 0, 600.0, FLIGHT + 2000))
+        ops.append(("g", write, [xo], [dst] + [SENT] * (k == LATEST), "st", 0, 3100.0 if (t, k) == (0, FIRST) else 600.0, FLIGHT + 1400))
 
     def useless():
-        m = B("M1", 256, 257)
+        m = B("M2", 384, 385)
         act(A("acch", 0, 3), A("acc", 0, 3), bias=-64.0)
         mm(m, ROW("ones"), ROW("cst", 0, 1), True)
         for k in range(3):
@@ -488,36 +528,38 @@ def rank_program(g, core, T, topo):
         act(E8("THn"), E8("THs"), bias=A("mneg", 0, 1))
 
     constants()
-    for n in range(8):
-        prices(ORDER[0], n, ("T0", "T1", "K", "D")[n % 4], "aaav"[n % 4])
+    matrices(0)
+    for n in range(6):
+        prices(FIRST, n, ("T0", "T1", "K", "D")[n % 4], "aaav"[n % 4])
     for k in ORDER[1:]:
-        for n in range(8):
-            prices(k, n, "KD"[n % 2], "av"[n % 2])
+        spread(k)
     for t in range(RO):
+        if t < RO - 1:
+            matrices(t + 1)
+        else:
+            iota(A("RY"), [[0, 192], [4096, 8]], 0, 0)
+        for k in ORDER[t > 0:]:
+            codes(t, k)
         for k in ORDER:
-            if k != ORDER[1]:
-                for j in (ORDER[t > 0:2] if k == ORDER[0] else [k]):
-                    codes(t, j)
             gains(t, k)
             votes(k)
             best(k)
-            claims(k)
             places(t, k)
+            claims(k)
         if t < RO - 1:
-            codes(t + 1, ORDER[0])
+            codes(t + 1, FIRST)
             useless()
         for k in ORDER:
             for u in (1, 0):
                 scatter(k, u)
 
     for j in range(16):
-        mm(B("T0"), I1, A("U", LOW + j, LOW + 2048, 16), j == 0, j == 15)
-    act(CH("yco", 0), B("T0"))
-    iota(A("RY"), [[0, 256], [4096, 8]], 0, 0)
-    scan(A("ys"), A("RY"), A("U", LOW + 2048, LOW + W), 0.0, ALU.min, ALU.add)
-    tt(CH("yco", 1), A("ys", 7, 2048, 16), A("ys", 15, 2048, 16), ALU.add)
-    for h in range(2):
-        dma("ay"[h], None, CH("yco", h), "o%d" % (3 + h), oap=T.yc[:, 128 * h:128 * h + 128])
+        mm(B("T0", 0, 160), I1, A("U", LOW + j, LOW + 2560, 16), j == 0, j == 15)
+    act(A("yco", 0, 160), B("T0", 0, 160))
+    scan(A("ys"), A("RY"), A("U", LOW + 2560, LOW + W), 0.0, ALU.min, ALU.add)
+    tt(A("yco", 160, 256), A("ys", 7, 1536, 16), A("ys", 15, 1536, 16), ALU.add)
+    dma("a", None, A("yco", 0, 160), "o3", oap=T.yc[:, 0:160])
+    dma("y", None, A("yco", 160, 256), "o4", oap=T.yc[:, 160:256])
 
     if not PLAN:
         PLAN.extend(order())

@@ -7,26 +7,59 @@ LOW = 80
 UW = LOW + W
 BW = 136
 RW = 16 * BW
-NOWT = RW + 16
+TOP = 256.0
+SPAN = (0, 17, 51, 102, 170)
 MAGIC = 12582912.0
 M256 = 256 * MAGIC
 BIG = 2.0 ** 30
-FAR = 8192.0
+FAR = 4352.0
+HIDE = 2.0 ** 60
 FLAG = 2.0 ** 24 + 2.0 ** 18
-CYCLE, HOP, FLIGHT, SLACK = 0.92, 200.0, 2500.0, 40.0
-ROUNDS, SHAKES = 3, 120
+CYCLE, HOP, FLIGHT, SLACK = 0.92, 240.0, 2200.0, 20.0
+REMOTE, SPARE = 3400.0, 300.0
+MARGIN, WAKE, BLUR, SELF = 240.0, 240.0, 40.0, 240.0
+PACES = (((0.9, 0.9, 0.9, 1), 215.0, 200.0), ((0.9, 0.7, 0.6, 1), 250.0, -500.0), ((1.3, 1.65, 1.85, 1), 215.0, 0.0),
+         ((1.1, 0.95, 1.3, 1), 270.0, 500.0), ((1.2, 0.92, 0.8, 1), 200.0, 0.0))
+ROUNDS, SHAKES, REPEATS, NUDGES, STRETCH = 1, 3, 100, 700, 2000.0
 ORDER = (2, 1, 0)
 FIRST, LATEST = ORDER[0], ORDER[2]
-PIECES = ((0, 3), (3, 6), (6, 9), (9, 12), (12, 14), (14, 16))
-ENDS = PIECES[:4] + ((12, 15), (15, 16))
-GATHERS = {FIRST: (("v", 0, 3), ("a", 3, 6), ("v", 6, 9), ("a", 9, 12), ("a", 12, 16)),
-           ORDER[1]: (("a", 0, 3), ("a", 3, 6), ("a", 6, 9), ("a", 9, 12), ("a", 12, 16)),
-           LATEST: tuple(("a",) + p for p in ENDS)}
 
+
+def _runs(text):
+    ends = np.cumsum([int(n) for n in text[1::2]]).tolist()
+    return tuple(zip(text[::2], [0] + ends, ends))
+
+
+PIECES = {FIRST: ((0, 4), (4, 10), (10, 16)), ORDER[1]: ((0, 8), (8, 16)), LATEST: ((0, 6), (6, 12), (12, 16))}
+GATHERS = dict(zip(ORDER, map(_runs, ("v3a5v3a5", "v4a4a4a4", "a4a4a3a3a2"))))
+OPENING = dict(zip(ORDER, map(_runs, ("v4a4a3a3a2", "a4v4a4a4", "a4a4v4a4"))))
+EARLY = (0, 0, 0)
+BARE = ()
+MIDDLE = True
+SIZES = "aav"
+TAKE = "ppv"
+TAKES = "VHK"
+ROWS = "DDDH"
+GAINS = "GHG"
+ROUND = True
+VISIT = "c0 g2 v2 b2 p2 q2 g1 v1 b1 p1 q1 g0 v0 b0 p0 q0 n2 n1 u0"
+CODES = "KKK"
+COPIES = "avvva"
+SHORT = 1
+WHO = dict(a="aaa", v="vvv", cf="vva", c16="aaa", cst="avv", RV="vav", LK="aaa", RS="vaa",
+           nH="vvv", t2="aaa", cu="aaa", FQ="aaa", plain="vva", wl="aav", sc="aav", LX="vav", lv="avv", Gt="vaa",
+           tk="aav", tkb="aav", nB="aav", fl="aav", Vr="aaa", xo="avv")
+START = dict(nB="vvv", LX="ava", tkb="avv", cu="vaa", tk="vav", RV="aav", LK="vva", wl="aaa")
+FINISH = dict(xo="aaa")
+LOAD = 600
+AT = {FIRST: 0, ORDER[1]: RW, 3: 2 * RW, LATEST: 3 * RW}
+SUMS = 144
+
+GRAPH = []
 SCRATCH = {}
 PLAN = []
-SEMAPHORES = (["sv", "sa", "sp", "sg", "ld0", "ld1", "ld2", "ld3", "ld4", "dp0", "dp1", "pt0", "pt1", "st", "o0", "o1", "o2", "o3", "o4"]
-              + ["arr%d_%d" % (t, k) for t in range(1, RO) for k in range(3)])
+SEMAPHORES = (["sv", "sa", "sp", "sg", "ld0", "ld1", "ld2", "ld3", "ld4", "dp0", "dp1", "dp2", "dp3", "pt0", "pt1", "pt2", "st",
+               "o0", "o1", "o2", "o3", "o4"] + ["arr%d_%d" % (t, k) for t in range(1, RO) for k in range(3)])
 
 
 def _sb(names, cols, dtype):
@@ -36,21 +69,24 @@ def _sb(names, cols, dtype):
 
 _sb("U", UW, "bfloat16")
 _sb("tsti", [24, 16], "int32"), _sb("prb", [24, 16], "bfloat16")
-_sb("FQ Vr nB", C, "bfloat16"), _sb("x0 x1 x2 x3 x4 nH cf", C, "float16"), _sb("xo", 4 * C, "float16")
-_sb("got0 got1 got2 WB", 2048, "bfloat16"), _sb("RT0 RT1 RT2", RW + 32, "bfloat16"), _sb("PT", 3 * RW, "bfloat16")
-_sb("pT", 3 * BW, "bfloat16"), _sb("ys", 1536, "float16"), _sb("RY", 1536, "bfloat16")
-_sb("TT", [4, 96], "float16"), _sb("XD", 128, "float16"), _sb("X1 XF", 8, "float32")
-_sb("DA", 528, "float32"), _sb("RSp", 528, "bfloat16"), _sb("MASK J RV", 512, "bfloat16")
-_sb("t1 yo", C, "float32"), _sb("t2 t3 KS", C, "int32"), _sb("cu", C, "uint16")
-_sb("MS VS uA mB si", 128, "int32"), _sb("KT KB uM uD", 128, "float32")
-_sb("ka", 8, "int32"), _sb("xp y1 y2 r1 r2 vx pc thi", 16, "int32"), _sb("wl lv rep r15", 16, "uint16"), _sb("oL", 3 * 528, "uint16")
-_sb("pf CV THs THn A16 XB acc mneg o16", 16, "float32"), _sb("tkb acch cst D8 BO", 16, "bfloat16")
-_sb("pk OH E2 ones onesN Blk Blk8 I4k B4k BlkN I16 I64k Ineg Im32 Rneg TriN Perm PermN PermF PermT LK RK TL DG RS0 RSm", 128, "bfloat16")
-_sb("R136", BW, "bfloat16"), _sb("SEL WR E3", 144, "bfloat16"), _sb("iN", 144, "int32")
-_sb("Pn Tri Ir", RO * 128, "bfloat16"), _sb("Pt", [8 * RO, 16], "bfloat16"), _sb("yco", 256, "float32")
-SCRATCH["Dp"] = ("dram", [2, 8, RW], "bfloat16")
-for _n in "T0 T1 G V K D T2 M2".split():
-    SCRATCH[_n] = ("psum", [128, 512], "float32")
+_sb("Vr nB", C, "bfloat16"), _sb("x0 x1 x2 x3 x4 nH cf", C, "float16"), _sb("xo", 4 * C, "float16")
+_sb("got0 got1 got2 WB", 2048, "bfloat16"), _sb("RT0 RT1 RT2", 16 + RW, "bfloat16"), _sb("PT", 4 * RW, "bfloat16")
+_sb("pT", 4 * BW, "bfloat16"), _sb("ys", 2048, "float16"), _sb("RY", 2048, "bfloat16")
+_sb("TT", [4, 96], "float16"), _sb("LX LY", 128, "float16"), _sb("DA", 3 * 544, "float32"), _sb("XI XS", 3 * 136, "float16")
+_sb("XH XJ Pp", 136, "bfloat16"), _sb("FQ", C, "bfloat16"), _sb("J RV", 512, "bfloat16"), _sb("tk", 48, "bfloat16"), _sb("RX", [2, SPAN[4]], "bfloat16")
+_sb("t1 yo", C, "float32"), _sb("t2 t3 MS", C, "int32"), _sb("KS", 3 * BW, "int32"), _sb("cu", C, "uint16")
+_sb("VS mB si", 128, "int32"), _sb("KT", 128, "float32")
+_sb("ka xp y1 r1 vx", 24, "int32"), _sb("pc thi", 16, "int32"), _sb("rep", 16, "uint16"), _sb("oL wl lv", 24, "uint16")
+_sb("pk sc OH", C, "bfloat16"), _sb("Gt c16", C, "float16")
+_sb("CV A16 XB rest o16", 16, "float32"), _sb("pf", 32, "float32"), _sb("pw", 48, "float32")
+_sb("acch cst BO R8", 16, "bfloat16")
+_sb("ones onesN Blk BlkF I1 I4k BlkN I16 I64k Ineg Im32 TriN Perm PermN PermF E2 Back LK TL RSm", 128, "bfloat16")
+_sb("Pm tkb R4k", 128, "bfloat16"), _sb("SEL WR E3", 144, "bfloat16"), _sb("Rneg KM Blk8", 256, "bfloat16"), _sb("RK", 384, "bfloat16"), _sb("RC", 2 * BW, "bfloat16")
+_sb("THs THn XF", 24, "float32")
+_sb("iN", 144, "int32"), _sb("Tri Ir", RO * 128, "bfloat16"), _sb("Pt Pn", [8 * RO, 16], "bfloat16"), _sb("B4k", 256, "bfloat16"), _sb("yco", 256, "float32")
+SCRATCH["Dp"] = ("dram", [8, 2, 4 * RW], "bfloat16")
+for _n in "T0 T1 G V H D K M2".split():
+    SCRATCH[_n] = ("psum", [128, 1024], "bfloat16") if _n[0] == "T" else ("psum", [128, 512], "float32")
 
 
 def rank_program(g, core, T, topo):
@@ -66,10 +102,10 @@ def rank_program(g, core, T, topo):
         ap = T[name][p[0]:p[1], c0:c1:step] if step != 1 else T[name][p[0]:p[1], c0:c1]
         return (ap, name, c0, c1, step, len(range(c0, c1, step)))
 
-    def A3(name, i, j):
+    def A3(name, i, j, p=128):
         n, w = SCRATCH[name][1][1:]
         ri, rj = [range(*x.indices(m)) if isinstance(x, slice) else range(x, x + 1) for x, m in ((i, n), (j, w))]
-        return (T[name][:, i, j], name, ri[0] * w, (ri[-1] + 1) * w, 1, len(ri) * len(rj))
+        return (T[name][0:p, i, j], name, ri[0] * w, (ri[-1] + 1) * w, 1, len(ri) * len(rj))
 
     S = slice
 
@@ -127,6 +163,8 @@ def rank_program(g, core, T, topo):
 
     ops = []
 
+    role, closes = {}, []
+
     def run(e, make, reads, writes, ns):
         ops.append((e, make, reads, writes, e, 1, ns, HOP))
 
@@ -151,7 +189,8 @@ def rank_program(g, core, T, topo):
                 ps = SCRATCH[x[1]][0] == "psum"
                 for h in last.get(x[1], []):
                     if ps or (meet(x[2:5], h[0:3]) and (wr or h[4])):
-                        d[h[3]] = max(d.get(h[3], 0.0), 0.0 if ps and ops[h[3]][0] == op[0] else ops[h[3]][7])
+                        own = ops[h[3]][4] == op[0]
+                        d[h[3]] = max(d.get(h[3], 0.0), (0.0 if ps else SELF) if own else ops[h[3]][7])
             for x, wr in [(x, False) for x in op[2]] + [(x, True) for x in op[3]]:
                 ps = SCRATCH[x[1]][0] == "psum"
                 last[x[1]] = [h for h in last.get(x[1], []) if not (ps or (wr and x[4] == 1 and h[0] >= x[2] and h[1] <= x[3]))] + [x[2:5] + (n, wr)]
@@ -165,40 +204,85 @@ def rank_program(g, core, T, topo):
         def lay(before, after, first):
             left, ready, free, out, end = [len(d) for d in before], [0.0] * len(ops), {e: 0.0 for e in Q}, [], [0.0] * len(ops)
             can = {e: [n for n, op in enumerate(ops) if op[0] == e and not before[n]] for e in Q}
+            start = lambda e, r: free[e] if r - HOP + MARGIN <= free[e] else r - HOP + WAKE
             while len(out) < len(ops):
-                t0, e = min((max(free[e], min(ready[n] for n in can[e])), e) for e in Q if can[e])
-                n = max((n for n in can[e] if ready[n] <= t0 + SLACK), key=lambda n: (first[n], -n))
+                t0, e = min((start(e, min(ready[n] for n in can[e])), e) for e in Q if can[e])
+                n = max((n for n in can[e] if start(e, ready[n]) <= t0 + SLACK), key=lambda n: (first[n], -n))
                 can[e].remove(n)
                 out.append(n)
-                end[n] = free[e] = max(free[e], ready[n]) + ops[n][6]
+                end[n] = free[e] = start(e, ready[n]) + ops[n][6]
                 for m, gap in after[n].items():
                     ready[m] = max(ready[m], free[e] + gap)
                     left[m] -= 1
                     if not left[m]:
                         can[ops[m][0]].append(m)
             return out, end
+        kind = [3 if op[4] != op[0] else 2 if len(op[3][0]) > 6 else 1 if op[2] and len(op[2][0]) > 6 else 0 for op in ops]
+        waits = [[[(m, hop + (gap - HOP + later - SPARE * (gap == REMOTE) if gap > HOP else 0.0)) for m, gap in d.items() if gap] for d in pre] for _, hop, later in PACES]
+
+        def takes(plan):
+            total = 0.0
+            for (pace, wake, _), wait in zip(PACES, waits):
+                end, free = [0.0] * len(ops), {e: 0.0 for e in Q}
+                for n in plan:
+                    e = ops[n][0]
+                    end[n] = free[e] = max([end[m] + gap for m, gap in wait[n]] + [free[e]]) + ops[n][6] * pace[kind[n]]
+                total += np.log(max(end))
+            return total
         best = None
+        GRAPH.append((ops, pre, post, way, lay))
         for early in (0, 5, 20):
             again = lay(pre, post, [way[n] - early * n for n in range(len(ops))])
             for _ in range(ROUNDS):
                 again = lay(pre, post, lay(post, pre, again[1])[1])
-                if best is None or max(again[1]) < max(best[1]):
+                again += (takes(again[0]),)
+                if best is None or again[2] < best[2]:
                     best = again
+        def repeat(end, r):
+            ref = [end[closes[0]]] + [end[n] for n in closes]
+            span, t = min((ref[t + 1] - ref[t], t) for t in range(1, RO - 1))
+            at = {role[n][1]: end[n] - ops[n][6] - ref[t] for n in role if role[n][0] == t}
+            if r:
+                t0, size = (r * 0.618034 % 1.0) * (span + STRETCH) - STRETCH, (100, 250, 600)[r % 3]
+                at = {x: y + ((j * 7919 + r * 104729) % size - size / 2) * (t0 <= y < t0 + STRETCH) for j, (x, y) in enumerate(at.items())}
+            first = []
+            for n, op in enumerate(ops):
+                v, x = role.get(n, (0 if n < closes[0] else RO, " "))
+                first.append(-max(v - 1, 0) * span - (at[x] if 0 < v < RO - (x[0][0] in "pm") else end[n] - op[6] - ref[v]))
+            again = lay(pre, post, first)
+            return again + (takes(again[0]),)
         for r in range(1, SHAKES):
             again = lay(pre, post, lay(post, pre, [e + (n * 7919 + r * 104729) % (101, 201, 401)[r % 3] for n, e in enumerate(best[1])])[1])
-            if max(again[1]) < max(best[1]):
+            for again in (again + (takes(again[0]),), repeat(again[1], 0)):
+                if again[2] < best[2]:
+                    best = again
+        for r in range(REPEATS):
+            again = repeat(best[1], r)
+            if again[2] < best[2]:
                 best = again
+        for r in range(1, NUDGES):
+            t0 = (r * 0.618034 % 1.0) * max(best[1])
+            size = (150, 400, 900)[r % 3]
+            again = lay(pre, post, [ops[n][6] - e + ((n * 7919 + r * 104729) % size if t0 <= e < t0 + STRETCH else size / 2)
+                                    for n, e in enumerate(best[1])])
+            again += (takes(again[0]),)
+            if again[2] < best[2]:
+                best = again
+        GRAPH.append(best[2])
         return best[0]
 
     def mm(out, l, r, start=False, stop=False):
         run("p", lambda q: q.matmul(out[0], l[0], r[0], start, stop), [l, r], [out], max(min(64, l[5]), r[5]) * CYCLE / 2)
 
+    def flip(out, a):
+        run("p", lambda q: q.transpose(out[0], a[0], I1[0]), [a, I1], [out], 128 * CYCLE / 2)
+
     def tt(out, a, b, op, xr=()):
         run("v", lambda q: q.tensor_tensor(out[0], a[0], b[0], op), [a, b] + list(xr), [out],
             cost(out, [a, b], 2.0 if SCRATCH[a[1]][0] == SCRATCH[b[1]][0] else 1.0))
 
-    def ts(out, a, s1, op0, s2=None, op1=None):
-        xr = [s for s in (s1, s2) if isinstance(s, tuple)]
+    def ts(out, a, s1, op0, s2=None, op1=None, xr=()):
+        xr = list(xr) + [s for s in (s1, s2) if isinstance(s, tuple)]
         v1 = s1[0] if isinstance(s1, tuple) else s1
         v2 = s2[0] if isinstance(s2, tuple) else s2
         if op1 is None:
@@ -218,6 +302,9 @@ def rank_program(g, core, T, topo):
     def scan(out, d0, d1, init, op0, op1):
         run("v", lambda q: q.tensor_tensor_scan(out[0], d0[0], d1[0], init, op0, op1), [d0, d1], [out], cost(out, [d0, d1]))
 
+    def reduce(out, a, op, size=False):
+        run("v", lambda q: q.tensor_reduce(out[0], a[0], AX.X, op, apply_absolute_value=size), [a], [out], cost(a, [a], 1.0))
+
     def act(out, a, func=AF.Identity, xr=(), acc=None, **kw):
         xr = list(xr) + [v for v in kw.values() if isinstance(v, tuple)]
         kw = {k: (v[0] if isinstance(v, tuple) else v) for k, v in kw.items()}
@@ -225,8 +312,17 @@ def rank_program(g, core, T, topo):
             kw["accum_out"] = acc[0]
         run("a", lambda q: q.activation(out[0], a[0], func, **kw), [a] + xr, [out] + ([acc] if acc else []), cost(out, [a], 1.0))
 
-    def pick(out, win, off, e="a"):
-        (act if e == "a" else cp)(out, IND(win, off), xr=[off])
+    NOW = [0]
+    scalar = lambda step, k: dict(WHO, **{0: START, RO - 1: FINISH}.get(NOW[0], {}))[step][k] == "a"
+
+    def copy(step, k, out, a, *xr):
+        (act if scalar(step, k) else cp)(out, a, xr=xr)
+
+    def line(step, k, out, a, scale, bias, *xr):
+        if scalar(step, k):
+            act(out, a, xr=xr, scale=scale, bias=bias)
+        else:
+            ts(out, a, scale, ALU.mult, bias, ALU.add, xr=xr)
 
     SENT = (None, "pc", 300, 301, 1, 1)
     POOL = (None, "pc", 100, 101, 1, 1)
@@ -241,22 +337,31 @@ def rank_program(g, core, T, topo):
     def fill(out, c):
         iota(out, [[0, out[5]]], int(c), 0)
 
+    def flat(out, c, p=(0, 128)):
+        act(out, A("iN", 0, out[5], 1, p), scale=0.0, bias=float(c))
+
+    def put(step, j, out, c, p=(0, 128)):
+        flat(out, c, p) if scalar(step, j) else ms(out, c)
+
     CH = lambda n, k, c0=0, c1=128, step=1: A(n, 128 * k + c0, 128 * k + c1, step)
     B = lambda n, c0=0, c1=128, step=1: A(n, c0, c1, step)
     LAST = lambda n, k=0: CH(n, k, 15, 128, 16)
-    E8 = lambda n: A(n, 0, 8)
+    E8 = lambda n, k=0: A(n, 8 * k, 8 * k + 8)
     F = lambda k, p=(0, 128): A("pf", k, k + 1, 1, p)
     ROW = lambda n, c0=0, c1=128, p=0: A(n, c0, c1, 1, (p, p + 1))
     PR = lambda k: A3("prb", S(8 * k, 8 * k + 8), S(0, 16))
-    PT3 = lambda t: A3("Pt", S(8 * t, 8 * t + 8), S(0, 16))
-    I1 = A("R136", 8, BW)
+    PT3 = lambda t, name="Pt": A3(name, S(8 * t, 8 * t + 8), S(0, 16))
+    I1 = A("I1")
+    BEST = lambda k: LAST("KS", k)
+    RX = lambda c0, c1, p, step=1, u=S(0, 2): (T.RX[0:p, u, c0:c1:step], "RX", c0, c1, 1, len(range(2)[u]) * len(range(c0, c1, step)))
+    SCALE, UNSCALE = F(13), F(14)
     LANE = [[0, 8], [1, 16]]
     rho = lambda t: (5 * t) % 16
 
-    dma("y", A3("tsti", S(0, 24), S(0, 16)), None, "ld0", iap=T.tst[:])
+    dma("y", A3("tsti", S(0, 24), S(0, 16))[:5] + (LOAD,), None, "ld0", iap=T.tst[:])
     dma("a", A3("prb", S(0, 24), S(0, 16)), None, "ld1", iap=T.pr[:])
-    dma("y", A("U", LOW, LOW + 2048), None, "ld3", iap=T.cov[:, 0:2048])
-    dma("a", A("U", LOW + 2048, LOW + W), None, "ld4", iap=T.cov[:, 2048:4096])
+    for u in range(16):
+        dma("ya"[u % 2], (T.U[u:128:16, LOW:UW], "U", LOW + u, UW, 16, 500), None, "ld%d" % (3 + u % 2), iap=T.cov[15 - u:128:16, :])
     dma("y", A("thi", 0, 1, 1, (0, 8)), None, "ld2", iap=T.th[:])
 
     def constants():
@@ -268,238 +373,378 @@ def rank_program(g, core, T, topo):
         ts(P(2), P(0), 15, ALU.bitwise_and)
         cp(A("pf", 0, 2), A("pc", 1, 3))
         ts(F(9), P(0), 256.0, ALU.add)
-        ts(A("uA"), B("iN"), -1.0, ALU.mult, F(9), ALU.add)
         ts(A("mB"), B("iN"), 4, ALU.arith_shift_right)
         ts(A("si"), B("iN"), 15, ALU.bitwise_and)
-        ts(A("uA"), A("uA"), 15, ALU.bitwise_and)
-        ts(A("uD"), A("mB"), F(0), ALU.subtract, -16.0, ALU.mult)
         act(F(6), F(1), scale=16.0 * 613)
-        tt(A("uM"), A("uA"), A("uD"), ALU.add)
-        ts(I1, A("uM"), 0.0, ALU.is_equal)
+        sel(I1, A("ones"), [[-1, 128]], ALU.is_equal, 0.0, 0, 1)
         ts(A("A16", 0, RO), A("iN", 0, RO), 16.0 * 77, ALU.mult, F(6), ALU.add)
         act(A("I4k"), I1, scale=4096.0)
-        sel(A("R136", 0, 8), A("ones", 0, 8), [[-16, 8]], ALU.is_equal, 0.0, 0, 1)
         ts(A("Blk"), A("mB"), F(0), ALU.is_equal)
-        act(A("B4k"), A("Blk"), scale=-4096.0)
+        ts(CH("B4k", 0), A("mB"), F(0), ALU.is_equal, -4096.0, ALU.mult)
+        ts(CH("B4k", 1), CH("B4k", 0), -1.0, ALU.mult)
         act(A("BlkN"), A("Blk"), scale=-1.0)
+        act(A("BlkF"), A("Blk"), scale=FAR)
         ts(A("o16"), A("iN", 0, 16), F(1), ALU.is_equal)
         for b in range(16):
             ts(CH("WB", b), A("Blk"), A("o16", b, b + 1), ALU.mult)
-        ms(A("pT"), VOID)
-        fill(A("U", 0, LOW), VOID)
+        flat(A("U", 0, LOW), VOID)
         for c in range(8):
             ts(A("x0", c, C, 8), A3("tsti", S(c, 24, 8), S(0, 16)), 1.0 / 32, ALU.mult, 1.0 / 64, ALU.add)
-        for k in ORDER:
-            mm(B("V", 128 * k, 128 * k + 128), PR(k), I1, True, True)
-            act(A("pT", BW * k + 8, BW * k + BW), B("V", 128 * k, 128 * k + 128))
         act(F(2), F(0), scale=16.0, bias=15.0)
-        act(F(3), F(1), scale=-136.0, bias=2048.0)
+        act(F(7), F(1), scale=-1.0, bias=15.0)
+        act(F(8), F(1), scale=-1.0, bias=F(2))
+        for j, (src, out) in enumerate(((1, SCALE), (7, F(15)))):
+            ts(F(17 + j), F(src), 15.0, ALU.is_lt, F(src), ALU.mult)
+            ts(A("pw", 16 * j, 16 * j + 16), A("iN", 0, 16), F(17 + j), ALU.is_ge, 2.0 ** -8, ALU.max)
+            reduce(out, A("pw", 16 * j, 16 * j + 16), ALU.mult)
+        ts(A("pw", 32, 48), A("pw", 0, 16), 1.0, ALU.is_lt, 255.0, ALU.mult)
+        act(A("pw", 32, 48), A("pw", 32, 48), bias=1.0)
+        reduce(UNSCALE, A("pw", 32, 48), ALU.mult)
+        act(F(16), UNSCALE, scale=4096.0)
+        act(F(10), F(0), scale=-15.0, bias=113.0)
+        ts(F(11), F(1), 0.0, ALU.is_equal, F(10), ALU.mult)
+        act(F(12), F(11), bias=F(8))
+        ts(A("Pm"), B("iN"), F(8), ALU.is_equal, F(15), ALU.mult)
+        ts(A("Pp"), A("iN", 0, BW), F(12), ALU.is_equal, F(15), ALU.mult)
+        ts(A("Back"), B("iN"), F(8), ALU.is_equal)
+        act(B("pk"), I1, scale=UNSCALE)
+        mm(B("M2"), A("ones"), B("pk"), True, True)
+        act(A("pT", 3 * BW, 3 * BW + 128), B("M2"))
+        put("RS", 2, A("pT", 3 * BW + 128, 4 * BW), 1.0)
+        price = lambda c0=0, c1=BW, step=1: A("RC", BW + c0, BW + c1, step, (0, 1))
+        flat(price(), 0.0, (0, 1)), flat(price(15, 128, 16), TOP, (0, 1))
+        for k in ORDER:
+            w, turned = (128, A("Back")) if k in BARE else (BW, A("Pp"))
+            bank = B("DHD"[k], 0, w)
+            mm(bank, PR(k), turned, True)
+            mm(bank, A("ones"), turned, False, k in BARE)
+            if k not in BARE:
+                mm(bank, ROW("ones"), price(), False, True)
+            act(A("pT", BW * k, BW * k + w), bank)
+        act(F(3), F(1), scale=128.0, bias=16.0)
         act(F(4), F(1), scale=128.0, bias=15.0)
-        act(F(5), F(1), scale=16.0, bias=-256.0)
-        act(A("Rneg"), I1, scale=-65536.0)
-        act(A("I16"), I1, scale=0.0625)
-        iota(A("RK"), [[-16, 8], [-1, 16]], 136, 0)
-        iota(A("RK", 0, 128, 16), [[-1, 8]], 144, 0)
-        ts(A("SEL"), A("iN"), F(2), ALU.is_equal, 4096.0, ALU.mult)
-        ts(E8("BO"), E8("iN"), F(0), ALU.is_equal, 4096.0, ALU.mult)
-        ts(A("KT"), A("RK"), F(3), ALU.add)
+        act(F(5), F(1), scale=-16.0, bias=-16.0)
+        act(F(19), F(1), scale=8.0, bias=16.0 + 2048)
+        act(CH("Rneg", 0), A("Pm"), scale=-16.0 if EARLY[0] else -65536.0)
+        if not ROUND:
+            act(A("I16"), I1, scale=0.0625)
+        p8, p96 = (0, 8), (96, 98)
+        if EARLY[0]:
+            act(A("R4k"), A("I4k"), scale=SCALE)
+        ts(E8("R8"), E8("iN"), F(0), ALU.is_equal)
+        mm(B("G"), A("ones"), A("Pm"), True, True)
+        mm(A("G", 128, 256, 1, p8), E8("R8"), A("Pm"), True, True)
+        act(B("RK"), B("G"))
+        act(ROW("RK", 128, 256), ROW("G"))
+        act(A("Blk8", 128, 256, 1, p8), A("G", 128, 256, 1, p8))
+        r64 = lambda n, c0=0, c1=128, step=1: A(n, c0, c1, step, (64, 66))
+        f64 = lambda k: F(k, (64, 66))
+        ts(f64(20), f64(9), 320.0, ALU.is_equal)
+        act(f64(21), f64(20), scale=-2032.0, bias=2048.0)
+        ts(r64("RC"), r64("iN"), 16.0, ALU.add, f64(20), ALU.mult)
+        act(r64("RC", 15, 128, 16), r64("iN", 0, 8), scale=f64(20), bias=f64(21))
+        tt(r64("RK"), r64("RC"), r64("RK"), ALU.mult)
+        flat(A("RK", 15, 128, 16, (32, 33)), 0.0625, (32, 33))
+        if min(EARLY) < 16:
+            ts(A("SEL"), A("iN"), F(2), ALU.is_equal, 4096.0, ALU.mult)
+        act(E8("BO"), E8("R8"), scale=F(16))
+        act(A("KT"), B("iN"), bias=F(3))
+        act(LAST("KT"), E8("iN"), bias=F(19))
+        ms(B("KM"), 2.0 ** -8), fill(A("KM", 0, 128, 16), 0), flat(LAST("KM"), 2.0 ** 56)
+        act(LAST("KM"), LAST("KM"), scale=2.0 ** 56)
         ms(A("LK"), 0.0), ms(A("RV", 0, 128), 0.0), ms(A("TL"), 0.0)
-        iota(ROW("LK", p=32), [[0, 8], [-136, 16]], 2048, 0, True)
-        ms(ROW("LK"), 1.0), ms(ROW("LK", p=64), 1.0), ms(A("LK", 0, 128, 1, (96, 98)), 1.0)
-        ms(ROW("RK", p=32), 1.0), ms(ROW("RK"), 0.0)
-        p8 = (0, 8)
-        sel(A("Blk8", 0, 128, 1, p8), A("ones", 0, 128, 1, p8), [[-1, 8], [0, 16]], ALU.is_equal, 0.0, 0, 1)
+        act(ROW("LK", p=32), ROW("si", p=32), scale=128.0)
+        for j, p in enumerate(((0, 1), (64, 66), p96)):
+            put("LK", j, A("LK", 0, 128, 1, p), 1.0, p)
+        flat(ROW("RK"), 0, (0, 1))
         ts(A("thi", 2, 3, 1, p8), A("thi", 0, 1, 1, p8), 4, ALU.arith_shift_right)
         ts(A("thi", 3, 4, 1, p8), A("thi", 0, 1, 1, p8), 15, ALU.bitwise_and)
-        ts(A("TL", 96, 97, 1, p8), A("thi", 2, 3, 1, p8), -65536.0, ALU.mult)
-        ts(A("TL", 97, 98, 1, p8), A("thi", 3, 4, 1, p8), -4096.0, ALU.mult)
-        for j in range(2):
-            ts(A("D8", 8 * j, 8 * j + 8, 1, p8), A("Blk8", 0, 128, 16, p8), A("TL", 96 + j, 97 + j, 1, p8), ALU.mult)
-        mm(A("M2", 0, 128, 1, (0, 98)), A("TL", 0, 98, 1, p8), A("Blk8", 0, 128, 1, p8), True, True)
-        for j in range(2):
-            mm(B("M2", 128, 136), A("ones", 0, 128, 1, p8), A("D8", 8 * j, 8 * j + 8, 1, p8), j == 0, j == 1)
-        act(A("RK", 0, 128, 1, (96, 98)), A("M2", 0, 128, 1, (96, 98)))
+        act(A("TL", 96, 97, 1, p8), A("thi", 2, 3, 1, p8), scale=-65536.0, bias=127.0 * 65536 if EARLY[0] else -65536.0)
+        act(A("TL", 97, 98, 1, p8), A("thi", 3, 4, 1, p8), scale=-4096.0)
+        ts(A("cst", 8, 16, 1, p8), A("I1", 0, 8, 1, p8), A("TL", 97, 98, 1, p8), ALU.mult)
+        mm(A("M2", 0, 128, 1, (0, 98)), A("TL", 0, 98, 1, p8), A("Blk8", 128, 256, 1, p8), True, True)
+        mm(B("M2", 128, 136), A("ones", 0, 128, 1, p8), A("cst", 8, 16, 1, p8), True, True)
+        act(A("RK", 0, 128, 1, p96), A("M2", 0, 128, 1, p96))
         act(E8("THs"), B("M2", 128, 136))
         act(E8("THn"), B("M2", 128, 136))
-        ms(ROW("RV"), -MAGIC), ms(ROW("RV", 128, 256), -0.46875), ms(ROW("RV", 256, 384), MAGIC)
-        iota(ROW("RV", p=64), [[0, 8], [-256, 16]], 3968, 0, True)
-        iota(ROW("RV", 384, 512), [[0, 8], [-4096, 16]], 63488, 0)
+        sel(A("Blk8", 0, 128, 1, p8), A("ones", 0, 128, 1, p8), [[-1, 8], [0, 16]], ALU.is_equal, 0.0, 0, 1)
+        if BARE:
+            act(CH("Rneg", 1), A("Back"), scale=-16.0 if EARLY[0] else -65536.0)
+            act(E8("BO", 1), E8("R8"), scale=4096.0)
+            fill(CH("KM", 1), 1), fill(CH("KM", 1, 0, 128, 16), 0)
+            fill(CH("RK", 2), 1), fill(ROW("RK", 256, 384), 0)
+            act(r64("RK", 256, 384), r64("RC"))
+            flat(A("RK", 256 + 15, 384, 16, (32, 33)), 0.0625, (32, 33))
+            mm(A("M2", 256, 384, 1, (0, 98)), A("TL", 0, 98, 1, p8), A("Blk8", 0, 128, 1, p8), True, True)
+            act(A("RK", 256, 384, 1, p96), A("M2", 256, 384, 1, p96))
+        for j, c in enumerate((-65536.0 - 1408 - 128,) if ROUND else (-MAGIC - 65536, -0.46875, MAGIC)):
+            put("RV", j, ROW("RV", 128 * j, 128 * j + 128), c, (0, 1))
+        act(ROW("RV", p=64), ROW("si", p=64), scale=-256.0, bias=3968.0)
+        act(ROW("RV", 384, 512), ROW("si"), scale=-4096.0, bias=-2048.0)
         sel(A("TriN"), A("BlkN"), [[1, 128]], ALU.is_gt, 0.0, 0, -1)
         sel(A("TriN"), A("TriN"), [[-1, 128]], ALU.not_equal, 1.0, 0, 1)
         for u in range(2):
             for g1 in range(2):
                 sel(CH("J", 2 * u + g1), A("ones"), [[32, 4], [1000, 2], [2, 16]], ALU.is_equal, 0.0, u - 1000 * g1, -1)
         for k in range(3):
-            fill(A("RT%d" % k, RW, RW + 32), VOID)
-        ms(A("RS0"), BIG), fill(A("RSp"), 0.0), fill(A("E3"), 0.0)
+            flat(A("RT%d" % k, 0, 16), VOID + 1)
+        flat(A("E3"), 0.0), ms(A("XI"), 0.0)
         cp(E8("rep"), E8("iN"))
-        ts(E8("r15"), E8("iN"), 16.0, ALU.mult, 15.0, ALU.add)
         sel(A("Perm"), A("ones"), [[1, 16], [16, 8]], ALU.is_equal, 0.0, 0, -1)
-        act(A("RSm"), A("RS0"))
-        ms(A("RS0", 0, 128, 16), 0.0), ms(A("RSm", 0, 128, 16), -BIG), ms(A("RSp", 0, 528, 66), BIG)
+        put("RS", 0, A("RSm"), BIG), put("RS", 1, A("RSm", 0, 128, 16), -BIG)
         act(A("I64k"), I1, scale=65536.0)
-        act(A("PermF"), A("Perm"), scale=FLAG)
+        act(A("PermF"), A("Perm"), scale=-16.0)
         act(A("PermN"), A("Perm"), scale=-1.0)
         act(A("Ineg"), I1, scale=-1.0)
-        ts(A("DG"), A("si"), F(1), ALU.is_equal)
-        iota(A("MASK"), [[0, 2], [-16, 4], [1, 64]], 0, 0)
-        ts(A("MASK"), A("MASK"), F(1), ALU.is_ge, FAR, ALU.mult)
-        act(F(8), F(1), bias=16.0)
-        for u in range(2):
-            ts(A("RSp", 264 * u + 65, 264 * u + 264, 66), A("iN", 0, 4), 16.0, ALU.mult, F(8), ALU.add)
-        fill(A("DA", 65, 528, 66), FAR)
+        iota(A("XJ"), [[0, 8], [1, 17]], -1, 0)
+        ts(A("XH"), A("XJ"), F(1), ALU.is_equal, HIDE, ALU.mult)
+        ts(A("XJ"), A("XJ"), F(1), ALU.is_lt)
+        tt(A("XH"), A("XH"), A("XJ"), ALU.add)
+        act(A("XH", 1, 136, 17), A("XH", 1, 136, 17), scale=1 / HIDE)
+        fill(A("XH", 0, 136, 17), 0)
+        p64 = (0, 64)
+        ts(A("LX", 0, 128, 1, p64), A("si", 0, 128, 1, p64), 288.0, ALU.add, F(9, p64), ALU.is_equal)
+        if "a" in SIZES:
+            act(A("LY", 0, 128, 1, p64), A("LX", 0, 128, 1, p64))
+        for v in range(4):
+            row = RX(SPAN[v], SPAN[v + 1], 64)
+            iota(row, [[0, row[5]]], LOW - 66 - 32 + 16 * v, 1)
+            sel(row, row, [[0, 2], [-16, v + 1], [-1, 17]], ALU.is_gt, BIG, 16 * v + 1 - 32, 1)
+        lead = RX(0, SPAN[4], 64, 17)
+        sel(lead, lead, [[0, 20]], ALU.is_gt, BIG, 0, 0)
+        ms(RX(0, SPAN[4], 32), -FAR)
+        for v in range(4):
+            fill(RX(SPAN[v], SPAN[v] + 1, 64), 2048.0 + LOW)
+            row = RX(SPAN[v] + 1, SPAN[v + 1], 32)
+            sel(row, row, [[4, 2], [0, row[5] // 2]], ALU.is_equal, 0.0, v, -1)
+            sel(RX(SPAN[v], SPAN[v] + 1, 32), A("ones", 0, 2, 1, (0, 32)), [[4, 2]], ALU.is_equal, 0.0, v, -1)
         ts(E8("CV"), E8("iN"), 16.0, ALU.mult, F(4), ALU.add)
         ts(A("WR"), A("iN"), F(2), ALU.is_equal, F(5), ALU.mult)
-        for t in range(RO):
-            last = t == RO - 1
-            ts(A("XB", t, t + 1), F(1), float(rho(t)), ALU.is_equal, 256.5 - 2176 if last else (256.5 - 2176) / 32, ALU.mult)
-        ts(A("XB", RO - 1, RO), A("XB", RO - 1, RO), -0.5, ALU.add)
+        act(A("XB", 0, RO - 1), A("o16", 0, 16, 5), scale=(256.5 - 2176) / 32)
+        act(A("XB", RO - 1, RO), A("o16", rho(RO - 1), rho(RO - 1) + 1), scale=256.5 - 2176, bias=-0.5)
         act(A("Im32"), I1, scale=-32.0)
         act(A("onesN"), A("ones"), scale=-1.0)
-        ms(ROW("cst", 0, 1), 127.5), ms(ROW("cst", 1, 2), M256), ms(ROW("cst", 2, 3), -M256)
-        sel(A("PermT"), A("ones"), [[1, 8], [8, 16]], ALU.is_equal, 0.0, 0, -1)
+        for j, c in enumerate((127.5, M256, -M256)):
+            put("cst", j, ROW("cst", j, j + 1), c, (0, 1))
 
     def matrices(t):
-        if t == 0:
-            ts(PT3(t), A("uM"), t + 1.0, ALU.is_equal, -4096.0, ALU.mult)
-            tt(CH("Pn", t), A("I4k"), PT3(t), ALU.subtract)
-        else:
-            sel(PT3(t), A("B4k"), [[-1, 128]], ALU.is_equal, 0.0, -1 - t, 1)
-            wrap = A3("Pt", S(8 * t, 8 * t + 8), S(15 - t, 16))
-            sel(wrap, wrap, [[-16, 8], [-1, t + 1]], ALU.not_equal, -4096.0, 0, 1)
-            act(CH("Pn", t), PT3(t), scale=-1.0)
-            sel(CH("Pn", t), CH("Pn", t), [[-1, 128]], ALU.not_equal, 4096.0, 0, 1)
+        for name, sign in (("Pt", -1), ("Pn", 1)):
+            sel(PT3(t, name), CH("B4k", sign > 0), [[-1, 128]], ALU.is_equal, 0.0, -1 - t, 1)
+        for name, sign in (("Pt", -1), ("Pn", 1)):
+            wrap = A3(name, S(8 * t, 8 * t + 8), S(15 - t, 16))
+            sel(wrap, wrap, [[-16, 8], [-1, t + 1]], ALU.not_equal, 4096.0 * sign, 0, 1)
+        sel(PT3(t, "Pn"), PT3(t, "Pn"), [[-1, 128]], ALU.not_equal, 4096.0, 0, 1)
         sel(CH("Tri", t), A("TriN"), LANE, ALU.not_equal, 0.0, -rho(t), 0)
         sel(CH("Ir", t), A("Im32"), LANE, ALU.not_equal, 0.0, -rho(t), 0)
 
     def prices(k, n, bank, e):
-        b0, b1 = PIECES[n]
-        for b in range(b0, b1):
-            mm(B(bank, BW * (b - b0), BW * (b - b0 + 1)), CH("WB", b), A("pT", BW * k, BW * k + BW), True, True)
-        (act if e == "a" else cp)(A("PT", RW * k + BW * b0, RW * k + BW * b1), B(bank, 0, BW * (b1 - b0)))
+        c0, w, blocks = (0, 128, range(4 * n, 4 * n + 4)) if n < 4 else (128, 8, range(16))
+        for j, b in enumerate(blocks):
+            mm(B(bank, w * j, w * j + w), CH("WB", b), A("pT", BW * k + c0, BW * k + c0 + w), True, True)
+        (act if e == "a" else cp)(A("PT", AT[k] + 512 * n, AT[k] + 512 * n + w * len(blocks)), B(bank, 0, w * len(blocks)))
 
-    def spread(k):
-        rows = (T.Dp[k], "Dp", k, k + 1, 1, BW)
-        dma("y", rows, A("pT", BW * k, BW * k + BW), "dp%d" % k)
-        for i in range(16):
-            dma("y", (T.PT[i:128:16, RW * k:RW * k + RW], "PT", RW * k + i, RW * k + RW, 16, 2500), rows, "pt%d" % k)
+    def spread(n, parts):
+        for k in parts:
+            for j in range(2):
+                for c0, c1, w0, w1 in ((0, 2048, 0, 128), (2048, RW, 128, BW))[:1 if k in BARE else 2]:
+                    c0, c1 = AT[k] + c0, AT[k] + c1
+                    dma("y", (T.Dp[:, j, c0:c1], "Dp", 2 * c0 + j, 2 * c1, 2, BW), A("pT", BW * k + w0, BW * k + w1), "dp%d" % k)
+        c0, c1 = AT[parts[0]], AT[parts[-1]] + (2048 if parts[-1] in BARE else RW)
+        for i in range(8):
+            dma("y", (T.PT[i:128:8, c0:c1], "PT", c0 + i, c1, 16, 1000 * len(parts)), (T.Dp[:, :, c0:c1], "Dp", 2 * c0, 2 * c1, 1, BW), "pt%d" % n)
 
     def codes(t, k):
         x = CH("x%d" % t, k)
-        act(CH("nH", k), x, AF.Relu, scale=2.0 ** 20, bias=-2.0 ** 23)
-        mm(B("V", 128, 256), PT3(t), x, True)
-        mm(B("V", 128, 256), CH("Pn", t), CH("nH", k), False, True)
-        tt(CH("t1", k), x, B("V", 128, 256), ALU.mult)
-        act(CH("t2", k), CH("t1", k), scale=-1.0, bias=A("A16", t, t + 1))
+        if scalar("nH", k):
+            act(CH("nH", k), x, AF.Relu, scale=2.0 ** 20, bias=-2.0 ** 23)
+        else:
+            ts(CH("nH", k), x, 8.0, ALU.is_gt, 2.0 ** 14, ALU.mult)
+        Y, M = B(CODES[k], 256, 384), B(CODES[k], 384, 512)
+        mm(Y, PT3(t), x, True)
+        mm(Y, PT3(t, "Pn"), CH("nH", k), False, True)
+        pair = (CH("Tri", t), CH("nH", k))[::1 if TAKE[k] == "p" or t == RO - 1 else -1]
+        if t:
+            mm(M, *pair, True, True)
+        tt(CH("t1", k), x, Y, ALU.mult)
+        if not t:
+            M = B("M2", 128 * k + 128, 128 * k + 256)
+            mm(M, *pair, True, True)
+        line("t2", k, CH("t2", k), CH("t1", k), -1.0, A("A16", t, t + 1))
         ts(CH("t3", k), CH("t2", k), 4, ALU.arith_shift_right, 4095 - 2 ** 31, ALU.bitwise_and)
-        if k == FIRST:
+        if scalar("cu", k):
             act(CH("cu", k), CH("t3", k), AF.Relu, bias=float(LOW))
         else:
             ts(CH("cu", k), CH("t3", k), float(LOW), ALU.add, 0.0, ALU.max)
-        mm(B("M2", 256, 384), CH("nH", k), CH("Tri", t), True, True)
-        act(CH("FQ", k), B("M2", 256, 384), AF.Relu, scale=1.0 / 16384)
-        ts(CH("cf", k), CH("cu", k), -2048.0 - LOW, ALU.add)
+        if scalar("FQ", k):
+            act(CH("FQ", k), M, AF.Relu, scale=1.0 / 16384)
+        else:
+            ts(CH("FQ", k), M, 0.0, ALU.is_gt)
+        line("cf", k, CH("cf", k), CH("cu", k), 1.0, -2048.0 - LOW)
         if k == LATEST:
             for c in range(4):
                 turn(A3("TT", c, S(0, 96)), A("cf", c, C, 4))
 
+    TURN = [0]
+
     def gains(t, k):
-        got, RT = "got%d" % k, "RT%d" % k
-        for e, b0, b1 in GATHERS[k]:
-            pick(A(got, 128 * b0, 128 * b1), A("U"), CH("cu", k, 8 * b0, 8 * b1), e)
-        mm(B("G"), PR(k), A("Rneg"), True)
-        mm(B("G"), A("LK", 0, 128, 1, (0, 98)), A("RK", 0, 128, 1, (0, 98)))
-        for n, (b0, b1) in enumerate(ENDS if k == LATEST else PIECES):
-            bank = "T%d" % (n % 3)
+        got, RT, bare = "got%d" % k, "RT%d" % k, k in BARE
+        for e, b0, b1 in (GATHERS if t else OPENING)[k]:
+            out, off = A(got, 128 * b0, 128 * b1), CH("cu", k, 8 * b0, 8 * b1)
+            line(e, k, out, IND(A("U"), off), 1.0 if bare else SCALE, 1.0 if bare else SCALE, off)
+        if EARLY[k]:
+            mm(B("H"), CH("Rneg", bare), PR(k), True)
+        else:
+            mm(B(GAINS[k]), PR(k), CH("Rneg", bare), True)
+            mm(B(GAINS[k]), A("LK", 0, 128, 1, (0, 98)), A("RK", 256 * bare, 256 * bare + 128, 1, (0, 98)))
+        for b0, b1 in PIECES[k]:
+            bank, n = "T%d" % (TURN[0] % 2), 128 * (b1 - b0)
+            TURN[0] += 1
             for b in range(b0, b1):
-                mm(B(bank, BW * (b - b0), BW * (b - b0 + 1)), A(got, 128 * b, 128 * b + 128), A("R136"), True, True)
-            tt(A(RT, BW * b0, BW * b1), B(bank, 0, BW * (b1 - b0)), A("PT", RW * k + BW * b0, RW * k + BW * b1), ALU.max)
+                flip(CH(bank, b - b0), CH(got, b))
+            out, price = A(RT, 16 + 128 * b0, 16 + 128 * b1), A("PT", AT[k] + 128 * b0, AT[k] + 128 * b1)
+            plain = A(RT, 2064 + 8 * b0, 2064 + 8 * b1)
+            if b1 - b0 <= SHORT or bare:
+                tt(out, A(bank, 0, n), price, ALU.max)
+                copy("plain", k, plain, A(bank, 15, n, 16))
+            else:
+                cp(plain, A(bank, 15, n, 16))
+                scan(out, A(bank, 0, n), price, TOP, ALU.min, ALU.max)
+                tt(A(RT, 31 + 128 * b0, 16 + 128 * b1, 16), plain, A("PT", AT[k] + 2048 + 8 * b0, AT[k] + 2048 + 8 * b1), ALU.max)
             for b in range(b0, b1):
-                mm(B("G"), A("SEL", 15 - b, 143 - b), A(RT, BW * b + 8, BW * b + BW), False, b == 15)
+                block = A(RT, 16 + 128 * b, 144 + 128 * b)
+                if b < EARLY[k]:
+                    mm(B("H", b, 128, 16), block, E8("R8"), False, b == EARLY[k] - 1)
+                else:
+                    mm(B(GAINS[k]), A("SEL", 15 - b, 143 - b), block, False, b == 15)
+                if b == EARLY[k] - 1:
+                    line("Gt", k, CH("Gt", k), B("H"), 1.0 if bare else UNSCALE, -2048.0)
+                    mm(B("G"), A("LK", 0, 128, 1, (0, 98)), A("RK", 256 * bare, 256 * bare + 128, 1, (0, 98)), True)
+                    mm(B("G"), CH("Gt", k), A("I4k" if bare else "R4k"), False, b == 15)
 
     def votes(k):
-        mm(B("V"), ROW("ones"), ROW("RV", 128, 256), True)
-        mm(B("V"), CH("cf", k), A("I16"))
-        mm(B("V"), ROW("ones"), ROW("RV", 256, 384))
+        if ROUND:
+            line("c16", k, CH("c16", k), CH("cu", k), 0.0625, 1408 - LOW / 16 - 0.46875)
+            mm(B("V"), CH("c16", k), I1, True)
+        else:
+            mm(B("V"), ROW("ones"), ROW("RV", 128, 256), True)
+            mm(B("V"), CH("cf", k), A("I16"))
+            mm(B("V"), ROW("ones"), ROW("RV", 256, 384))
         mm(B("V"), A("LK", 0, 128, 1, (0, 65)), A("RV", 0, 128, 1, (0, 65)))
         for i in range(16):
-            mm(B("V", i, 128, 16), A("got%d" % k, i, 2048, 16), E8("BO"))
+            mm(B("V", i, 128, 16), A("got%d" % k, i, 2048, 16), E8("BO", k in BARE), False, i == 15)
+        scan(A("VS"), A("RSm"), B("V"), -BIG, ALU.min, ALU.max)
+        ts(E8("vx", k), LAST("VS"), 255 + 2 ** 24, ALU.bitwise_and)
+        if scalar("tk", k):
+            act(E8("tk", k), E8("vx", k), AF.Relu, scale=-1.0, bias=256.0)
+        else:
+            ts(E8("tk", k), E8("vx", k), -256.0, ALU.add, 0.0, ALU.min)
 
     def best(k):
-        scan(CH("KS", k), A("RS0"), B("G"), 0.0, ALU.min, ALU.max)
-        ts(A("ka"), LAST("KS", k), 4095, ALU.bitwise_and)
-        act(E8("wl"), A("ka"), scale=-1.0, bias=float(NOWT))
-        pick(A("pk"), A("RT%d" % k), E8("wl"))
-        if k == LATEST:
-            pick(A("KB"), CH("KS", k), E8("r15"))
-            tt(A("OH"), A("KB"), B("G"), ALU.is_equal)
+        wl = E8("wl", k)
+        scan(CH("KS", k), CH("KM", k in BARE), B(GAINS[k]), 0.0, ALU.mult, ALU.max)
+        ts(E8("ka", k), BEST(k), 4095, ALU.bitwise_and)
+        copy("wl", k, wl, E8("ka", k))
+        if k in BARE:
+            copy("sc", k, CH("pk", k), IND(A("RT%d" % k), wl), wl)
         else:
-            tt(A("OH"), IND(A("ka"), E8("rep")), A("KT"), ALU.is_equal, xr=[E8("rep")])
-        mm(B("M2"), A("OH"), I1, True, True)
-        act(CH("nB", k), B("M2"), scale=-1.0, bias=1.0, acc=A("acc", k, k + 1))
-
-    OL = lambda k, u, c0=260, c1=264, step=1: A("oL", 528 * k + 264 * u + c0, 528 * k + 264 * u + c1, step)
+            copy("sc", k, CH("sc", k), IND(A("PT", AT[3] - 16, AT[3] + RW), wl), wl)
+            tt(CH("pk", k), IND(A("RT%d" % k), wl), CH("sc", k), ALU.mult, xr=[wl])
+        tt(CH("OH", k), IND(E8("ka", k), E8("rep")), A("KT"), ALU.is_equal, xr=[E8("rep")])
+        mm(B("M2"), CH("OH", k), I1, True, True)
+        line("nB", k, CH("nB", k), B("M2"), -1.0, 1.0)
 
     def claims(k):
-        mm(B("K"), ROW("ones"), ROW("RV", 384, 512), True)
+        K = lambda c0=0, c1=128, p=(0, 128): A("K", c0, c1, 1, p)
+        mm(K(), ROW("ones"), ROW("RV", 384, 512), True)
         for u in range(2):
             for g1 in range(2):
-                mm(B("K", 64 * u, 64 * u + 64), CH("J", 2 * u + g1), A3("TT", S(0, 4), S(32 * k + 16 * g1, 32 * k + 16 * g1 + 16)))
-        mm(B("K"), A("pk"), A("I64k"), False, True)
-        scan(A("MS"), A("RSm"), B("K"), -BIG, ALU.min, ALU.max)
-        ts(E8("xp"), LAST("MS"), 4095 - 2 ** 31, ALU.bitwise_and)
-        ts(A("X1"), E8("xp"), -2048.0, ALU.add, -2048.0 - LOW, ALU.max)
-        D = lambda c0, c1: B("T0" if k == LATEST and c0 < 256 else "D", c0, c1)
+                mm(K(64 * u, 64 * u + 64), CH("J", 2 * u + g1), A3("TT", S(0, 4), S(32 * k + 16 * g1, 32 * k + 16 * g1 + 16)))
+        mm(K(), CH("pk", k), A("I64k"), False, True)
+        scan(CH("MS", k), A("RSm"), K(), -BIG, ALU.min, ALU.max)
+        ts(E8("xp", k), LAST("MS", k), 4095 - 2 ** 31, ALU.bitwise_and)
+        x0, d0, rows = 136 * k, 544 * k, ROWS[k]
+        own, p8, p48, h = A("XI", x0, x0 + 136, 17), (0, 8), (0, 48), SPAN[4]
+        ts(own, E8("xp", k), -2048.0, ALU.add, -2050.0, ALU.max)
+        sizes = SIZES[k] == "a"
+        if sizes:
+            act(E8("XF", k), own, scale=-FAR)
+            act(A("DA", d0, d0 + 544, 68), own, bias=2048.0 + LOW)
+        else:
+            mm(A(rows, 384, 512, 1, p8), own, I1, True, True)
+            copy("LX", k, A("LX", 0, 128, 1, p8), A(rows, 384, 512, 1, p8))
+        scan(A("XS", x0, x0 + 136), A("XH"), A("XI", x0, x0 + 136), 0.0, ALU.mult, ALU.add)
+        D = lambda u, c0, c1: B(ROWS[3], 256 + c0, 256 + c1) if k == LATEST and u == 0 else B(rows, h * u + c0, h * u + c1)
         for u, m in (((1, 1), (0, 1)) if k == LATEST else ((0, 2),)):
-            r = A("rep", 4 * u, 4 * (u + m))
-            tt(A("XD", 64 * u, 64 * (u + m)), IND(A("X1"), r), A("DG", 0, 64 * m), ALU.mult, xr=[r])
-            mm(D(256 * u, 256 * (u + m)), I1, A("MASK", 0, 256 * m), True)
+            if sizes:
+                mm(D(u, 0, h * m), A("LY", 0, 128, 1, p48), RX(0, h, 48, 1, S(u, u + m)), True)
+            else:
+                mm(D(u, 0, h * m), A("LX", 0, 128, 1, p48), RX(0, h, 48, 1, S(u, u + m)), True)
             for c in range(4 * u, 4 * (u + m)):
-                mm(D(64 * c, 64 * c + 64), A("Blk"), A("XD", 64 * (c // 4), 64 * (c // 4) + 64), False, c == 4 * (u + m) - 1)
-        act(A("DA", 64, 528, 66), A("X1"), bias=2048.0 + LOW)
-        act(A("XF"), A("X1"), scale=FAR)
-        if k != FIRST:
-            ts(E8("y1"), LAST("MS"), 12, ALU.arith_shift_right, 15, ALU.bitwise_and)
-            tt(E8("y2"), E8("CV"), E8("y1"), ALU.subtract)
-            act(E8("lv"), E8("y2"))
-            pick(CH("Vr", k), A("got%d" % k), E8("lv"))
+                v = c % 4
+                mm(D(c // 4, SPAN[v] + 1, SPAN[v + 1]), A("BlkF"), A("XS", x0 + 68 * (c // 4) + 1, x0 + 68 * (c // 4) + 17 * v + 17), False, c == 4 * (u + m) - 1)
+        if k == ORDER[1] and MIDDLE:
+            act(E8("lv", k), E8("xp", k), AF.Relu, bias=float(LOW))
+            copy("Vr", k, CH("Vr", k), IND(A("U"), E8("lv", k)), E8("lv", k))
+        elif k != FIRST:
+            y = E8("y1", k)
+            ts(y, LAST("MS", k), 12, ALU.arith_shift_right, 15, ALU.bitwise_and)
+            tt(y, y, E8("CV"), ALU.subtract)
+            line("lv", k, E8("lv", k), y, -1.0, 0.0)
+            line("Vr", k, CH("Vr", k), IND(A("got%d" % k), E8("lv", k)), 1.0 if k in BARE else UNSCALE, -1.0, E8("lv", k))
         for u in (1, 0):
             for c in range(4 * u, 4 * u + 4):
-                act(A("DA", 66 * c, 66 * c + 64), D(64 * c, 64 * c + 64), AF.Abs, scale=-FAR, bias=A("XF", c, c + 1))
-                scan(OL(k, u, c % 4, 264, 4), A("RSp", 66 * c, 66 * c + 66), A("DA", 66 * c, 66 * c + 66), 0.0, ALU.max, ALU.min)
-            if k == FIRST:
-                pick(CH("Vr", k, 64 * u, 64 * u + 64), A("U"), OL(k, u))
+                row, w = D(u, SPAN[c % 4], SPAN[c % 4 + 1]), 17 * (c % 4 + 1)
+                if sizes:
+                    c0 = d0 + 68 * c
+                    act(A("DA", c0 + 1, c0 + w), D(u, SPAN[c % 4] + 1, SPAN[c % 4 + 1]), AF.Abs, bias=A("XF", 8 * k + c, 8 * k + c + 1))
+                    row = A("DA", c0, c0 + w)
+                reduce(A("oL", 8 * k + c, 8 * k + c + 1), row, ALU.min, True)
+        if k == FIRST:
+            copy("Vr", k, CH("Vr", k), IND(A("U"), A("oL", 8 * k, 8 * k + 8)), A("oL", 8 * k, 8 * k + 8))
 
     def scatter(k, u):
-        o = OL(k, u)
+        o = A("oL", 8 * k + 4 * u, 8 * k + 4 * u + 4)
         tt(IND(A("U"), o), CH("Vr", k, 64 * u, 64 * u + 64), CH("nB", k, 64 * u, 64 * u + 64), ALU.mult, xr=[o])
 
     def places(t, k):
-        tt(E8("r1"), LAST("KS", k), E8("THn"), ALU.subtract)
-        ts(E8("r2"), E8("r1"), 12, ALU.arith_shift_right, 15, ALU.bitwise_and)
-        tt(LAST("E3"), E8("r2"), LAST("KS", k), ALU.min)
-        mm(B("V"), A("PermF"), A("OH"), False, True)
-        scan(A("VS"), A("RSm"), B("V"), -BIG, ALU.min, ALU.max)
-        ts(E8("vx"), LAST("VS"), 255 + 3 * 2 ** 24, ALU.bitwise_and)
-        act(E8("tkb"), E8("vx"), AF.Relu, scale=-1.0, bias=256.0)
-        tt(A("E2"), IND(E8("tkb"), E8("rep")), CH("FQ", k), ALU.mult, xr=[E8("rep")])
+        r, p8 = E8("r1", k), (0, 8)
+        tt(r, BEST(k), E8("THn"), ALU.subtract)
+        ts(r, r, 12, ALU.arith_shift_right, 15, ALU.bitwise_and)
+        tt(LAST("E3"), r, BEST(k), ALU.min)
+        wide = TAKE[k] == "p" or t == RO - 1
+        bank = {"M": "M2"}.get(TAKES[k], TAKES[k])
+        take, tkb = (A(bank, 256, 384, 1, p8), A("tkb", 0, 128, 1, p8)) if wide else (B(bank, 256, 264), A("tk", 32, 40))
+        pair = (lambda l, r: (l, r)) if wide else (lambda l, r: (r, l))
+        copy("fl", k, E8("tk", 3), BEST(k))
+        mm(take, *pair(E8("tk", k), I1 if scalar("tk", k) else A("Ineg")), True)
+        mm(take, *pair(E8("tk", 3), A("PermF")), False, True)
+        if scalar("tkb", k):
+            act(tkb, take, AF.Relu)
+        else:
+            ts(tkb, take, 0.0, ALU.max)
+        if wide:
+            mm(B(bank, 384, 512), A("Blk8", 0, 128, 1, p8), tkb, True, True)
+            tt(A("E2"), B(bank, 384, 512), CH("FQ", k), ALU.mult)
+        else:
+            tt(A("E2"), IND(tkb, E8("rep")), CH("FQ", k), ALU.mult, xr=[E8("rep")])
         s, X = 15 - rho(t), lambda c0=0, c1=128: B("M2", 128 + c0, 128 + c1)
         if t == RO - 1:
             mm(X(), A("E3", s, s + 128), A("Ineg"), True)
             for c in range(8):
                 mm(X(16 * c, 16 * c + 16), CH("Ir", t), CH("x%d" % t, k, c, 128, 8))
             mm(X(), A("WR", s, s + 128), CH("nB", k))
-            mm(X(), A("E2"), A("PermT"), False, True)
-            act(CH("yo", k), X(), scale=-1.0, bias=A("XB", t, t + 1))
+            for c in range(8):
+                mm(X(16 * c, 16 * c + 16), I1, B("E2", c, 128, 8), False, c == 7)
+            line("xo", k, CH("yo", k), X(), -1.0, A("XB", t, t + 1))
             dma("y", None, CH("yo", k), "o%d" % k, oap=T.yt[:, 128 * k:128 * k + 128])
             return
         mm(X(), CH("Ir", t), CH("x%d" % t, k), True)
+        mm(X(), A("E3", s, s + 128), A("PermN"))
         for c in range(8):
             mm(B("M2", 128 + c, 256, 8), A("WR", s, s + 128), CH("nB", k, 16 * c, 16 * c + 16))
-        mm(X(), A("E3", s, s + 128), A("PermN"))
-        mm(X(), A("E2"), I1, False, True)
+        mm(X(), *pair(I1, A("E2")), False, True)
         xo = CH("xo", 3 * t + k)
-        act(xo, X(), scale=-1.0 / 32, bias=A("XB", t, t + 1))
+        line("xo", k, xo, X(), -1.0 / 32, A("XB", t, t + 1))
         to, src = T.cores[(rank + 1) % len(T.cores)], T.cores[(rank - 1) % len(T.cores)]
         rid, pid = topo.addr(to, core)
         eng = topo.engines(core, to)[:8]
@@ -511,55 +756,66 @@ def rank_program(g, core, T, topo):
             sem[a], cnt[a] = T.sem[a], len(topo.engines(src, core)[:8])
             snap[(a, cnt[a])] = {}
             hist.setdefault(dst[1], []).append(dst[2:5] + (a, cnt[a], True))
-        ops.append(("g", write, [xo], [dst] + [SENT] * (k == LATEST), "st", 0, 3100.0 if (t, k) == (0, FIRST) else 600.0, FLIGHT + 1400))
+        ops.append(("g", write, [xo], [dst] + [SENT] * (k == (LATEST if t else FIRST)), "st", 0, 3100.0 if (t, k) == (0, FIRST) else 600.0, REMOTE))
 
     def useless():
         m = B("M2", 384, 385)
-        act(A("acch", 0, 3), A("acc", 0, 3), bias=-64.0)
-        mm(m, ROW("ones"), ROW("cst", 0, 1), True)
         for k in range(3):
-            mm(m, A("onesN"), A("acch", k, k + 1))
+            mm(B("M2", 385, 386), CH("nB", k), A("ones", 0, 1), k == 0, k == 2)
+        act(A("acch", 0, 1), B("M2", 385, 386), bias=-360.0)
+        mm(m, ROW("ones"), ROW("cst", 0, 1), True)
+        mm(m, A("onesN"), A("acch", 0, 1))
         mm(m, ROW("ones"), ROW("cst", 1, 2))
         mm(m, ROW("ones"), ROW("cst", 2, 3))
-        for k in range(3):
-            mm(m, A("ones"), A("acch", k, k + 1), False, k == 2)
-        act(A("mneg", 0, 1), m, scale=-4096.0)
-        act(ROW("RK"), ROW("ones"), scale=A("mneg", 0, 1, 1, (0, 1)))
-        act(E8("THn"), E8("THs"), bias=A("mneg", 0, 1))
+        mm(m, A("ones"), A("acch", 0, 1), False, True)
+        act(A("rest", 0, 1), m, scale=-4096.0)
+        act(ROW("RK"), ROW("RK", 128, 256), scale=ROW("rest", 0, 1))
+        act(E8("THn"), E8("THs"), bias=A("rest", 0, 1))
+        if BARE:
+            act(ROW("RK", 256, 384), ROW("ones"), scale=ROW("rest", 0, 1))
 
     constants()
     matrices(0)
-    for n in range(6):
-        prices(FIRST, n, ("T0", "T1", "K", "D")[n % 4], "aaav"[n % 4])
-    for k in ORDER[1:]:
-        spread(k)
+    for n in (0, 1, 4, 2, 3):
+        prices(FIRST, n, "VD"[n % 2], COPIES[n])
+    for n, parts in enumerate(((ORDER[1], 3), (LATEST,))):
+        spread(n, parts)
+    for k in ORDER:
+        for b0, b1 in PIECES[k]:
+            if b1 - b0 <= SHORT and k not in BARE:
+                cp(A("PT", AT[k] + 128 * b0 + 15, AT[k] + 128 * b1, 16), A("PT", AT[k] + 2048 + 8 * b0, AT[k] + 2048 + 8 * b1))
+    scanned = 16 * (256 - SUMS)
     for t in range(RO):
-        if t < RO - 1:
+        NOW[0] = t
+        n0 = len(ops)
+        if 0 < t < RO - 1:
             matrices(t + 1)
-        else:
-            iota(A("RY"), [[0, 192], [4096, 8]], 0, 0)
-        for k in ORDER[t > 0:]:
-            codes(t, k)
+        elif t:
+            iota(A("RY", 0, scanned), [[0, scanned // 8], [4096, 8]], 0, 0)
+        role.update({n: (t, ("m", n - n0)) for n in range(n0, len(ops))})
         for k in ORDER:
-            gains(t, k)
-            votes(k)
-            best(k)
-            places(t, k)
-            claims(k)
-        if t < RO - 1:
-            codes(t + 1, FIRST)
-            useless()
-        for k in ORDER:
-            for u in (1, 0):
-                scatter(k, u)
+            if t == 0 and "n%d" % k in VISIT:
+                codes(t, k)
+        steps = dict(c=lambda k: codes(t, k), g=lambda k: gains(t, k), v=votes, b=best, p=lambda k: places(t, k), q=claims,
+                     n=lambda k: t < RO - 1 and codes(t + 1, k), u=lambda k: t < RO - 1 and useless())
+        steps["s"] = lambda k: [scatter(k, u) for u in (1, 0)]
+        for step in VISIT.split() + ["s%d" % k for k in ORDER]:
+            n0 = len(ops)
+            steps[step[0]](int(step[1]))
+            role.update({n: (t, (step, n - n0)) for n in range(n0, len(ops))})
+            if (t, step) == (0, "p%d" % FIRST):
+                matrices(1)
+        closes.append(len(ops) - 1)
 
+    scan(A("ys", 0, scanned), A("RY", 0, scanned), A("U", LOW + 16 * SUMS, UW), 0.0, ALU.min, ALU.add)
     for j in range(16):
-        mm(B("T0", 0, 160), I1, A("U", LOW + j, LOW + 2560, 16), j == 0, j == 15)
-    act(A("yco", 0, 160), B("T0", 0, 160))
-    scan(A("ys"), A("RY"), A("U", LOW + 2560, LOW + W), 0.0, ALU.min, ALU.add)
-    tt(A("yco", 160, 256), A("ys", 7, 1536, 16), A("ys", 15, 1536, 16), ALU.add)
-    dma("a", None, A("yco", 0, 160), "o3", oap=T.yc[:, 0:160])
-    dma("y", None, A("yco", 160, 256), "o4", oap=T.yc[:, 160:256])
+        mm(B("D", 0, SUMS), A("Back"), A("U", LOW + j, LOW + 16 * SUMS, 16), j == 0, j == 15)
+    act(A("yco", 0, SUMS), B("D", 0, SUMS))
+    for j in range(2):
+        mm(B("G", SUMS, 256), A("Back"), A("ys", 7 + 8 * j, scanned, 16), j == 0, j == 1)
+    cp(A("yco", SUMS, 256), B("G", SUMS, 256))
+    dma("a", None, A("yco", 0, SUMS), "o3", oap=T.yc[:, 0:SUMS])
+    dma("y", None, A("yco", SUMS, 256), "o4", oap=T.yc[:, SUMS:256])
 
     if not PLAN:
         PLAN.extend(order())

import numpy as np
from concourse.mybir import AluOpType as ALU, AxisListType as AX, ActivationFunctionType as AF

C, W, RO = 384, 4096, 5
VOID = -2.0
LOW = 80
UW = LOW + W
BW = 136
RW = 16 * BW
TOP = 256.0
SPAN = (0, 17, 51, 102, 170)
MAGIC = 12582912.0
M256 = 256 * MAGIC
BIG = 2.0 ** 30
FAR = 4352.0
HIDE = 2.0 ** 60
FLAG = 2.0 ** 24 + 2.0 ** 18
CYCLE, HOP, FLIGHT, SLACK = 0.92, 240.0, 2200.0, 20.0
REMOTE, SPARE = 3400.0, 300.0
MARGIN, WAKE, BLUR, SELF = 240.0, 240.0, 40.0, 240.0
PACES = (((0.9, 0.9, 0.9, 1), 215.0, 200.0), ((0.9, 0.7, 0.6, 1), 250.0, -500.0), ((1.3, 1.65, 1.85, 1), 215.0, 0.0),
         ((1.1, 0.95, 1.3, 1), 270.0, 500.0), ((1.2, 0.92, 0.8, 1), 200.0, 0.0))
ROUNDS, SHAKES, REPEATS, NUDGES, STRETCH = 1, 3, 100, 700, 2000.0
ORDER = (2, 1, 0)
FIRST, LATEST = ORDER[0], ORDER[2]


def _runs(text):
    ends = np.cumsum([int(n) for n in text[1::2]]).tolist()
    return tuple(zip(text[::2], [0] + ends, ends))


PIECES = {FIRST: ((0, 4), (4, 10), (10, 16)), ORDER[1]: ((0, 8), (8, 16)), LATEST: ((0, 6), (6, 12), (12, 16))}
GATHERS = dict(zip(ORDER, map(_runs, ("v3a5v3a5", "v4a4a4a4", "a4a4a3a3a2"))))
OPENING = dict(zip(ORDER, map(_runs, ("v4a4a3a3a2", "a4v4a4a4", "a4a4v4a4"))))
EARLY = (0, 0, 0)
BARE = ()
MIDDLE = True
SIZES = "aav"
TAKE = "ppv"
TAKES = "VHK"
ROWS = "DDDH"
GAINS = "GHG"
ROUND = True
VISIT = "c0 g2 v2 b2 p2 q2 g1 v1 b1 p1 q1 g0 v0 b0 p0 q0 n2 n1 u0"
CODES = "KKK"
COPIES = "avvva"
SHORT = 1
WHO = dict(a="aaa", v="vvv", cf="vva", c16="aaa", cst="avv", RV="vav", LK="aaa", RS="vaa",
           nH="vvv", t2="aaa", cu="aaa", FQ="aaa", plain="vva", wl="aav", sc="aav", LX="vav", lv="avv", Gt="vaa",
           tk="aav", tkb="aav", nB="aav", fl="aav", Vr="aaa", xo="avv")
START = dict(nB="vvv", LX="ava", tkb="avv", cu="vaa", tk="vav", RV="aav", LK="vva", wl="aaa")
FINISH = dict(xo="aaa")
LOAD = 600
AT = {FIRST: 0, ORDER[1]: RW, 3: 2 * RW, LATEST: 3 * RW}
SUMS = 144

GRAPH = []
SCRATCH = {}
PLAN = []
SEMAPHORES = (["sv", "sa", "sp", "sg", "ld0", "ld1", "ld2", "ld3", "ld4", "dp0", "dp1", "dp2", "dp3", "pt0", "pt1", "pt2", "st",
               "o0", "o1", "o2", "o3", "o4"] + ["arr%d_%d" % (t, k) for t in range(1, RO) for k in range(3)])


def _sb(names, cols, dtype):
    for n in names.split():
        SCRATCH[n] = ("sbuf", [128] + (cols if isinstance(cols, list) else [cols]), dtype)


_sb("U", UW, "bfloat16")
_sb("tsti", [24, 16], "int32"), _sb("prb", [24, 16], "bfloat16")
_sb("Vr nB", C, "bfloat16"), _sb("x0 x1 x2 x3 x4 nH cf", C, "float16"), _sb("xo", 4 * C, "float16")
_sb("got0 got1 got2 WB", 2048, "bfloat16"), _sb("RT0 RT1 RT2", 16 + RW, "bfloat16"), _sb("PT", 4 * RW, "bfloat16")
_sb("pT", 4 * BW, "bfloat16"), _sb("ys", 2048, "float16"), _sb("RY", 2048, "bfloat16")
_sb("TT", [4, 96], "float16"), _sb("LX LY", 128, "float16"), _sb("DA", 3 * 544, "float32"), _sb("XI XS", 3 * 136, "float16")
_sb("XH XJ Pp", 136, "bfloat16"), _sb("FQ", C, "bfloat16"), _sb("J RV", 512, "bfloat16"), _sb("tk", 48, "bfloat16"), _sb("RX", [2, SPAN[4]], "bfloat16")
_sb("t1 yo", C, "float32"), _sb("t2 t3 MS", C, "int32"), _sb("KS", 3 * BW, "int32"), _sb("cu", C, "uint16")
_sb("VS mB si", 128, "int32"), _sb("KT", 128, "float32")
_sb("ka xp y1 r1 vx", 24, "int32"), _sb("pc thi", 16, "int32"), _sb("rep", 16, "uint16"), _sb("oL wl lv", 24, "uint16")
_sb("pk sc OH", C, "bfloat16"), _sb("Gt c16", C, "float16")
_sb("CV A16 XB rest o16", 16, "float32"), _sb("pf", 32, "float32"), _sb("pw", 48, "float32")
_sb("acch cst BO R8", 16, "bfloat16")
_sb("ones onesN Blk BlkF I1 I4k BlkN I16 I64k Ineg Im32 TriN Perm PermN PermF E2 Back LK TL RSm", 128, "bfloat16")
_sb("Pm tkb R4k", 128, "bfloat16"), _sb("SEL WR E3", 144, "bfloat16"), _sb("Rneg KM Blk8", 256, "bfloat16"), _sb("RK", 384, "bfloat16"), _sb("RC", 2 * BW, "bfloat16")
_sb("THs THn XF", 24, "float32")
_sb("iN", 144, "int32"), _sb("Tri Ir", RO * 128, "bfloat16"), _sb("Pt Pn", [8 * RO, 16], "bfloat16"), _sb("B4k", 256, "bfloat16"), _sb("yco", 256, "float32")
SCRATCH["Dp"] = ("dram", [8, 2, 4 * RW], "bfloat16")
for _n in "T0 T1 G V H D K M2".split():
    SCRATCH[_n] = ("psum", [128, 1024], "bfloat16") if _n[0] == "T" else ("psum", [128, 512], "float32")


def rank_program(g, core, T, topo):
    rank = T.rank_of(core)
    if rank is None:
        return
    Q = {"v": g.vector, "a": g.scalar, "p": g.tensor, "g": g, "y": g.sync}
    sem = {"v": T.sem.sv, "a": T.sem.sa, "p": T.sem.sp, "g": T.sem.sg}
    cnt, clock, snap, hist = {}, {e: {} for e in Q}, {}, {}

    def A(name, c0=0, c1=None, step=1, p=(0, 128)):
        c1 = SCRATCH[name][1][1] if c1 is None else c1
        ap = T[name][p[0]:p[1], c0:c1:step] if step != 1 else T[name][p[0]:p[1], c0:c1]
        return (ap, name, c0, c1, step, len(range(c0, c1, step)))

    def A3(name, i, j, p=128):
        n, w = SCRATCH[name][1][1:]
        ri, rj = [range(*x.indices(m)) if isinstance(x, slice) else range(x, x + 1) for x, m in ((i, n), (j, w))]
        return (T[name][0:p, i, j], name, ri[0] * w, (ri[-1] + 1) * w, 1, len(ri) * len(rj))

    S = slice

    def IND(win, off):
        return (win[0].indirect(off[0]),) + win[1:5] + (16 * off[5], True)

    def meet(a, b):
        if a[0] >= b[1] or b[0] >= a[1]:
            return False
        if a[2] == b[2] and a[2] > 1 and (a[0] - b[0]) % a[2]:
            return False
        return True

    def need(e, reads, writes):
        want = {}

        def ask(f, n):
            want[f] = max(want.get(f, 0), n)
        for x, wr in [(x, False) for x in reads] + [(x, True) for x in writes]:
            ps = SCRATCH[x[1]][0] == "psum"
            for h in hist.get(x[1], []):
                hit = meet(x[2:5], h[0:3])
                if h[3] != e:
                    if ps or (hit and (wr or h[5])):
                        ask(h[3], h[4])
                elif hit and (wr or h[5]) and e != "p":
                    ask(h[3], h[4])
        for f in sorted(want, key=lambda k: -want[k]):
            if clock[e].get(f, 0) < want[f]:
                Q[e].wait_ge(sem[f], want[f])
                for k, n in snap[(f, want[f])].items():
                    clock[e][k] = max(clock[e].get(k, 0), n)
                clock[e][f] = max(clock[e].get(f, 0), want[f])

    def note(f, n, e, reads, writes):
        snap[(f, n)] = dict(clock[e])
        for x in writes:
            old = hist.get(x[1], [])
            hist[x[1]] = [h for h in old if not (x[4] == 1 and h[0] >= x[2] and h[1] <= x[3] and (clock[e].get(h[3], 0) >= h[4] or h[3] == f))]
            hist[x[1]].append((x[2], x[3], x[4], f, n, True))
        for x in reads:
            L = hist.setdefault(x[1], [])
            L[:] = [h for h in L if not (not h[5] and h[3] == f and h[0:3] == x[2:5])]
            L.append((x[2], x[3], x[4], f, n, False))

    def issue(e, make, reads, writes, s, n):
        need(e, reads, writes)
        ins = make(Q[e])
        if n:
            if s not in sem:
                sem[s] = T.sem[s]
            cnt[s] = cnt.get(s, 0) + n
            ins.then_inc(sem[s], n)
            note(s, cnt[s], e, reads, writes)

    ops = []

    role, closes = {}, []

    def run(e, make, reads, writes, ns):
        ops.append((e, make, reads, writes, e, 1, ns, HOP))

    def dma(e, out, in_, s, oap=None, iap=None):
        ops.append((e, lambda q: q.dma_start(out[0] if out else oap, in_[0] if in_ else iap), [x for x in (in_,) if x], [x for x in (out,) if x],
                    s, 16, 100.0, FLIGHT + (out or in_)[5]))

    def cost(out, ins, c=None):
        if len(out) > 6:
            return 50 + out[5] * 3.8 * CYCLE
        if len(ins[0]) > 6:
            return 60 + out[5] * 1.56 * CYCLE
        if c is None:
            c = 0.5 if all(SCRATCH[x[1]][2] in ("bfloat16", "float16", "uint16") for x in [out] + ins) else 1.0
        return max(64, out[5] * c) * CYCLE

    def order():
        last, pre = {}, []
        for n, op in enumerate(ops):
            d = {}
            for x, wr in [(x, False) for x in op[2]] + [(x, True) for x in op[3]]:
                ps = SCRATCH[x[1]][0] == "psum"
                for h in last.get(x[1], []):
                    if ps or (meet(x[2:5], h[0:3]) and (wr or h[4])):
                        own = ops[h[3]][4] == op[0]
                        d[h[3]] = max(d.get(h[3], 0.0), (0.0 if ps else SELF) if own else ops[h[3]][7])
            for x, wr in [(x, False) for x in op[2]] + [(x, True) for x in op[3]]:
                ps = SCRATCH[x[1]][0] == "psum"
                last[x[1]] = [h for h in last.get(x[1], []) if not (ps or (wr and x[4] == 1 and h[0] >= x[2] and h[1] <= x[3]))] + [x[2:5] + (n, wr)]
            pre.append(d)
        way, post = [op[6] for op in ops], [{} for _ in ops]
        for n in range(len(ops) - 1, -1, -1):
            for m, gap in pre[n].items():
                post[m][n] = gap
                way[m] = max(way[m], ops[m][6] + gap + way[n])

        def lay(before, after, first):
            left, ready, free, out, end = [len(d) for d in before], [0.0] * len(ops), {e: 0.0 for e in Q}, [], [0.0] * len(ops)
            can = {e: [n for n, op in enumerate(ops) if op[0] == e and not before[n]] for e in Q}
            start = lambda e, r: free[e] if r - HOP + MARGIN <= free[e] else r - HOP + WAKE
            while len(out) < len(ops):
                t0, e = min((start(e, min(ready[n] for n in can[e])), e) for e in Q if can[e])
                n = max((n for n in can[e] if start(e, ready[n]) <= t0 + SLACK), key=lambda n: (first[n], -n))
                can[e].remove(n)
                out.append(n)
                end[n] = free[e] = start(e, ready[n]) + ops[n][6]
                for m, gap in after[n].items():
                    ready[m] = max(ready[m], free[e] + gap)
                    left[m] -= 1
                    if not left[m]:
                        can[ops[m][0]].append(m)
            return out, end
        kind = [3 if op[4] != op[0] else 2 if len(op[3][0]) > 6 else 1 if op[2] and len(op[2][0]) > 6 else 0 for op in ops]
        waits = [[[(m, hop + (gap - HOP + later - SPARE * (gap == REMOTE) if gap > HOP else 0.0)) for m, gap in d.items() if gap] for d in pre] for _, hop, later in PACES]

        def takes(plan):
            total = 0.0
            for (pace, wake, _), wait in zip(PACES, waits):
                end, free = [0.0] * len(ops), {e: 0.0 for e in Q}
                for n in plan:
                    e = ops[n][0]
                    end[n] = free[e] = max([end[m] + gap for m, gap in wait[n]] + [free[e]]) + ops[n][6] * pace[kind[n]]
                total += np.log(max(end))
            return total
        best = None
        GRAPH.append((ops, pre, post, way, lay))
        for early in (0, 5, 20):
            again = lay(pre, post, [way[n] - early * n for n in range(len(ops))])
            for _ in range(ROUNDS):
                again = lay(pre, post, lay(post, pre, again[1])[1])
                again += (takes(again[0]),)
                if best is None or again[2] < best[2]:
                    best = again
        def repeat(end, r):
            ref = [end[closes[0]]] + [end[n] for n in closes]
            span, t = min((ref[t + 1] - ref[t], t) for t in range(1, RO - 1))
            at = {role[n][1]: end[n] - ops[n][6] - ref[t] for n in role if role[n][0] == t}
            if r:
                t0, size = (r * 0.618034 % 1.0) * (span + STRETCH) - STRETCH, (100, 250, 600)[r % 3]
                at = {x: y + ((j * 7919 + r * 104729) % size - size / 2) * (t0 <= y < t0 + STRETCH) for j, (x, y) in enumerate(at.items())}
            first = []
            for n, op in enumerate(ops):
                v, x = role.get(n, (0 if n < closes[0] else RO, " "))
                first.append(-max(v - 1, 0) * span - (at[x] if 0 < v < RO - (x[0][0] in "pm") else end[n] - op[6] - ref[v]))
            again = lay(pre, post, first)
            return again + (takes(again[0]),)
        for r in range(1, SHAKES):
            again = lay(pre, post, lay(post, pre, [e + (n * 7919 + r * 104729) % (101, 201, 401)[r % 3] for n, e in enumerate(best[1])])[1])
            for again in (again + (takes(again[0]),), repeat(again[1], 0)):
                if again[2] < best[2]:
                    best = again
        for r in range(REPEATS):
            again = repeat(best[1], r)
            if again[2] < best[2]:
                best = again
        for r in range(1, NUDGES):
            t0 = (r * 0.618034 % 1.0) * max(best[1])
            size = (150, 400, 900)[r % 3]
            again = lay(pre, post, [ops[n][6] - e + ((n * 7919 + r * 104729) % size if t0 <= e < t0 + STRETCH else size / 2)
                                    for n, e in enumerate(best[1])])
            again += (takes(again[0]),)
            if again[2] < best[2]:
                best = again
        GRAPH.append(best[2])
        return best[0]

    def mm(out, l, r, start=False, stop=False):
        run("p", lambda q: q.matmul(out[0], l[0], r[0], start, stop), [l, r], [out], max(min(64, l[5]), r[5]) * CYCLE / 2)

    def flip(out, a):
        run("p", lambda q: q.transpose(out[0], a[0], I1[0]), [a, I1], [out], 128 * CYCLE / 2)

    def tt(out, a, b, op, xr=()):
        run("v", lambda q: q.tensor_tensor(out[0], a[0], b[0], op), [a, b] + list(xr), [out],
            cost(out, [a, b], 2.0 if SCRATCH[a[1]][0] == SCRATCH[b[1]][0] else 1.0))

    def ts(out, a, s1, op0, s2=None, op1=None, xr=()):
        xr = list(xr) + [s for s in (s1, s2) if isinstance(s, tuple)]
        v1 = s1[0] if isinstance(s1, tuple) else s1
        v2 = s2[0] if isinstance(s2, tuple) else s2
        if op1 is None:
            run("v", lambda q: q.tensor_scalar(out[0], a[0], v1, None, op0), [a] + xr, [out], cost(out, [a]))
        else:
            run("v", lambda q: q.tensor_scalar(out[0], a[0], v1, v2, op0, op1), [a] + xr, [out], cost(out, [a]))

    def cp(out, a, xr=()):
        run("v", lambda q: q.tensor_copy(out[0], a[0]), [a] + list(xr), [out], cost(out, [a]))

    def turn(out, a):
        run("v", lambda q: q.transpose(out[0], a[0]), [a], [out], cost(out, [a]))

    def ms(out, c):
        run("v", lambda q: q.memset(out[0], c), [], [out], cost(out, [out]))

    def scan(out, d0, d1, init, op0, op1):
        run("v", lambda q: q.tensor_tensor_scan(out[0], d0[0], d1[0], init, op0, op1), [d0, d1], [out], cost(out, [d0, d1]))

    def reduce(out, a, op, size=False):
        run("v", lambda q: q.tensor_reduce(out[0], a[0], AX.X, op, apply_absolute_value=size), [a], [out], cost(a, [a], 1.0))

    def act(out, a, func=AF.Identity, xr=(), acc=None, **kw):
        xr = list(xr) + [v for v in kw.values() if isinstance(v, tuple)]
        kw = {k: (v[0] if isinstance(v, tuple) else v) for k, v in kw.items()}
        if acc:
            kw["accum_out"] = acc[0]
        run("a", lambda q: q.activation(out[0], a[0], func, **kw), [a] + xr, [out] + ([acc] if acc else []), cost(out, [a], 1.0))

    NOW = [0]
    scalar = lambda step, k: dict(WHO, **{0: START, RO - 1: FINISH}.get(NOW[0], {}))[step][k] == "a"

    def copy(step, k, out, a, *xr):
        (act if scalar(step, k) else cp)(out, a, xr=xr)

    def line(step, k, out, a, scale, bias, *xr):
        if scalar(step, k):
            act(out, a, xr=xr, scale=scale, bias=bias)
        else:
            ts(out, a, scale, ALU.mult, bias, ALU.add, xr=xr)

    SENT = (None, "pc", 300, 301, 1, 1)
    POOL = (None, "pc", 100, 101, 1, 1)

    def iota(out, pattern, base, cm, alone=False):
        kw = {} if SCRATCH[out[1]][2] == "int32" else {"allow_small_or_imprecise_dtypes": True}
        run("g", lambda q: q.iota(out[0], pattern, base, cm, **kw), [POOL, SENT], [out] + [POOL] * alone, 130 + 2 * out[5] * CYCLE)

    def sel(out, a, pattern, op, fill, base, cm):
        run("g", lambda q: q.affine_select(out[0], a[0], pattern, op, fill, base, cm), [a, POOL, SENT], [out], 170 + 2 * out[5] * CYCLE)

    def fill(out, c):
        iota(out, [[0, out[5]]], int(c), 0)

    def flat(out, c, p=(0, 128)):
        act(out, A("iN", 0, out[5], 1, p), scale=0.0, bias=float(c))

    def put(step, j, out, c, p=(0, 128)):
        flat(out, c, p) if scalar(step, j) else ms(out, c)

    CH = lambda n, k, c0=0, c1=128, step=1: A(n, 128 * k + c0, 128 * k + c1, step)
    B = lambda n, c0=0, c1=128, step=1: A(n, c0, c1, step)
    LAST = lambda n, k=0: CH(n, k, 15, 128, 16)
    E8 = lambda n, k=0: A(n, 8 * k, 8 * k + 8)
    F = lambda k, p=(0, 128): A("pf", k, k + 1, 1, p)
    ROW = lambda n, c0=0, c1=128, p=0: A(n, c0, c1, 1, (p, p + 1))
    PR = lambda k: A3("prb", S(8 * k, 8 * k + 8), S(0, 16))
    PT3 = lambda t, name="Pt": A3(name, S(8 * t, 8 * t + 8), S(0, 16))
    I1 = A("I1")
    BEST = lambda k: LAST("KS", k)
    RX = lambda c0, c1, p, step=1, u=S(0, 2): (T.RX[0:p, u, c0:c1:step], "RX", c0, c1, 1, len(range(2)[u]) * len(range(c0, c1, step)))
    SCALE, UNSCALE = F(13), F(14)
    LANE = [[0, 8], [1, 16]]
    rho = lambda t: (5 * t) % 16

    dma("y", A3("tsti", S(0, 24), S(0, 16))[:5] + (LOAD,), None, "ld0", iap=T.tst[:])
    dma("a", A3("prb", S(0, 24), S(0, 16)), None, "ld1", iap=T.pr[:])
    for u in range(16):
        dma("ya"[u % 2], (T.U[u:128:16, LOW:UW], "U", LOW + u, UW, 16, 500), None, "ld%d" % (3 + u % 2), iap=T.cov[15 - u:128:16, :])
    dma("y", A("thi", 0, 1, 1, (0, 8)), None, "ld2", iap=T.th[:])

    def constants():
        iota(A("pc", 0, 1), [[0, 1]], 0, 1)
        iota(A("iN"), [[1, 144]], 0, 0)
        P = lambda k: A("pc", k, k + 1)
        ms(A("ones"), 1.0)
        ts(P(1), P(0), 4, ALU.arith_shift_right)
        ts(P(2), P(0), 15, ALU.bitwise_and)
        cp(A("pf", 0, 2), A("pc", 1, 3))
        ts(F(9), P(0), 256.0, ALU.add)
        ts(A("mB"), B("iN"), 4, ALU.arith_shift_right)
        ts(A("si"), B("iN"), 15, ALU.bitwise_and)
        act(F(6), F(1), scale=16.0 * 613)
        sel(I1, A("ones"), [[-1, 128]], ALU.is_equal, 0.0, 0, 1)
        ts(A("A16", 0, RO), A("iN", 0, RO), 16.0 * 77, ALU.mult, F(6), ALU.add)
        act(A("I4k"), I1, scale=4096.0)
        ts(A("Blk"), A("mB"), F(0), ALU.is_equal)
        ts(CH("B4k", 0), A("mB"), F(0), ALU.is_equal, -4096.0, ALU.mult)
        ts(CH("B4k", 1), CH("B4k", 0), -1.0, ALU.mult)
        act(A("BlkN"), A("Blk"), scale=-1.0)
        act(A("BlkF"), A("Blk"), scale=FAR)
        ts(A("o16"), A("iN", 0, 16), F(1), ALU.is_equal)
        for b in range(16):
            ts(CH("WB", b), A("Blk"), A("o16", b, b + 1), ALU.mult)
        flat(A("U", 0, LOW), VOID)
        for c in range(8):
            ts(A("x0", c, C, 8), A3("tsti", S(c, 24, 8), S(0, 16)), 1.0 / 32, ALU.mult, 1.0 / 64, ALU.add)
        act(F(2), F(0), scale=16.0, bias=15.0)
        act(F(7), F(1), scale=-1.0, bias=15.0)
        act(F(8), F(1), scale=-1.0, bias=F(2))
        for j, (src, out) in enumerate(((1, SCALE), (7, F(15)))):
            ts(F(17 + j), F(src), 15.0, ALU.is_lt, F(src), ALU.mult)
            ts(A("pw", 16 * j, 16 * j + 16), A("iN", 0, 16), F(17 + j), ALU.is_ge, 2.0 ** -8, ALU.max)
            reduce(out, A("pw", 16 * j, 16 * j + 16), ALU.mult)
        ts(A("pw", 32, 48), A("pw", 0, 16), 1.0, ALU.is_lt, 255.0, ALU.mult)
        act(A("pw", 32, 48), A("pw", 32, 48), bias=1.0)
        reduce(UNSCALE, A("pw", 32, 48), ALU.mult)
        act(F(16), UNSCALE, scale=4096.0)
        act(F(10), F(0), scale=-15.0, bias=113.0)
        ts(F(11), F(1), 0.0, ALU.is_equal, F(10), ALU.mult)
        act(F(12), F(11), bias=F(8))
        ts(A("Pm"), B("iN"), F(8), ALU.is_equal, F(15), ALU.mult)
        ts(A("Pp"), A("iN", 0, BW), F(12), ALU.is_equal, F(15), ALU.mult)
        ts(A("Back"), B("iN"), F(8), ALU.is_equal)
        act(B("pk"), I1, scale=UNSCALE)
        mm(B("M2"), A("ones"), B("pk"), True, True)
        act(A("pT", 3 * BW, 3 * BW + 128), B("M2"))
        put("RS", 2, A("pT", 3 * BW + 128, 4 * BW), 1.0)
        price = lambda c0=0, c1=BW, step=1: A("RC", BW + c0, BW + c1, step, (0, 1))
        flat(price(), 0.0, (0, 1)), flat(price(15, 128, 16), TOP, (0, 1))
        for k in ORDER:
            w, turned = (128, A("Back")) if k in BARE else (BW, A("Pp"))
            bank = B("DHD"[k], 0, w)
            mm(bank, PR(k), turned, True)
            mm(bank, A("ones"), turned, False, k in BARE)
            if k not in BARE:
                mm(bank, ROW("ones"), price(), False, True)
            act(A("pT", BW * k, BW * k + w), bank)
        act(F(3), F(1), scale=128.0, bias=16.0)
        act(F(4), F(1), scale=128.0, bias=15.0)
        act(F(5), F(1), scale=-16.0, bias=-16.0)
        act(F(19), F(1), scale=8.0, bias=16.0 + 2048)
        act(CH("Rneg", 0), A("Pm"), scale=-16.0 if EARLY[0] else -65536.0)
        if not ROUND:
            act(A("I16"), I1, scale=0.0625)
        p8, p96 = (0, 8), (96, 98)
        if EARLY[0]:
            act(A("R4k"), A("I4k"), scale=SCALE)
        ts(E8("R8"), E8("iN"), F(0), ALU.is_equal)
        mm(B("G"), A("ones"), A("Pm"), True, True)
        mm(A("G", 128, 256, 1, p8), E8("R8"), A("Pm"), True, True)
        act(B("RK"), B("G"))
        act(ROW("RK", 128, 256), ROW("G"))
        act(A("Blk8", 128, 256, 1, p8), A("G", 128, 256, 1, p8))
        r64 = lambda n, c0=0, c1=128, step=1: A(n, c0, c1, step, (64, 66))
        f64 = lambda k: F(k, (64, 66))
        ts(f64(20), f64(9), 320.0, ALU.is_equal)
        act(f64(21), f64(20), scale=-2032.0, bias=2048.0)
        ts(r64("RC"), r64("iN"), 16.0, ALU.add, f64(20), ALU.mult)
        act(r64("RC", 15, 128, 16), r64("iN", 0, 8), scale=f64(20), bias=f64(21))
        tt(r64("RK"), r64("RC"), r64("RK"), ALU.mult)
        flat(A("RK", 15, 128, 16, (32, 33)), 0.0625, (32, 33))
        if min(EARLY) < 16:
            ts(A("SEL"), A("iN"), F(2), ALU.is_equal, 4096.0, ALU.mult)
        act(E8("BO"), E8("R8"), scale=F(16))
        act(A("KT"), B("iN"), bias=F(3))
        act(LAST("KT"), E8("iN"), bias=F(19))
        ms(B("KM"), 2.0 ** -8), fill(A("KM", 0, 128, 16), 0), flat(LAST("KM"), 2.0 ** 56)
        act(LAST("KM"), LAST("KM"), scale=2.0 ** 56)
        ms(A("LK"), 0.0), ms(A("RV", 0, 128), 0.0), ms(A("TL"), 0.0)
        act(ROW("LK", p=32), ROW("si", p=32), scale=128.0)
        for j, p in enumerate(((0, 1), (64, 66), p96)):
            put("LK", j, A("LK", 0, 128, 1, p), 1.0, p)
        flat(ROW("RK"), 0, (0, 1))
        ts(A("thi", 2, 3, 1, p8), A("thi", 0, 1, 1, p8), 4, ALU.arith_shift_right)
        ts(A("thi", 3, 4, 1, p8), A("thi", 0, 1, 1, p8), 15, ALU.bitwise_and)
        act(A("TL", 96, 97, 1, p8), A("thi", 2, 3, 1, p8), scale=-65536.0, bias=127.0 * 65536 if EARLY[0] else -65536.0)
        act(A("TL", 97, 98, 1, p8), A("thi", 3, 4, 1, p8), scale=-4096.0)
        ts(A("cst", 8, 16, 1, p8), A("I1", 0, 8, 1, p8), A("TL", 97, 98, 1, p8), ALU.mult)
        mm(A("M2", 0, 128, 1, (0, 98)), A("TL", 0, 98, 1, p8), A("Blk8", 128, 256, 1, p8), True, True)
        mm(B("M2", 128, 136), A("ones", 0, 128, 1, p8), A("cst", 8, 16, 1, p8), True, True)
        act(A("RK", 0, 128, 1, p96), A("M2", 0, 128, 1, p96))
        act(E8("THs"), B("M2", 128, 136))
        act(E8("THn"), B("M2", 128, 136))
        sel(A("Blk8", 0, 128, 1, p8), A("ones", 0, 128, 1, p8), [[-1, 8], [0, 16]], ALU.is_equal, 0.0, 0, 1)
        if BARE:
            act(CH("Rneg", 1), A("Back"), scale=-16.0 if EARLY[0] else -65536.0)
            act(E8("BO", 1), E8("R8"), scale=4096.0)
            fill(CH("KM", 1), 1), fill(CH("KM", 1, 0, 128, 16), 0)
            fill(CH("RK", 2), 1), fill(ROW("RK", 256, 384), 0)
            act(r64("RK", 256, 384), r64("RC"))
            flat(A("RK", 256 + 15, 384, 16, (32, 33)), 0.0625, (32, 33))
            mm(A("M2", 256, 384, 1, (0, 98)), A("TL", 0, 98, 1, p8), A("Blk8", 0, 128, 1, p8), True, True)
            act(A("RK", 256, 384, 1, p96), A("M2", 256, 384, 1, p96))
        for j, c in enumerate((-65536.0 - 1408 - 128,) if ROUND else (-MAGIC - 65536, -0.46875, MAGIC)):
            put("RV", j, ROW("RV", 128 * j, 128 * j + 128), c, (0, 1))
        act(ROW("RV", p=64), ROW("si", p=64), scale=-256.0, bias=3968.0)
        act(ROW("RV", 384, 512), ROW("si"), scale=-4096.0, bias=-2048.0)
        sel(A("TriN"), A("BlkN"), [[1, 128]], ALU.is_gt, 0.0, 0, -1)
        sel(A("TriN"), A("TriN"), [[-1, 128]], ALU.not_equal, 1.0, 0, 1)
        for u in range(2):
            for g1 in range(2):
                sel(CH("J", 2 * u + g1), A("ones"), [[32, 4], [1000, 2], [2, 16]], ALU.is_equal, 0.0, u - 1000 * g1, -1)
        for k in range(3):
            flat(A("RT%d" % k, 0, 16), VOID + 1)
        flat(A("E3"), 0.0), ms(A("XI"), 0.0)
        cp(E8("rep"), E8("iN"))
        sel(A("Perm"), A("ones"), [[1, 16], [16, 8]], ALU.is_equal, 0.0, 0, -1)
        put("RS", 0, A("RSm"), BIG), put("RS", 1, A("RSm", 0, 128, 16), -BIG)
        act(A("I64k"), I1, scale=65536.0)
        act(A("PermF"), A("Perm"), scale=-16.0)
        act(A("PermN"), A("Perm"), scale=-1.0)
        act(A("Ineg"), I1, scale=-1.0)
        iota(A("XJ"), [[0, 8], [1, 17]], -1, 0)
        ts(A("XH"), A("XJ"), F(1), ALU.is_equal, HIDE, ALU.mult)
        ts(A("XJ"), A("XJ"), F(1), ALU.is_lt)
        tt(A("XH"), A("XH"), A("XJ"), ALU.add)
        act(A("XH", 1, 136, 17), A("XH", 1, 136, 17), scale=1 / HIDE)
        fill(A("XH", 0, 136, 17), 0)
        p64 = (0, 64)
        ts(A("LX", 0, 128, 1, p64), A("si", 0, 128, 1, p64), 288.0, ALU.add, F(9, p64), ALU.is_equal)
        if "a" in SIZES:
            act(A("LY", 0, 128, 1, p64), A("LX", 0, 128, 1, p64))
        for v in range(4):
            row = RX(SPAN[v], SPAN[v + 1], 64)
            iota(row, [[0, row[5]]], LOW - 66 - 32 + 16 * v, 1)
            sel(row, row, [[0, 2], [-16, v + 1], [-1, 17]], ALU.is_gt, BIG, 16 * v + 1 - 32, 1)
        lead = RX(0, SPAN[4], 64, 17)
        sel(lead, lead, [[0, 20]], ALU.is_gt, BIG, 0, 0)
        ms(RX(0, SPAN[4], 32), -FAR)
        for v in range(4):
            fill(RX(SPAN[v], SPAN[v] + 1, 64), 2048.0 + LOW)
            row = RX(SPAN[v] + 1, SPAN[v + 1], 32)
            sel(row, row, [[4, 2], [0, row[5] // 2]], ALU.is_equal, 0.0, v, -1)
            sel(RX(SPAN[v], SPAN[v] + 1, 32), A("ones", 0, 2, 1, (0, 32)), [[4, 2]], ALU.is_equal, 0.0, v, -1)
        ts(E8("CV"), E8("iN"), 16.0, ALU.mult, F(4), ALU.add)
        ts(A("WR"), A("iN"), F(2), ALU.is_equal, F(5), ALU.mult)
        act(A("XB", 0, RO - 1), A("o16", 0, 16, 5), scale=(256.5 - 2176) / 32)
        act(A("XB", RO - 1, RO), A("o16", rho(RO - 1), rho(RO - 1) + 1), scale=256.5 - 2176, bias=-0.5)
        act(A("Im32"), I1, scale=-32.0)
        act(A("onesN"), A("ones"), scale=-1.0)
        for j, c in enumerate((127.5, M256, -M256)):
            put("cst", j, ROW("cst", j, j + 1), c, (0, 1))

    def matrices(t):
        for name, sign in (("Pt", -1), ("Pn", 1)):
            sel(PT3(t, name), CH("B4k", sign > 0), [[-1, 128]], ALU.is_equal, 0.0, -1 - t, 1)
        for name, sign in (("Pt", -1), ("Pn", 1)):
            wrap = A3(name, S(8 * t, 8 * t + 8), S(15 - t, 16))
            sel(wrap, wrap, [[-16, 8], [-1, t + 1]], ALU.not_equal, 4096.0 * sign, 0, 1)
        sel(PT3(t, "Pn"), PT3(t, "Pn"), [[-1, 128]], ALU.not_equal, 4096.0, 0, 1)
        sel(CH("Tri", t), A("TriN"), LANE, ALU.not_equal, 0.0, -rho(t), 0)
        sel(CH("Ir", t), A("Im32"), LANE, ALU.not_equal, 0.0, -rho(t), 0)

    def prices(k, n, bank, e):
        c0, w, blocks = (0, 128, range(4 * n, 4 * n + 4)) if n < 4 else (128, 8, range(16))
        for j, b in enumerate(blocks):
            mm(B(bank, w * j, w * j + w), CH("WB", b), A("pT", BW * k + c0, BW * k + c0 + w), True, True)
        (act if e == "a" else cp)(A("PT", AT[k] + 512 * n, AT[k] + 512 * n + w * len(blocks)), B(bank, 0, w * len(blocks)))

    def spread(n, parts):
        for k in parts:
            for j in range(2):
                for c0, c1, w0, w1 in ((0, 2048, 0, 128), (2048, RW, 128, BW))[:1 if k in BARE else 2]:
                    c0, c1 = AT[k] + c0, AT[k] + c1
                    dma("y", (T.Dp[:, j, c0:c1], "Dp", 2 * c0 + j, 2 * c1, 2, BW), A("pT", BW * k + w0, BW * k + w1), "dp%d" % k)
        c0, c1 = AT[parts[0]], AT[parts[-1]] + (2048 if parts[-1] in BARE else RW)
        for i in range(8):
            dma("y", (T.PT[i:128:8, c0:c1], "PT", c0 + i, c1, 16, 1000 * len(parts)), (T.Dp[:, :, c0:c1], "Dp", 2 * c0, 2 * c1, 1, BW), "pt%d" % n)

    def codes(t, k):
        x = CH("x%d" % t, k)
        if scalar("nH", k):
            act(CH("nH", k), x, AF.Relu, scale=2.0 ** 20, bias=-2.0 ** 23)
        else:
            ts(CH("nH", k), x, 8.0, ALU.is_gt, 2.0 ** 14, ALU.mult)
        Y, M = B(CODES[k], 256, 384), B(CODES[k], 384, 512)
        mm(Y, PT3(t), x, True)
        mm(Y, PT3(t, "Pn"), CH("nH", k), False, True)
        pair = (CH("Tri", t), CH("nH", k))[::1 if TAKE[k] == "p" or t == RO - 1 else -1]
        if t:
            mm(M, *pair, True, True)
        tt(CH("t1", k), x, Y, ALU.mult)
        if not t:
            M = B("M2", 128 * k + 128, 128 * k + 256)
            mm(M, *pair, True, True)
        line("t2", k, CH("t2", k), CH("t1", k), -1.0, A("A16", t, t + 1))
        ts(CH("t3", k), CH("t2", k), 4, ALU.arith_shift_right, 4095 - 2 ** 31, ALU.bitwise_and)
        if scalar("cu", k):
            act(CH("cu", k), CH("t3", k), AF.Relu, bias=float(LOW))
        else:
            ts(CH("cu", k), CH("t3", k), float(LOW), ALU.add, 0.0, ALU.max)
        if scalar("FQ", k):
            act(CH("FQ", k), M, AF.Relu, scale=1.0 / 16384)
        else:
            ts(CH("FQ", k), M, 0.0, ALU.is_gt)
        line("cf", k, CH("cf", k), CH("cu", k), 1.0, -2048.0 - LOW)
        if k == LATEST:
            for c in range(4):
                turn(A3("TT", c, S(0, 96)), A("cf", c, C, 4))

    TURN = [0]

    def gains(t, k):
        got, RT, bare = "got%d" % k, "RT%d" % k, k in BARE
        for e, b0, b1 in (GATHERS if t else OPENING)[k]:
            out, off = A(got, 128 * b0, 128 * b1), CH("cu", k, 8 * b0, 8 * b1)
            line(e, k, out, IND(A("U"), off), 1.0 if bare else SCALE, 1.0 if bare else SCALE, off)
        if EARLY[k]:
            mm(B("H"), CH("Rneg", bare), PR(k), True)
        else:
            mm(B(GAINS[k]), PR(k), CH("Rneg", bare), True)
            mm(B(GAINS[k]), A("LK", 0, 128, 1, (0, 98)), A("RK", 256 * bare, 256 * bare + 128, 1, (0, 98)))
        for b0, b1 in PIECES[k]:
            bank, n = "T%d" % (TURN[0] % 2), 128 * (b1 - b0)
            TURN[0] += 1
            for b in range(b0, b1):
                flip(CH(bank, b - b0), CH(got, b))
            out, price = A(RT, 16 + 128 * b0, 16 + 128 * b1), A("PT", AT[k] + 128 * b0, AT[k] + 128 * b1)
            plain = A(RT, 2064 + 8 * b0, 2064 + 8 * b1)
            if b1 - b0 <= SHORT or bare:
                tt(out, A(bank, 0, n), price, ALU.max)
                copy("plain", k, plain, A(bank, 15, n, 16))
            else:
                cp(plain, A(bank, 15, n, 16))
                scan(out, A(bank, 0, n), price, TOP, ALU.min, ALU.max)
                tt(A(RT, 31 + 128 * b0, 16 + 128 * b1, 16), plain, A("PT", AT[k] + 2048 + 8 * b0, AT[k] + 2048 + 8 * b1), ALU.max)
            for b in range(b0, b1):
                block = A(RT, 16 + 128 * b, 144 + 128 * b)
                if b < EARLY[k]:
                    mm(B("H", b, 128, 16), block, E8("R8"), False, b == EARLY[k] - 1)
                else:
                    mm(B(GAINS[k]), A("SEL", 15 - b, 143 - b), block, False, b == 15)
                if b == EARLY[k] - 1:
                    line("Gt", k, CH("Gt", k), B("H"), 1.0 if bare else UNSCALE, -2048.0)
                    mm(B("G"), A("LK", 0, 128, 1, (0, 98)), A("RK", 256 * bare, 256 * bare + 128, 1, (0, 98)), True)
                    mm(B("G"), CH("Gt", k), A("I4k" if bare else "R4k"), False, b == 15)

    def votes(k):
        if ROUND:
            line("c16", k, CH("c16", k), CH("cu", k), 0.0625, 1408 - LOW / 16 - 0.46875)
            mm(B("V"), CH("c16", k), I1, True)
        else:
            mm(B("V"), ROW("ones"), ROW("RV", 128, 256), True)
            mm(B("V"), CH("cf", k), A("I16"))
            mm(B("V"), ROW("ones"), ROW("RV", 256, 384))
        mm(B("V"), A("LK", 0, 128, 1, (0, 65)), A("RV", 0, 128, 1, (0, 65)))
        for i in range(16):
            mm(B("V", i, 128, 16), A("got%d" % k, i, 2048, 16), E8("BO", k in BARE), False, i == 15)
        scan(A("VS"), A("RSm"), B("V"), -BIG, ALU.min, ALU.max)
        ts(E8("vx", k), LAST("VS"), 255 + 2 ** 24, ALU.bitwise_and)
        if scalar("tk", k):
            act(E8("tk", k), E8("vx", k), AF.Relu, scale=-1.0, bias=256.0)
        else:
            ts(E8("tk", k), E8("vx", k), -256.0, ALU.add, 0.0, ALU.min)

    def best(k):
        wl = E8("wl", k)
        scan(CH("KS", k), CH("KM", k in BARE), B(GAINS[k]), 0.0, ALU.mult, ALU.max)
        ts(E8("ka", k), BEST(k), 4095, ALU.bitwise_and)
        copy("wl", k, wl, E8("ka", k))
        if k in BARE:
            copy("sc", k, CH("pk", k), IND(A("RT%d" % k), wl), wl)
        else:
            copy("sc", k, CH("sc", k), IND(A("PT", AT[3] - 16, AT[3] + RW), wl), wl)
            tt(CH("pk", k), IND(A("RT%d" % k), wl), CH("sc", k), ALU.mult, xr=[wl])
        tt(CH("OH", k), IND(E8("ka", k), E8("rep")), A("KT"), ALU.is_equal, xr=[E8("rep")])
        mm(B("M2"), CH("OH", k), I1, True, True)
        line("nB", k, CH("nB", k), B("M2"), -1.0, 1.0)

    def claims(k):
        K = lambda c0=0, c1=128, p=(0, 128): A("K", c0, c1, 1, p)
        mm(K(), ROW("ones"), ROW("RV", 384, 512), True)
        for u in range(2):
            for g1 in range(2):
                mm(K(64 * u, 64 * u + 64), CH("J", 2 * u + g1), A3("TT", S(0, 4), S(32 * k + 16 * g1, 32 * k + 16 * g1 + 16)))
        mm(K(), CH("pk", k), A("I64k"), False, True)
        scan(CH("MS", k), A("RSm"), K(), -BIG, ALU.min, ALU.max)
        ts(E8("xp", k), LAST("MS", k), 4095 - 2 ** 31, ALU.bitwise_and)
        x0, d0, rows = 136 * k, 544 * k, ROWS[k]
        own, p8, p48, h = A("XI", x0, x0 + 136, 17), (0, 8), (0, 48), SPAN[4]
        ts(own, E8("xp", k), -2048.0, ALU.add, -2050.0, ALU.max)
        sizes = SIZES[k] == "a"
        if sizes:
            act(E8("XF", k), own, scale=-FAR)
            act(A("DA", d0, d0 + 544, 68), own, bias=2048.0 + LOW)
        else:
            mm(A(rows, 384, 512, 1, p8), own, I1, True, True)
            copy("LX", k, A("LX", 0, 128, 1, p8), A(rows, 384, 512, 1, p8))
        scan(A("XS", x0, x0 + 136), A("XH"), A("XI", x0, x0 + 136), 0.0, ALU.mult, ALU.add)
        D = lambda u, c0, c1: B(ROWS[3], 256 + c0, 256 + c1) if k == LATEST and u == 0 else B(rows, h * u + c0, h * u + c1)
        for u, m in (((1, 1), (0, 1)) if k == LATEST else ((0, 2),)):
            if sizes:
                mm(D(u, 0, h * m), A("LY", 0, 128, 1, p48), RX(0, h, 48, 1, S(u, u + m)), True)
            else:
                mm(D(u, 0, h * m), A("LX", 0, 128, 1, p48), RX(0, h, 48, 1, S(u, u + m)), True)
            for c in range(4 * u, 4 * (u + m)):
                v = c % 4
                mm(D(c // 4, SPAN[v] + 1, SPAN[v + 1]), A("BlkF"), A("XS", x0 + 68 * (c // 4) + 1, x0 + 68 * (c // 4) + 17 * v + 17), False, c == 4 * (u + m) - 1)
        if k == ORDER[1] and MIDDLE:
            act(E8("lv", k), E8("xp", k), AF.Relu, bias=float(LOW))
            copy("Vr", k, CH("Vr", k), IND(A("U"), E8("lv", k)), E8("lv", k))
        elif k != FIRST:
            y = E8("y1", k)
            ts(y, LAST("MS", k), 12, ALU.arith_shift_right, 15, ALU.bitwise_and)
            tt(y, y, E8("CV"), ALU.subtract)
            line("lv", k, E8("lv", k), y, -1.0, 0.0)
            line("Vr", k, CH("Vr", k), IND(A("got%d" % k), E8("lv", k)), 1.0 if k in BARE else UNSCALE, -1.0, E8("lv", k))
        for u in (1, 0):
            for c in range(4 * u, 4 * u + 4):
                row, w = D(u, SPAN[c % 4], SPAN[c % 4 + 1]), 17 * (c % 4 + 1)
                if sizes:
                    c0 = d0 + 68 * c
                    act(A("DA", c0 + 1, c0 + w), D(u, SPAN[c % 4] + 1, SPAN[c % 4 + 1]), AF.Abs, bias=A("XF", 8 * k + c, 8 * k + c + 1))
                    row = A("DA", c0, c0 + w)
                reduce(A("oL", 8 * k + c, 8 * k + c + 1), row, ALU.min, True)
        if k == FIRST:
            copy("Vr", k, CH("Vr", k), IND(A("U"), A("oL", 8 * k, 8 * k + 8)), A("oL", 8 * k, 8 * k + 8))

    def scatter(k, u):
        o = A("oL", 8 * k + 4 * u, 8 * k + 4 * u + 4)
        tt(IND(A("U"), o), CH("Vr", k, 64 * u, 64 * u + 64), CH("nB", k, 64 * u, 64 * u + 64), ALU.mult, xr=[o])

    def places(t, k):
        r, p8 = E8("r1", k), (0, 8)
        tt(r, BEST(k), E8("THn"), ALU.subtract)
        ts(r, r, 12, ALU.arith_shift_right, 15, ALU.bitwise_and)
        tt(LAST("E3"), r, BEST(k), ALU.min)
        wide = TAKE[k] == "p" or t == RO - 1
        bank = {"M": "M2"}.get(TAKES[k], TAKES[k])
        take, tkb = (A(bank, 256, 384, 1, p8), A("tkb", 0, 128, 1, p8)) if wide else (B(bank, 256, 264), A("tk", 32, 40))
        pair = (lambda l, r: (l, r)) if wide else (lambda l, r: (r, l))
        copy("fl", k, E8("tk", 3), BEST(k))
        mm(take, *pair(E8("tk", k), I1 if scalar("tk", k) else A("Ineg")), True)
        mm(take, *pair(E8("tk", 3), A("PermF")), False, True)
        if scalar("tkb", k):
            act(tkb, take, AF.Relu)
        else:
            ts(tkb, take, 0.0, ALU.max)
        if wide:
            mm(B(bank, 384, 512), A("Blk8", 0, 128, 1, p8), tkb, True, True)
            tt(A("E2"), B(bank, 384, 512), CH("FQ", k), ALU.mult)
        else:
            tt(A("E2"), IND(tkb, E8("rep")), CH("FQ", k), ALU.mult, xr=[E8("rep")])
        s, X = 15 - rho(t), lambda c0=0, c1=128: B("M2", 128 + c0, 128 + c1)
        if t == RO - 1:
            mm(X(), A("E3", s, s + 128), A("Ineg"), True)
            for c in range(8):
                mm(X(16 * c, 16 * c + 16), CH("Ir", t), CH("x%d" % t, k, c, 128, 8))
            mm(X(), A("WR", s, s + 128), CH("nB", k))
            for c in range(8):
                mm(X(16 * c, 16 * c + 16), I1, B("E2", c, 128, 8), False, c == 7)
            line("xo", k, CH("yo", k), X(), -1.0, A("XB", t, t + 1))
            dma("y", None, CH("yo", k), "o%d" % k, oap=T.yt[:, 128 * k:128 * k + 128])
            return
        mm(X(), CH("Ir", t), CH("x%d" % t, k), True)
        mm(X(), A("E3", s, s + 128), A("PermN"))
        for c in range(8):
            mm(B("M2", 128 + c, 256, 8), A("WR", s, s + 128), CH("nB", k, 16 * c, 16 * c + 16))
        mm(X(), *pair(I1, A("E2")), False, True)
        xo = CH("xo", 3 * t + k)
        line("xo", k, xo, X(), -1.0 / 32, A("XB", t, t + 1))
        to, src = T.cores[(rank + 1) % len(T.cores)], T.cores[(rank - 1) % len(T.cores)]
        rid, pid = topo.addr(to, core)
        eng = topo.engines(core, to)[:8]
        a, dst = "arr%d_%d" % (t + 1, k), CH("x%d" % (t + 1), k)

        def write(q):
            q.remote_dma(dst[0], xo[0], T.sem[a], T.sem.st, pid, rid, sum(1 << e for e in eng))
            sem["st"], cnt["st"] = T.sem.st, cnt.get("st", 0) + len(eng)
            sem[a], cnt[a] = T.sem[a], len(topo.engines(src, core)[:8])
            snap[(a, cnt[a])] = {}
            hist.setdefault(dst[1], []).append(dst[2:5] + (a, cnt[a], True))
        ops.append(("g", write, [xo], [dst] + [SENT] * (k == (LATEST if t else FIRST)), "st", 0, 3100.0 if (t, k) == (0, FIRST) else 600.0, REMOTE))

    def useless():
        m = B("M2", 384, 385)
        for k in range(3):
            mm(B("M2", 385, 386), CH("nB", k), A("ones", 0, 1), k == 0, k == 2)
        act(A("acch", 0, 1), B("M2", 385, 386), bias=-360.0)
        mm(m, ROW("ones"), ROW("cst", 0, 1), True)
        mm(m, A("onesN"), A("acch", 0, 1))
        mm(m, ROW("ones"), ROW("cst", 1, 2))
        mm(m, ROW("ones"), ROW("cst", 2, 3))
        mm(m, A("ones"), A("acch", 0, 1), False, True)
        act(A("rest", 0, 1), m, scale=-4096.0)
        act(ROW("RK"), ROW("RK", 128, 256), scale=ROW("rest", 0, 1))
        act(E8("THn"), E8("THs"), bias=A("rest", 0, 1))
        if BARE:
            act(ROW("RK", 256, 384), ROW("ones"), scale=ROW("rest", 0, 1))

    constants()
    matrices(0)
    for n in (0, 1, 4, 2, 3):
        prices(FIRST, n, "VD"[n % 2], COPIES[n])
    for n, parts in enumerate(((ORDER[1], 3), (LATEST,))):
        spread(n, parts)
    for k in ORDER:
        for b0, b1 in PIECES[k]:
            if b1 - b0 <= SHORT and k not in BARE:
                cp(A("PT", AT[k] + 128 * b0 + 15, AT[k] + 128 * b1, 16), A("PT", AT[k] + 2048 + 8 * b0, AT[k] + 2048 + 8 * b1))
    scanned = 16 * (256 - SUMS)
    for t in range(RO):
        NOW[0] = t
        n0 = len(ops)
        if 0 < t < RO - 1:
            matrices(t + 1)
        elif t:
            iota(A("RY", 0, scanned), [[0, scanned // 8], [4096, 8]], 0, 0)
        role.update({n: (t, ("m", n - n0)) for n in range(n0, len(ops))})
        for k in ORDER:
            if t == 0 and "n%d" % k in VISIT:
                codes(t, k)
        steps = dict(c=lambda k: codes(t, k), g=lambda k: gains(t, k), v=votes, b=best, p=lambda k: places(t, k), q=claims,
                     n=lambda k: t < RO - 1 and codes(t + 1, k), u=lambda k: t < RO - 1 and useless())
        steps["s"] = lambda k: [scatter(k, u) for u in (1, 0)]
        for step in VISIT.split() + ["s%d" % k for k in ORDER]:
            n0 = len(ops)
            steps[step[0]](int(step[1]))
            role.update({n: (t, (step, n - n0)) for n in range(n0, len(ops))})
            if (t, step) == (0, "p%d" % FIRST):
                matrices(1)
        closes.append(len(ops) - 1)

    scan(A("ys", 0, scanned), A("RY", 0, scanned), A("U", LOW + 16 * SUMS, UW), 0.0, ALU.min, ALU.add)
    for j in range(16):
        mm(B("D", 0, SUMS), A("Back"), A("U", LOW + j, LOW + 16 * SUMS, 16), j == 0, j == 15)
    act(A("yco", 0, SUMS), B("D", 0, SUMS))
    for j in range(2):
        mm(B("G", SUMS, 256), A("Back"), A("ys", 7 + 8 * j, scanned, 16), j == 0, j == 1)
    cp(A("yco", SUMS, 256), B("G", SUMS, 256))
    dma("a", None, A("yco", 0, SUMS), "o3", oap=T.yc[:, 0:SUMS])
    dma("y", None, A("yco", SUMS, 256), "o4", oap=T.yc[:, SUMS:256])

    if not PLAN:
        PLAN.extend(order())
    for n in PLAN:
        issue(*ops[n][:6])
    for s in sem:
        if cnt.get(s, 0):
            g.wait_ge(sem[s], cnt[s])
